import numpy as np, ml_dtypes
CORES = [8,136,40,168]
N = 4
BF = ml_dtypes.bfloat16
def gentries(a):
    return np.ascontiguousarray(a.reshape(8, 16, -1).transpose(0, 2, 1)).reshape(8, -1)
def gtable(e):
    e = np.asarray(e); return np.ascontiguousarray(e.reshape(8, -1, 16).transpose(0, 2, 1)).reshape(128, -1).astype(np.int32)
V, R, L, S = 2048, 384, 4, 2
def trees(rng, deep):
    T = N * 8; ar = np.arange(T); P = V // 2 - 1; i = np.arange(P)[:, None]
    pair = 2 * (np.argsort(rng.random((T, P)), axis=1) + 1); side = rng.integers(0, 2, (P, T))
    pick = np.where(rng.random((P, T)) < deep, i, np.minimum((rng.random((P, T)) * (i + 1)).astype(np.int64), i))
    kid = np.full((T, V), -1, np.int64); up = np.zeros((T, V), np.int64); leaf = np.zeros((T, P + 1), np.int64); cnt = np.ones((T, V), np.int64)
    for t in range(P):
        j = pick[t]; n = leaf[ar, j]; k = pair[:, t]; b = side[t]
        kid[ar, n] = k; up[ar, k] = n; up[ar, k + 1] = n
        leaf[ar, j] = k + b; leaf[ar, t + 1] = k + 1 - b
    for t in range(P - 1, -1, -1):
        k = pair[:, t]; cnt[ar, up[ar, k]] = cnt[ar, k] + cnt[ar, k + 1]
    return kid, up, cnt
def quads(rng, kid, cnt, top, drop):
    T = N * 8; Q = 4 * R; ar = np.arange(T)[:, None]; ar3 = ar[:, :, None]
    ok = cnt >= 4; order = np.argsort(~ok, axis=1, kind="stable"); num = np.sum(ok, axis=1)[:, None]
    x = order[ar, np.minimum((rng.random((T, Q)) * num).astype(np.int64), num - 1)]
    c = np.full((T, Q, 4), -1, np.int64); c[:, :, 0] = np.where(rng.random((T, Q)) < top, 0, x)
    for w in (1, 2, 3):
        k = kid[ar3, np.maximum(c, 0)]
        t = np.argmax(np.where((c >= 0) & (k >= 0), rng.random(c.shape), -1.0), axis=2)[..., None]
        k = np.take_along_axis(k, t, 2); np.put_along_axis(c, t, k, 2); c[:, :, w] = k[..., 0] + 1
    m = rng.random((T, Q, 1)) < drop
    for w in range(4):
        k = kid[ar3, c]; go = m & (k >= 0) & (rng.random(c.shape) < 0.3)
        c = np.where(go, k + rng.integers(0, 2, c.shape), c)
    return np.take_along_axis(c, np.argsort(rng.random(c.shape), axis=2), 2)
def parts(rng, deep=0.2, top=0.15, drop=0.5):
    kid, up, cnt = trees(rng, deep)
    return {"s": rng.integers(0, 256, (N, 8, 16, V)), "m": rng.integers(0, 256, (N, 8, 16, V)), "kid": kid, "up": up,
            "a": rng.integers(0, 256, (N, 8, 16, R)), "a0": rng.integers(0, 256, (N, 8, 16, R)), "lk": rng.integers(0, R, (N, 8, L, R)), "cut0": quads(rng, kid, cnt, top, drop)}
def pack(d):
    q = {}
    for k in ("s", "m", "kid", "up", "a", "a0", "lk", "cut0"):
        v = d[k]
        if k in ("kid", "up"): q[k] = np.ascontiguousarray(v.reshape(N, 8, V)).astype(np.int32)
        elif k in ("lk", "cut0"): q[k] = np.stack([gtable(x) for x in v.reshape(N, 8, -1)])
        else: q[k] = np.ascontiguousarray(v.reshape(N, 128, -1)).astype(np.float32).astype(BF)
    return q
def setup_inputs(rng):
    return pack(parts(rng))
def setup_inputs_ties(rng):
    d = parts(rng, 0.2, 0.3, 0.4)
    d["a"] = rng.integers(1, 3, (N, 8, 16, R)); d["a0"] = rng.integers(1, 3, (N, 8, 16, R))
    d["s"] = np.repeat(rng.integers(0, 3, (N, 8, 1, V)) * rng.choice(np.array([1, 7, 100]), (N, 8, 1, 1)), 16, axis=2)
    d["s"][:, 3] = 7; d["s"][:, 5] = np.where(rng.random((N, 16, V)) < 0.5, 1, 2)
    return pack(d)
def setup_inputs_deep(rng):
    T = N * 8; Q = 4 * R; deep = rng.choice(np.array([0.0, 0.9, 1.0]), (1, T)); deep[0, 0] = 1.0; deep[0, T - 1] = 0.0
    d = parts(rng, deep, 0.05, 0.3); n = np.arange(V)[None, :]
    leaf = np.argsort(np.where((d["kid"] < 0) & (n != 1), n, V + n), axis=1)[:, :V // 2]
    at = rng.integers(0, V // 2 - 3, (T, Q)); at[:, 0] = 0; at[:, 1] = V // 2 - 4
    m = rng.random((T, Q)) < 0.4; m[:, :2] = True
    four = leaf[np.arange(T)[:, None, None], at[:, :, None] + np.arange(4)]
    four = np.take_along_axis(four, np.argsort(rng.random(four.shape), axis=2), 2)
    d["cut0"] = np.where(m[:, :, None], four, d["cut0"])
    return pack(d)
def top_end(rng, d, g):
    ar = np.arange(N); c = d["cut0"].reshape(N, 8, R, 4, 4).copy(); k = d["kid"].reshape(N, 8, V)[:, g]; u = d["up"].reshape(N, 8, V)[:, g]
    q = c[:, g].reshape(N, 4 * R, 4); sib = np.any(q[..., None, :] == (q ^ 1)[..., :, None], axis=3)
    q = np.take_along_axis(q, np.argsort(~sib, axis=2, kind="stable"), 2)
    inner = k[ar[:, None, None], q] >= 0; good = (np.sum(sib, axis=2) == 2) & inner[..., 2] & inner[..., 3]
    p = q[ar, np.argmax(good, axis=1)]
    c[:, g] = q.reshape(N, R, 4, 4); c[:, g, ::2, 0] = p[:, None, :]; d["cut0"] = c
    j = rng.integers(0, 16, (N, V))
    j[ar, p[:, 0]] = 2; j[ar, p[:, 1]] = 2; j[ar, u[ar, p[:, 0]]] = 2; j[ar, p[:, 2]] = 1; j[ar, p[:, 3]] = 1
    d["s"][:, g] = 255 - (np.arange(16)[None, :, None] == j[:, None, :]).astype(np.int64)
    d["a"][:, g] = rng.integers(254, 256, (N, 16, R)); d["a"][:, g, 12:] = 255; d["a"][:, g, 1, ::2] = 254; d["a"][:, g, 2, ::2] = 255
    d["a0"][:, g] = rng.integers(0, 2, (N, 16, R))
def setup_inputs_ends(rng):
    d = parts(rng)
    for k in ("s", "m", "a", "a0"):
        e = rng.random(d[k].shape); d[k] = np.where(e < 0.4, 255, np.where(e < 0.7, 0, d[k]))
    for k in ("s", "m", "a"): d[k][:, 0] = 255
    d["a"][:, 1, :, ::2] = 0; d["s"][:, 2] = 0
    d["lk"][:, ::2] = rng.choice(np.array([0, R - 1]), (N, 4, L, R))
    top_end(rng, d, 7)
    return pack(d)
def setup_inputs_alike(rng):
    d = parts(rng, 0.0, 1.0, 0.2)
    d["lk"][:, 1::2] = rng.integers(0, R, (N, 4, 1, 1))
    c = d["cut0"].reshape(N, 8, R, 16).copy(); c[:, ::2] = c[:, ::2, :1].copy(); d["cut0"] = c
    d["a"][:, :4] = np.repeat(d["a"][:, :4, :, :R // 16], 16, axis=3); d["a0"][:, 2:6, :, :R // 2] = d["a"][:, 2:6, :, :R // 2]
    return pack(d)
def setup_inputs_spread(rng):
    d = parts(rng)
    for k in ("s", "m", "a", "a0"):
        n = d[k].shape[3]; d[k] = np.floor(np.exp2(8 * rng.random((N, 8, 1, n))) * rng.random((N, 8, 16, n))).astype(np.int64)
    return pack(d)
def check_inputs(d):
    bad = []
    for k in ("s", "m", "a", "a0"):
        x = np.asarray(d[k]).astype(np.float32)
        if not np.all((x >= 0) & (x <= 255) & (x == np.floor(x))): bad.append("numbers of " + k)
    if np.min(d["lk"]) < 0 or np.max(d["lk"]) > R - 1: bad.append("range of lk")
    if np.min(d["cut0"]) < 2 or np.max(d["cut0"]) > V - 1: bad.append("range of cut0")
    T = N * 8; kid = np.asarray(d["kid"]).astype(np.int64).reshape(T, V); up = np.asarray(d["up"]).astype(np.int64).reshape(T, V)
    if np.min(kid) < -1 or np.max(kid) > V - 1 or np.min(up) < 0 or np.max(up) > V - 1: return bad + ["range of the trees"]
    ar = np.arange(T)[:, None]; n = np.arange(V)[None, :]
    ok = np.all(up[:, :2] == 0) and np.all(kid[:, 1] == -1) and np.all((kid == -1) | ((kid >= 2) & (kid % 2 == 0)))
    ok = ok and np.all(kid[ar, up][:, 2:] == (n - n % 2)[:, 2:]) and np.all(up[:, 0::2] == up[:, 1::2])
    ok = ok and np.all((kid < 0) | (up[ar, np.maximum(kid, 0)] == n))
    jump = [up]; dep = np.where(n == 0, 0, 1) + np.zeros((T, 1), np.int64); K = V.bit_length()
    for k in range(K):
        dep = dep + dep[ar, jump[-1]]; jump.append(jump[-1][ar, jump[-1]])
    if not ok or np.any(jump[-1]): return bad + ["trees"]
    if "range of cut0" in bad: return bad
    c = np.stack([gentries(np.asarray(x)) for x in d["cut0"]]).astype(np.int64).reshape(T, 4 * R, 4); wrong = False
    for i in range(4):
        for j in range(i):
            x, y = c[:, :, i], c[:, :, j]; dx, dy = dep[ar, x], dep[ar, y]
            low = np.where(dx >= dy, x, y); high = np.where(dx >= dy, y, x); dif = np.abs(dx - dy)
            for k in range(K): low = np.where(((dif >> k) & 1) > 0, jump[k][ar, low], low)
            wrong = wrong or bool(np.any(low == high))
    if wrong: bad.append("quads of cut0")
    return bad
def reference(s, m, kid, up, a, a0, lk, cut0):
    def rows(x, n): return np.ascontiguousarray(x.astype(np.float32).astype(np.int64).reshape(N, 8, 16, n).transpose(0, 1, 3, 2))
    sv, mv, av, ka = rows(s, V), rows(m, V), rows(a, R), rows(a0, R)
    kd, pu = kid.astype(np.int64), up.astype(np.int64)
    lv = np.stack([gentries(x) for x in lk]).astype(np.int64).reshape(N, 8, L, R)
    cut = np.stack([gentries(x) for x in cut0]).astype(np.int64).reshape(N, 8, R, 4, 4)
    G3 = np.arange(8)[:, None, None]; G4 = G3[..., None]; E = np.zeros((N, 8, R, 16), np.int64)
    def at(x, i): return np.take_along_axis(x, i, 3)
    for h in range(N):
        newcut = []; newa = []
        for r in range(N):
            b = (r - h) % N; x = av[b]; w = lv[b]
            dist = np.sum(np.abs(x[:, None] - ka[r][G3, w]).reshape(8, L, R, 4, 4), axis=4)
            best = np.argmin(dist, axis=1)
            own = w[G3, best, np.arange(R)[None, :, None]]
            c = cut[r][G3, own, np.arange(4)[None, None, :]]
            xx = x[:, :, None, None, :]
            for step in range(S):
                k = kd[r][G4, c]; p = pu[r][G4, c]
                err = np.where(k >= 0, np.sum(sv[r][G4, c] * xx, axis=4), -1)
                cost = np.sum(sv[r][G4, p] * xx, axis=4)
                i = np.argmax(err, axis=3)[..., None]; free = np.arange(4) != i
                mate = (c[..., None, :] == (c ^ 1)[..., :, None]) & free[..., None, :] & free[..., :, None]
                pair = np.any(mate, axis=4); j = np.argmax(pair, axis=3)[..., None]
                j2 = np.argmax(np.take_along_axis(mate, j[..., None], 3)[..., 0, :], axis=3)[..., None]
                go = np.any(pair, axis=3)[..., None] & (at(cost, j) < at(err, i)); left = at(k, i)
                new = c.copy()
                np.put_along_axis(new, i, left, 3); np.put_along_axis(new, j, at(p, j), 3); np.put_along_axis(new, j2, left + 1, 3)
                c = np.where(go, new, c)
            E[b] += x * np.sum(mv[r][G4, c], axis=(2, 3))
            newcut.append(c); newa.append(x)
        cut = np.stack(newcut); ka = np.stack(newa)
    return {"ye": np.ascontiguousarray(E.transpose(0, 1, 3, 2)).reshape(N, 128, R).astype(np.float32), "yc": np.stack([gtable(x.reshape(8, -1)) for x in cut]).astype(np.float32)}

@@ -1,0 +1,782 @@
+import numpy as np
+from concourse.mybir import dt, AluOpType, ActivationFunctionType
+ADD, SUB, MUL, MAX, MIN = AluOpType.add, AluOpType.subtract, AluOpType.mult, AluOpType.max, AluOpType.min
+EQ, GT, LT, GE, AND = AluOpType.is_equal, AluOpType.is_gt, AluOpType.is_lt, AluOpType.is_ge, AluOpType.bitwise_and
+SHR = AluOpType.arith_shift_right
+ACT = ActivationFunctionType
+F32, F16, BF, I32, U16 = "float32", "float16", "bfloat16", "int32", "uint16"
+N = 4
+D5 = [128, 2, 8, 4, 4]
+U4 = [128, 2, 8, 4]
+SCRATCH = {}
+ALIAS = {}
+
+
+def _m(buf, names, shape, dtype):
+    names = names.split()
+    for i, n in enumerate(names):
+        ALIAS[n] = (buf, i)
+    SCRATCH[buf] = ("sbuf", [128, len(names)] + shape[1:], dtype)
+
+
+def _b(names, shape, dtype, where="sbuf"):
+    for n in names.split():
+        SCRATCH[n] = (where, shape, dtype)
+
+
+_b("A0 B0 K0 A1 B1 K1", [128, 2, 2, 8, 4, 4], F32, "psum")
+_b("fb", [128, 512], F32, "psum")
+_b("mb", [128, 4, 2, 8, 2, 4], F32, "psum")
+_b("av0 av1 av2 av3 ak0", [128, 384], BF)
+_b("lku0 lku1 lku2 lku3", [128, 96], U16)
+_b("lki", [128, 96], I32)
+_b("aexp0 aexp1", [128, 4, 1536], BF)
+_b("aexq0 aexq1", [128, 2, 1536], BF)
+_b("st mt sm", [128, 2048], BF)
+_b("w1 w2 num", [128, 4096], BF)
+_m("tmp2", "tmpn tmpm", [128, 2048], BF)
+_b("tmpu", [128, 1024], BF)
+_b("kidi upi", [128, 128], I32)
+_b("khi klo kmk", [128, 128], BF)
+_b("uhi ulo usg", [128, 64], BF)
+_b("upe ubit", [128, 64], I32)
+_b("km8", [128, 2048], BF)
+_b("k2i", [128, 8, 16], I32)
+_b("u2i", [128, 8, 32], I32)
+_b("k2h", [128, 128], F16)
+_b("u2h u2b", [128, 8, 16], F16)
+_m("lk2", "lkl lkr", [128, 128], U16)
+_m("lu2", "lup lup2", [128, 64], U16)
+_b("cuti", [128, 384], I32)
+_b("fw", [128, 384], F32)
+_b("fu", [128, 384], U16)
+_b("mg", [128, 6144], BF)
+_m("ef", "ef0 ef1 ef2 yes", [128, 384], F32)
+_b("el1 el2", [128, 384], F32)
+_b("el3a el3b", [128, 192], F32)
+_m("eh", "ef3a ef3b", [128, 192], F32)
+_m("idt", "i16 n1 n2 n3 n4", [128, 128], F16)
+_b("ib nb", [128, 128], BF)
+_b("i32", [128, 128], F32)
+_b("ones4", [128, 2, 8], F32)
+_b("g8", [128, 8], F32)
+_b("g8i", [128, 128], BF)
+_b("pkk", [128, 8, 2], F32)
+_b("pick", [128, 4, 8, 4], F32)
+_b("qb", [128, 32], BF)
+_b("gx", [128, 32], F32)
+_b("r2", [128, 48], F16)
+_b("pi", [128, 5], I32)
+_b("pc", [128, 5], F32)
+_b("io16 clm clx", [128, 16], F32)
+_b("koff", [128, 96], F32)
+_m("gms", "gl gkl gkr", [128, 8], BF)
+_m("pks", "pk1 pk0 pkz", [128, 2, 8, 4], BF)
+_b("bias1", [128, 64, 4], BF)
+_m("cks", "cb cz ck2", [128, 2, 2, 8, 4, 4], BF)
+_b("lkf", [128, 96], F32)
+_b("lkx", [128, 4, 24, 16], F32)
+_b("absd dif", [128, 1536], BF)
+_b("dcp", [128, 256], F32)
+_b("dm2", [128, 2, 128], F32)
+_b("owi owk", [128, 16, 8], I32)
+_b("owp", [128, 16, 2, 8], F16)
+_b("owl0 owl1", [128, 96], U16)
+for _h in "01":
+    _b("G" + _h, [128, 768], F32)
+    _m("qd" + _h, " ".join(n + _h for n in "cs h16 e v v1 v2 fm px pa pb pd".split()), D5, F16)
+    _b("kf" + _h, D5, F32)
+    _b("l1" + _h, [128, 2, 96], U16)
+    _b("xl" + _h, [128, 96], U16)
+    _b("sq%s pm%s" % (_h, _h), [128, 2, 2, 8, 4, 4], BF)
+    _b("ph" + _h, [128, 2, 2, 8, 4, 4], F16)
+    _b("prA%s prB%s" % (_h, _h), [128, 1536], F32)
+    _b("kc%s m2%s" % (_h, _h), [128, 2, 8, 4, 2], F32)
+    _b("mx" + _h, U4, F32)
+    _b("pr" + _h, [128, 8, 2, 2, 4, 4], F16)
+    _b("ng" + _h, [128, 1536], BF)
+    _b("uw" + _h, [128, 24, 2, 8, 4], F16)
+    _b("uf" + _h, [128, 4, 2, 8, 4], F32)
+SEMAPHORES = ["cV", "cS", "cP", "cG", "lsem"] + ["ar%d" % h for h in (1, 2, 3)] + ["er%d" % h for h in (1, 2, 3, 4)] + ["d%d" % i for i in range(60)]
+WHOLE = np.s_[:]
+
+
+def rank_program(g, core, T, topo):
+    rank = T.rank_of(core)
+    if rank is None:
+        return
+    ENG = {"V": g.vector, "S": g.scalar, "P": g.tensor, "G": g, "Y": g.sync}
+    cnt = {"cV": 0, "cS": 0, "cP": 0, "cG": 0}
+    total = {}
+    known = {e: {} for e in ENG}
+    ops = []
+    wr, rd, cache, bank = {}, {}, {}, {}
+    ndma = [0]
+    prog = []
+
+    def R(name, idx=WHOLE):
+        if name in ALIAS:
+            ix = idx if isinstance(idx, tuple) else (idx,)
+            return (ALIAS[name][0], (ix[0], ALIAS[name][1]) + ix[1:])
+        return (name, idx)
+
+    def IND(win, off):
+        return ("@", win, off)
+
+    def ap(r):
+        if r[0] == "@":
+            return ap(r[1]).indirect(ap(r[2]))
+        return T[r[0]][r[1]]
+
+    def psum(r):
+        return SCRATCH[r[0]][0] == "psum"
+
+    def size(n):
+        return 16 * 4096 if n == "num" else int(np.prod(SCRATCH[n][1][1:]))
+
+    def cols(r):
+        key = (r[0], repr(r[1]))
+        if key not in cache:
+            ix = r[1] if isinstance(r[1], tuple) else (r[1],)
+            if r[0] == "num":
+                rows = np.unique(np.arange(128)[ix[0]] % 16)
+                c = np.arange(16 * 4096).reshape(16, 4096)[rows][:, ix[1] if len(ix) > 1 else WHOLE]
+            else:
+                c = np.arange(size(r[0])).reshape(SCRATCH[r[0]][1][1:])[ix[1:]]
+            cache[key] = np.unique(c.reshape(-1))
+        return cache[key]
+
+    def parts(rs):
+        out = []
+        for r in rs:
+            if r[0] == "@":
+                out += [r[1], r[2]]
+            elif r[0] in SCRATCH:
+                out.append(r)
+        return out
+
+    def hazards(W, L, outs, ins, skip):
+        need = set()
+        for r in list(ins) + list(outs):
+            if not psum(r) and r[0] in W:
+                need.update(np.unique(W[r[0]][cols(r)]).tolist())
+        for r in outs:
+            if psum(r):
+                continue
+            c, keep = cols(r), []
+            for (o, m) in L.get(r[0], []):
+                if m[c].any():
+                    if not skip(o):
+                        need.add(o)
+                    m[c] = False
+                    if not m.any():
+                        continue
+                keep.append((o, m))
+            L[r[0]] = keep
+        need.discard(-1)
+        return need
+
+    def note(W, L, o, outs, ins):
+        for r in outs:
+            if not psum(r):
+                if r[0] not in W:
+                    W[r[0]] = np.full(size(r[0]), -1)
+                W[r[0]][cols(r)] = o
+        for r in ins:
+            if not psum(r):
+                m = np.zeros(size(r[0]), bool)
+                m[cols(r)] = True
+                L.setdefault(r[0], []).append((o, m))
+
+    def waits(e, outs, ins, queued):
+        need = hazards(wr, rd, outs, ins, lambda o: queued and ops[o][0] == e)
+        for r in outs + ins:
+            if psum(r):
+                need.update(o for e2, o in bank.get(r[0], {}).items() if e2 != e)
+        k, want = known[e], {}
+        for o in need:
+            _, s, c, snap = ops[o]
+            if k.get(s, 0) < c and (s not in want or want[s][0] < c):
+                want[s] = (c, snap)
+        for s in list(want):
+            if any(s2 != s and want[s2][1].get(s, 0) >= want[s][0] for s2 in want):
+                del want[s]
+        for s, (c, snap) in want.items():
+            if k.get(s, 0) >= c:
+                continue
+            ENG[e].wait_ge(T.sem[s], c)
+            for s2, c2 in snap.items():
+                k[s2] = max(k.get(s2, 0), c2)
+            k[s] = max(k.get(s, 0), c)
+
+    def issued(e, s, c, snap, outs, ins):
+        total[s] = c
+        ops.append((e, s, c, snap))
+        note(wr, rd, len(ops) - 1, outs, ins)
+        for r in outs + ins:
+            if psum(r):
+                bank.setdefault(r[0], {})[e] = len(ops) - 1
+
+    def issue(o):
+        e, outs, ins, a = o["e"], o["o"], o["i"], o["a"]
+        if o["k"] == "arr":
+            issued(None, a[0], a[1], {}, outs, [])
+            return
+        if o["k"] == "send":
+            waits("G", [], ins, False)
+            src, dst, dstname, s = a
+            rid, pid = topo.addr(dst, core)
+            g.remote_dma(T[dstname][:], ap(src), T.sem[s], T.sem.lsem, pid, rid, topo.mask(core, dst))
+            total["lsem"] = total.get("lsem", 0) + len(topo.engines(core, dst))
+            return
+        waits(e, outs, ins, o["k"] == "op")
+        if o["k"] == "dma":
+            s = "d%d" % ndma[0]
+            ndma[0] += 1
+            ENG[e].dma_start(ap(a[0]), ap(a[1])).then_inc(T.sem[s], 16)
+            issued(None, s, 16, dict(known[e]), outs, ins)
+        else:
+            s = "c" + e
+            cnt[s] += 1
+            a().then_inc(T.sem[s], 1)
+            issued(e, s, cnt[s], dict(known[e]), outs, ins)
+
+    def op(e, outs, ins, fn):
+        o, i = parts(outs), parts(ins)
+        ind = any(r[0] == "@" for r in list(outs) + list(ins))
+        if ind:
+            d = 60 + 1.7 * len(cols(outs[0]))
+        elif e == "P":
+            d = 0.52 * max(min(64, len(cols(ins[0]))), len(cols(ins[1]))) * (4 if SCRATCH[ins[0][0]][2] == F32 else 1)
+        else:
+            n = max(len(cols(r)) // (16 if r[0] == "num" else 1) for r in o + i)
+            d = 200 + 2 * n if e == "G" else max(64, n * (2 if e == "V" and len(ins) == 2 and not any(psum(r) for r in i) else 1))
+        prog.append({"k": "op", "e": e, "o": o, "i": i, "a": fn, "d": d, "lat": 0})
+
+    def dma(e, out, in_):
+        prog.append({"k": "dma", "e": e, "o": parts([out]), "i": parts([in_]), "a": (out, in_), "d": 60, "lat": 2200})
+
+    def arrival(names, s, c, lat):
+        prog.append({"k": "arr", "e": "X", "o": [R(n) for n in names.split()], "i": [], "a": (s, c), "d": 0, "lat": lat})
+
+    def send(src, dst, dstname, s):
+        prog.append({"k": "send", "e": "G", "o": [R(dstname)], "i": [R(src)], "a": (R(src), dst, dstname, s), "d": 1200, "lat": 0})
+
+    def schedule():
+        n = len(prog)
+        W, L, hist, pre = {}, {}, {}, []
+        for i, o in enumerate(prog):
+            S = hazards(W, L, o["o"], o["i"], lambda j: False)
+            note(W, L, i, o["o"], o["i"])
+            for b in set(r[0] for r in o["o"] + o["i"] if psum(r)):
+                hb = hist.setdefault(b, {"P": [], "V": [], "S": []})
+                if o["e"] == "P":
+                    S.update(hb["P"][-1:] + hb["V"] + hb["S"])
+                    hb["V"], hb["S"] = [], []
+                else:
+                    S.update(hb["P"][-1:] + hb["S" if o["e"] == "V" else "V"][-1:])
+                hb[o["e"]].append(i)
+            S.discard(i)
+            pre.append(S)
+        suc = [[] for _ in range(n)]
+        for i, S in enumerate(pre):
+            for j in S:
+                suc[j].append(i)
+        WAKE, OV = 130, 35
+        gap = lambda i, j: 0 if prog[i]["e"] == prog[j]["e"] == "P" else WAKE
+        prio = [0.0] * n
+        for i in range(n - 1, -1, -1):
+            prio[i] = max([prio[j] + gap(i, j) for j in suc[i]] + [0.0]) + prog[i]["d"] + prog[i]["lat"]
+        left, ready = [len(S) for S in pre], [0.0] * n
+        avail, t = {e: [] for e in "XYGPSV"}, {e: 0.0 for e in "XYGPSV"}
+        for i in range(n):
+            if not left[i]:
+                avail[prog[i]["e"]].append(i)
+        order = []
+        while len(order) < n:
+            pick = None
+            for e in "XYGPSV":
+                if avail[e]:
+                    now = max(t[e], min(ready[i] for i in avail[e]))
+                    if pick is None or now < pick[0]:
+                        pick = (now, max((i for i in avail[e] if ready[i] <= now), key=lambda i: (prio[i], -i)), e)
+            now, c, e = pick
+            avail[e].remove(c)
+            end = now + prog[c]["d"] + OV
+            if e != "X":
+                t[e] = end
+            order.append(c)
+            for j in suc[c]:
+                ready[j] = max(ready[j], end + prog[c]["lat"] + gap(c, j))
+                left[j] -= 1
+                if not left[j]:
+                    avail[prog[j]["e"]].append(j)
+        return order
+
+    def tt(out, a, b, o):
+        op("V", [out], [a, b], lambda: g.vector.tensor_tensor(ap(out), ap(a), ap(b), o))
+
+    def tc(out, a):
+        op("V", [out], [a], lambda: g.vector.tensor_copy(ap(out), ap(a)))
+
+    def ts(out, a, s1, o1, s2=None, o2=None):
+        v = lambda x: ap(x) if isinstance(x, tuple) else x
+        ins = [a] + [x for x in (s1, s2) if isinstance(x, tuple)]
+        if o2 is None:
+            op("V", [out], ins, lambda: g.vector.tensor_scalar(ap(out), ap(a), v(s1), None, o1))
+        else:
+            op("V", [out], ins, lambda: g.vector.tensor_scalar(ap(out), ap(a), v(s1), v(s2), o1, o2))
+
+    def ms(out, c):
+        op("V", [out], [], lambda: g.vector.memset(ap(out), c))
+
+    def act(out, a, f=ACT.Copy, bias=0.0, scale=1.0):
+        col = isinstance(scale, tuple)
+        op("S", [out], [a] + ([scale] if col else []), lambda: g.scalar.activation(ap(out), ap(a), f, bias=bias, scale=ap(scale) if col else scale))
+
+    def mm(out, l, r, start, stop):
+        op("P", [out], [l, r], lambda: g.tensor.matmul(ap(out), ap(l), ap(r), start, stop))
+
+    def group(lst):
+        for i, (o, l, r) in enumerate(lst):
+            mm(o, l, r, i == 0, i == len(lst) - 1)
+
+    def sel(out, in_, pattern, cmp, fill, base, cm):
+        op("G", [out], [in_], lambda: g.affine_select(ap(out), ap(in_), pattern, cmp, fill, base, cm))
+
+    def iota(out, pattern, base, cm):
+        if SCRATCH[out[0]][2] == I32:
+            op("G", [out], [], lambda: g.iota(ap(out), pattern, base, cm))
+        else:
+            op("G", [out], [], lambda: g.iota(ap(out), pattern, base, cm, allow_small_or_imprecise_dtypes=True))
+
+    s_ = np.s_
+    P96 = slice(0, 96)
+    I96 = lambda n: R(n, s_[0:96, 0:96])
+    cores = list(T.cores)
+    nxt = lambda h: cores[(rank + h) % N]
+
+    dma("Y", R("av0"), ("a", s_[:, :]))
+    dma("S", R("lki"), ("lk", s_[:, :]))
+    dma("Y", R("ak0"), ("a0", s_[:, :]))
+    dma("S", R("kidi"), ("kid", s_[:, :]))
+    dma("Y", R("cuti"), ("cut0", s_[:, :]))
+    dma("S", R("upi"), ("up", s_[:, :]))
+    dma("Y", R("st"), ("s", s_[:, :]))
+    ms(R("i16"), 1.0)
+    sel(R("i16"), R("i16"), [[-1, 128]], EQ, 0.0, 0, 1)
+    ms(R("qb"), 2048.0)
+    ms(R("gx"), 1.0)
+    sel(R("qb"), R("qb"), [[-16, 8], [-4, 4]], GE, 0.0, 0, 1)
+    sel(R("qb"), R("qb"), [[16, 8], [4, 4]], GE, 0.0, 3, -1)
+    iota(R("pi", s_[:, 0:1]), [[0, 1]], 0, 1)
+    sel(R("gx"), R("gx"), [[-16, 8], [0, 4]], GE, 0.0, 0, 1)
+    sel(R("gx"), R("gx"), [[16, 8], [0, 4]], GE, 0.0, 15, -1)
+    iota(R("koff"), [[512, 4], [0, 24]], 0, 0)
+    iota(R("io16"), [[1, 16]], 0, 0)
+    ms(R("r2"), 1.0)
+    sel(R("r2"), R("r2"), [[-2, 48]], GE, 0.0, 0, 1)
+    sel(R("r2"), R("r2"), [[2, 48]], GE, 0.0, 1, -1)
+    ms(R("pick"), 1.0)
+    sel(R("pick"), R("pick"), [[-4, 4], [-16, 8], [-1, 4]], EQ, 0.0, 0, 1)
+    ms(R("ones4"), 4.0)
+    sel(R("ones4"), R("ones4"), [[0, 2], [-16, 8]], GE, 0.0, 0, 1)
+    sel(R("ones4"), R("ones4"), [[0, 2], [16, 8]], GE, 0.0, 15, -1)
+    iota(R("bias1"), [[0, 64], [-1, 4]], 3, 0)
+    tc(R("lku0"), R("lki"))
+    for h in (1, 2, 3):
+        send("av0", nxt(h), "av%d" % h, "ar%d" % h)
+        send("lku0", nxt(h), "lku%d" % h, "ar%d" % h)
+        arrival("av%d lku%d" % (h, h), "ar%d" % h, 2 * len(topo.engines(nxt(-h), core)), 8000)
+    ts(R("pi", s_[:, 1:2]), R("pi", s_[:, 0:1]), 1, AND)
+    ts(R("pi", s_[:, 2:3]), R("pi", s_[:, 0:1]), 1, SHR, 7, AND)
+    ts(R("pi", s_[:, 3:4]), R("pi", s_[:, 0:1]), 2, SHR, 1, AND)
+    ts(R("pi", s_[:, 4:5]), R("pi", s_[:, 0:1]), 15, AND)
+    tc(R("pc", s_[:, 0:1]), R("pi", s_[:, 1:2]))
+    ts(R("pc", s_[:, 1:2]), R("pi", s_[:, 1:2]), -1.0, MUL, 1.0, ADD)
+    tc(R("pc", s_[:, 2:3]), R("pi", s_[:, 2:3]))
+    ts(R("pc", s_[:, 3:4]), R("pi", s_[:, 3:4]), 2048.0, MUL)
+    tc(R("pc", s_[:, 4:5]), R("pi", s_[:, 4:5]))
+    ts(R("clm"), R("io16"), R("pc", s_[:, 2:3]), EQ)
+    ts(R("clx"), R("io16"), R("pc", s_[:, 4:5]), EQ)
+
+    def dist(h):
+        av, lku, ow = "av%d" % h, "lku%d" % h, "owl%d" % (h % 2)
+        ak = "ak0" if h == 0 else "av%d" % (h - 1)
+        for k in range(4):
+            c = s_[:, 384 * k:384 * k + 384]
+            i = IND(R(ak, s_[:, 0:384]), R(lku, s_[:, 24 * k:24 * k + 24]))
+            if h == 0:
+                tt(R("dif", c), i, R(av), SUB)
+                act(R("absd", c), R("dif", c), ACT.Abs)
+            else:
+                act(R("dif", c), i)
+        for k in range(4 if h else 0):
+            c = s_[:, 384 * k:384 * k + 384]
+            group([(R("fb", s_[:, 0:384]), R("ib"), R("dif", c)), (R("fb", s_[:, 0:384]), R("nb"), R(av))])
+            act(R("absd", c), R("fb", s_[:, 0:384]), ACT.Abs)
+        ts(R("lkf"), R(lku), 1.0, MUL)
+        tt(R("lkf"), R("lkf"), R("koff"), ADD)
+        for cl in range(16):
+            act(R("lkx", s_[:, :, :, cl]), R("lkf"), ACT.Copy, 0.0, R("clx", s_[:, cl:cl + 1]))
+        for k in range(4):
+            for H in (0, 1):
+                for bl in (0, 1):
+                    o = R("mb", s_[0:96, k, H, :, bl, :])
+                    j = 2 * H + bl
+                    group([(o, R("absd", s_[:, 384 * k + 96 * j:384 * k + 96 * j + 96]), R("qb")),
+                           (o, R("lkx", s_[:, k, 6 * j:6 * j + 6, :]), R("gx"))])
+        act(R("dcp", s_[P96, :]), R("mb", s_[P96, 2:4, :, :, :, :]))
+        tt(R("dm2", s_[P96, :, :]), R("mb", s_[P96, 0:2, :, :, :, :]), R("dcp", s_[P96, :]), MIN)
+        tt(R("owi", s_[P96]), R("dm2", s_[P96, 0, :]), R("dm2", s_[P96, 1, :]), MIN)
+        ts(R("owk", s_[P96]), R("owi", s_[P96]), 511, AND)
+        for b in (0, 1):
+            ts(R("owp", s_[P96, :, b, :]), R("owk", s_[P96]), R("pc", s_[P96, 1 - b:2 - b]), MUL)
+        for H in (0, 1):
+            mm(R("mb", s_[:, 0, H, 0:6, :, :]), R("owp", s_[P96, 8 * H:8 * H + 8, :, :]), R("r2", s_[P96, :]), True, True)
+        tc(R(ow), R("mb", s_[:, 0, :, 0:6, :, :]))
+
+    def inherit(h, H):
+        x = str(H)
+        A, G = "A" + x, "G" + x
+        act(R(G), IND(R("fw", s_[:, 0:384]), R("owl%d" % (h % 2), s_[:, 48 * H:48 * H + 48])))
+        for bl in (0, 1):
+            for q in range(4):
+                mm(R(A, s_[P96, 0, bl, :, q, :]), R(G, s_[:, 4 * bl + q::8]), R("pick", s_[:, q, :, :]), True, True)
+        tc(R("cs" + x, s_[P96]), R(A, s_[P96, 0]))
+        for bl in (0, 1):
+            mm(R(A, s_[:, 1, bl, 0:6, :, :]), R("cs" + x, s_[P96, bl]), I96("i16"), True, True)
+        tc(R("l1" + x), R(A, s_[:, 1, :, 0:6, :, :]))
+
+    def gather1(h, H):
+        x = str(H)
+        A, B, K = "A" + x, "B" + x, "K" + x
+        ax, h16 = "aexp%d" % (h % 2), "h16" + x
+        for bl, pr in ((0, "prA" + x), (1, "prB" + x)):
+            tt(R(pr), IND(R("sm", s_[:, 0:2048]), R("l1" + x, s_[:, bl, :])), R(ax, s_[:, 2 * H + bl, :]), MUL)
+        ts(R(h16, s_[P96]), R("cs" + x, s_[P96]), 0.5, MUL, 1023.75, ADD)
+        ends = ((R(B, s_[P96, 0, :, :, :, 0:3]), R(A, s_[P96, 1, :, :, :, 0:3]), 3, 1), (R(B, s_[P96, 0, :, :, :, 3:4]), R(A, s_[P96, 1, :, :, :, 3:4]), 1, 3),
+                (R(B, s_[P96, 1, :, :, :, 0:2]), R(B, s_[P96, 1, :, :, :, 2:4]), 2, 2))
+        for (o, o2, n, dl) in ends:
+            group([(o, I96("i16"), R(h16, s_[P96, :, :, :, 0:n])), (o, I96("n1"), R(h16, s_[P96, :, :, :, dl:dl + n]))])
+        for (o, o2, n, dl) in ends:
+            mm(o2, I96("i16"), R(h16, s_[P96, :, :, :, 0:n]), True, True)
+        for i in (s_[P96, 0], s_[P96, 1, :, :, :, 0:2]):
+            act(R("sq" + x, i), R(B, i), ACT.Square)
+            act(R("pm" + x, i), R("sq" + x, i), ACT.Relu, 1.0, -1.0)
+        tt(R("ph" + x, s_[P96, 0]), R(A, s_[P96, 1]), R("pm" + x, s_[P96, 0]), MUL)
+        tt(R("ph" + x, s_[P96, 1, :, :, :, 0:2]), R(B, s_[P96, 1, :, :, :, 2:4]), R("pm" + x, s_[P96, 1, :, :, :, 0:2]), MUL)
+        lst = [(R(K, s_[P96, 0]), I96("ib"), R("bias1", s_[P96]))]
+        for bl, pr in ((0, "prA" + x), (1, "prB" + x)):
+            for q in range(4):
+                for t in range(4):
+                    lst.append((R(K, s_[P96, 0, bl, :, q, t]), R(pr, s_[:, 4 * q + t::16]), R("ones4", s_[:, 0, :])))
+        group(lst)
+        sl = (((0, 1), 0, 0), ((1, 2), 0, 1), ((2, 3), 0, 2), ((0, 3), 0, 3), ((0, 2), 1, 0), ((1, 3), 1, 1))
+        for t in range(4):
+            group([(R(B, s_[P96, 0, :, :, :, t]), I96("i16"), R("ph" + x, s_[P96, i, :, :, :, j])) for tu, i, j in sl if t not in tu])
+
+    def logic1a(h, H):
+        x = str(H)
+        A, B, K = "A" + x, "B" + x, "K" + x
+        e, pr = "e" + x, "pr" + x
+        tc(R("kc" + x, s_[P96]), R(K, s_[P96, 0, :, :, :, 2:4]))
+        tt(R("m2" + x, s_[P96]), R(K, s_[P96, 0, :, :, :, 0:2]), R("kc" + x, s_[P96]), MAX)
+        tt(R("mx" + x, s_[P96]), R("m2" + x, s_[P96, :, :, :, 0]), R("m2" + x, s_[P96, :, :, :, 1]), MAX)
+        for t in range(4):
+            tt(R(e, s_[P96, :, :, :, t]), R(K, s_[P96, 0, :, :, :, t]), R("mx" + x, s_[P96]), EQ)
+        for l, src in ((0, B), (1, A)):
+            for bl in (0, 1):
+                tt(R(pr, s_[P96, :, bl, l, :, :]), R(src, s_[P96, 0, bl]), R(e, s_[P96, bl]), MUL)
+        o = R(B, s_[:, 1, 0, 0:6, :, :])
+        group([(o, R(pr, s_[P96, :, :, :, :, t]), I96("i16")) for t in range(4)])
+        for bl in (0, 1):
+            group([(R(A, s_[P96, 1, bl, :, 0:2, :]), I96("i16"), R(pr, s_[P96, :, bl, :, :, t])) for t in range(4)])
+        ts(R("xl" + x), o, R("pc", s_[:, 3:4]), ADD)
+
+    def uw(x, i):
+        return R("uw" + x, s_[P96, i])
+
+    def logic1b(h, H):
+        x = str(H)
+        A, K = "A" + x, "K" + x
+        U = lambda n, t: R(n + x, s_[P96, :, :, :, t])
+        for t in range(4):
+            tt(U("v", t), R(A, s_[P96, 1, :, :, 0, :]), U("h16", t), EQ)
+        ts(uw(x, 0), R(A, s_[P96, 1, :, :, 0, :]), -1024.0, ADD)
+        tc(uw(x, 1), R(A, s_[P96, 1, :, :, 1, :]))
+        tt(U("v2", 1), U("v", 1), U("v", 0), MUL)
+        tt(U("v2", 2), U("v", 2), U("v", 3), GT)
+        tt(U("v1", 1), U("v", 1), U("v", 0), GT)
+        tt(U("v1", 2), U("v", 2), U("v", 3), MUL)
+        cf = R(K, s_[P96, 1, :, :, 3, :])
+        group([(cf, I96("ib"), R("cz", s_[P96, 0, :, :, 0, :]))] + [(cf, I96("i16"), U("cs", t)) for t in range(4)] + [(cf, I96("n1"), uw(x, 1)), (cf, I96("n4"), uw(x, 0))])
+        V1 = {0: U("v", 0), 1: U("v1", 1), 2: U("v1", 2)}
+        V2 = {1: U("v2", 1), 2: U("v2", 2), 3: U("v", 3)}
+        for t in (1, 2, 3):
+            tt(uw(x, 2 + t), R(A, s_[P96, 0, :, :, :, t]), V2[t], MUL)
+        tc(uw(x, 2), cf)
+        for t in range(4):
+            tt(U("fm", t), cf, U("cs", t), EQ)
+        tt(R("kf" + x, s_[P96]), R(K, s_[P96, 0]), R("fm" + x, s_[P96]), MUL)
+        return V1, V2
+
+    def gather2(h, H, V1, V2):
+        x = str(H)
+        A, B, K = "A" + x, "B" + x, "K" + x
+        ax, ng = "aexq%d" % (h % 2), "ng" + x
+        U = lambda n, t: R(n + x, s_[P96, :, :, :, t])
+        for w, pr in (("w1", "prA" + x), ("w2", "prB" + x)):
+            tt(R(pr), IND(R(w, s_[:, 0:4096]), R("xl" + x)), R(ax, s_[:, H, :]), MUL)
+        act(R(ng), IND(R("num", s_[:, 0:4096]), R("xl" + x)))
+        reg = lambda hf, r: R(K, s_[P96, hf, :, :, r, :])
+        sc = ["i16", "n1", "n2", "n3"]
+        lst = [(R(K, s_[P96]), I96("ib"), R("ck2", s_[P96]))]
+        for t in (1, 2, 3):
+            lst += [(reg(0, 2), I96(sc[t]), U("e", t)), (reg(0, 3), I96(sc[t]), V2[t]), (reg(1, 2), I96(sc[t]), U("e", t)), (reg(1, 2), I96(sc[t]), V2[t])]
+        for t in (1, 2):
+            lst += [(reg(0, 1), I96(sc[t]), V1[t]), (reg(1, 2), I96(["", "n2", "n4"][t]), V1[t])]
+        for t in range(4):
+            lst.append((reg(1, 1), I96("i32"), R("kf" + x, s_[P96, :, :, :, t])))
+        for w, pr in ((0, "prA" + x), (1, "prB" + x)):
+            for bl in (0, 1):
+                for q in range(4):
+                    if w == 0:
+                        lst.append((R(K, s_[P96, 0, bl, :, 0:2, q]), R(pr, s_[:, 8 * bl + q::16]), R("pkk")))
+                    else:
+                        lst.append((R(K, s_[P96, 1, bl, :, 0, q]), R(pr, s_[:, 8 * bl + q::16]), R("ones4", s_[:, 0, :])))
+                    lst.append((R(K, s_[P96, 0, bl, :, 2 + w, q]), R(pr, s_[:, 8 * bl + 4 + q::16]), R("ones4", s_[:, 0, :])))
+        lb = [(R(B, s_[P96]), I96("ib"), R("cb", s_[P96]))]
+        for bl in (0, 1):
+            for q in range(4):
+                o = R(B, s_[P96, :, bl, :, :, q])
+                lb += [(o, R(ng, s_[:, 8 * bl + 4 + q::16]), R("pk1")), (o, R(ng, s_[:, 8 * bl + q::16]), R("pk0"))]
+        rb = lambda hf, r: R(B, s_[P96, hf, :, :, r, :])
+        lb += [(rb(0, 0), I96("n1"), uw(x, 1)), (rb(1, 3), I96("n4"), uw(x, 0))]
+        for i in (3, 4, 5):
+            lb += [(rb(1, 3), I96("i16"), uw(x, i)), (rb(0, 2), I96("n1"), uw(x, i))]
+        group(lb)
+        la = [(R(A, s_[P96, 1, :, :, 2:4, :]), I96("ib"), R("cz", s_[P96, 1, :, :, 2:4, :]))]
+        for bl in (0, 1):
+            for q in range(4):
+                la.append((R(A, s_[P96, 1, bl, :, 2:4, q]), R(ng, s_[:, 8 * bl + q::16]), R("pkz", s_[:, 0, :, 0:2])))
+        for r in (2, 3):
+            la.append((R(A, s_[P96, 1, :, :, r, :]), I96("n1"), uw(x, 2)))
+        group(la)
+        group(lst)
+
+    def logic2(h, H, V1, V2):
+        x = str(H)
+        A, B, K = "A" + x, "B" + x, "K" + x
+        U = lambda n, t: R(n + x, s_[P96, :, :, :, t])
+        kr = lambda hf, r: R(K, s_[P96, hf, :, :, r, :])
+        rb = lambda hf, r: R(B, s_[P96, hf, :, :, r, :])
+        ra = lambda r: R(A, s_[P96, 1, :, :, r, :])
+        uf = lambda i: R("uf" + x, s_[P96, i])
+        G1, G2, W, O, P2, GW, GN, WKD, Q, OQ = 6, 7, 8, 9, 10, 11, 12, 13, 14, 15
+        ts(uw(x, P2), ra(3), 0.0, EQ)
+        ts(uw(x, O), kr(1, 2), 0.0, GT)
+        tc(uf(0), kr(0, 1))
+        tc(uf(1), kr(0, 2))
+        tt(uw(x, G1), kr(0, 0), R("mx" + x, s_[P96]), LT)
+        tt(uf(2), kr(1, 1), uf(0), MAX)
+        tt(uf(3), kr(0, 3), uf(1), MAX)
+        tt(uw(x, W), kr(0, 3), uf(1), GT)
+        tt(uf(0), kr(1, 0), uf(2), MAX)
+        tt(uw(x, P2), uw(x, P2), uw(x, G1), MUL)
+        tt(uw(x, WKD), rb(1, 0), uw(x, W), MUL)
+        tt(uw(x, G2), uf(3), uf(0), GT)
+        tt(uw(x, Q), rb(1, 2), uw(x, WKD), SUB)
+        tt(uw(x, G2), uw(x, G2), uw(x, P2), MUL)
+        tt(uw(x, OQ), uw(x, O), uw(x, Q), MUL)
+        tt(uw(x, GW), uw(x, G2), uw(x, W), MUL)
+        tt(uf(1), uw(x, WKD), uw(x, OQ), ADD)
+        tt(uw(x, GN), uw(x, G2), uw(x, GW), SUB)
+        tt(uw(x, 16), ra(2), uw(x, OQ), SUB)
+        tt(uw(x, 17), rb(1, 1), uf(1), ADD)
+        tt(uw(x, 18), rb(0, 0), uw(x, G1), MUL)
+        tt(uw(x, 19), rb(0, 2), uw(x, G1), MUL)
+        tt(uw(x, 20), rb(1, 3), uw(x, G1), MUL)
+        tt(uw(x, 21), rb(0, 1), uw(x, GN), MUL)
+        tt(uw(x, 22), rb(0, 3), uw(x, GW), MUL)
+        tt(uw(x, 16), uw(x, 16), uw(x, G2), MUL)
+        tt(uw(x, 17), uw(x, 17), uw(x, G2), MUL)
+        go = lambda r: R(A, s_[P96, 0, :, :, r, :])
+        group([(go(0), I96("i16"), uw(x, 18)), (go(0), I96("i16"), uw(x, 21))])
+        group([(go(2), I96("i16"), uw(x, 19)), (go(2), I96("i16"), uw(x, 22))])
+        mm(go(3), I96("i16"), uw(x, 16), True, True)
+        group([(go(1), I96("i16"), uw(x, 20)), (go(1), I96("i16"), uw(x, 17))])
+        for t in range(4):
+            tt(U("px", t), go(0), U("e", t), MUL)
+        for t in (1, 2, 3):
+            tt(U("pb", t), go(2), V2[t], MUL)
+        for t in range(4):
+            tt(U("pd", t), go(3), U("fm", t), MUL)
+        for t in (0, 1, 2):
+            tt(U("pa", t), go(1), V1[t], MUL)
+        for bl in (0, 1):
+            o = R("fb", s_[:, 192 * H + 96 * bl:192 * H + 96 * bl + 96])
+            group([(o, R(n + x, s_[P96, bl]), I96("i16")) for n in ("cs", "px", "pb", "pd", "pa")])
+        c = s_[:, 192 * H:192 * H + 192]
+        act(R("fw", c), R("fb", c))
+        tc(R("fu", c), R("fb", c))
+
+    def out_half(h, H):
+        n = "3" + "ab"[H]
+        act(R("ef" + n), R("mb", s_[:, 2 * H:2 * H + 2, :, 0:6, :, :]))
+        send("ef" + n, nxt(-h), "el" + n, "er%d" % (3 + H))
+        arrival("el" + n, "er%d" % (3 + H), len(topo.engines(nxt(h), core)), 4000)
+
+    def msum(h, last=False):
+        for b in range(4):
+            o = R("mg", s_[:, 1536 * b:1536 * b + 1536])
+            i = IND(R("mt", s_[:, 0:2048]), R("fu", s_[:, 96 * b:96 * b + 96]))
+            if last and b % 2 == 0:
+                tc(o, i)
+            else:
+                act(o, i)
+        for b in range(4):
+            if last and b == 2:
+                out_half(h, 0)
+            group([(R("mb", s_[:, b, :, 0:6, :, :]), R("ib"), R("mg", s_[:, 1536 * b + t:1536 * b + 1536:16])) for t in range(16)])
+        if last:
+            out_half(h, 1)
+            return
+        act(R("ef%d" % h), R("mb", s_[:, :, :, 0:6, :, :]))
+        if h:
+            send("ef%d" % h, nxt(-h), "el%d" % h, "er%d" % h)
+            arrival("el%d" % h, "er%d" % h, len(topo.engines(nxt(h), core)), 4000)
+
+    def expand(h):
+        for t in range(16):
+            if h == 0:
+                tc(R("aexp0", s_[:, :, t::16]), R("av0"))
+            else:
+                sel(R("aexp%d" % (h % 2), s_[:, :, t::16]), R("av%d" % h), [[0, 384]], EQ, 0.0, 0, 0)
+        for H in (0, 1):
+            for t in range(16):
+                j = 192 * H + 96 * (t // 8)
+                sel(R("aexq%d" % (h % 2), s_[:, H, t::16]), R("av%d" % h, s_[:, j:j + 96]), [[0, 96]], EQ, 0.0, 0, 0)
+
+    ts(R("fw"), R("cuti"), 1.0, MUL)
+    dist(0)
+    ts(R("kmk"), R("kidi"), 0.0, GE)
+    dma("Y", R("km8", s_[0:8, :]), R("kmk"))
+    for gg in range(8):
+        dma("Y", R("k2i", s_[:, gg, :]), ("kid", s_[gg, :]))
+        dma("S", R("u2i", s_[0:64, gg, :]), ("up", s_[gg, :]))
+    dma("Y", R("mt"), ("m", s_[:, :]))
+    tc(R("khi"), R("kidi"))
+    ms(R("num"), 0.0)
+    ms(R("w1", s_[:, 0:1024]), 255.0)
+    ms(R("w2", s_[:, 0:1024]), 255.0)
+    tt(R("klo"), R("kidi"), R("khi"), SUB)
+    tc(R("uhi"), R("upi", s_[:, 0:128:2]))
+    tc(R("upe"), R("upi", s_[:, 0:128:2]))
+    tt(R("ulo"), R("upi", s_[:, 0:128:2]), R("uhi"), SUB)
+    ts(R("ubit"), R("upe"), 1, AND)
+    ts(R("usg"), R("ubit"), -2.0, MUL, 1.0, ADD)
+    dma("Y", R("num", s_[0::16, 2048:4096]), R("khi"))
+    dma("S", R("num", s_[1::16, 2048:4096]), R("klo"))
+    dma("Y", R("num", s_[0::16, 1024:2048]), R("uhi"))
+    dma("S", R("num", s_[1::16, 1024:2048]), R("ulo"))
+    dma("Y", R("num", s_[4::16, 1024:2048]), R("usg"))
+    for k, n in enumerate(("n1", "n2", "n3", "n4")):
+        ts(R(n, s_[P96, :]), R("i16", s_[P96, :]), -1.0 - k, MUL)
+    tc(R("ib"), R("i16"))
+    tc(R("i32"), R("i16"))
+    ts(R("nb"), R("i16"), -1.0, MUL)
+    ms(R("g8i"), 1.0)
+    sel(R("g8i"), R("g8i"), [[1, 128]], GE, 0.0, 0, -16)
+    sel(R("g8i"), R("g8i"), [[-1, 128]], GE, 0.0, 15, 16)
+    for i, bk in enumerate(("A1", "B1", "K1", "K0")):
+        mm(R(bk), R("g8i", s_[0:8, :]), R("km8", s_[0:8, 512 * i:512 * i + 512]), True, True)
+        tt(R("sm", s_[:, 512 * i:512 * i + 512]), R(bk), R("st", s_[:, 512 * i:512 * i + 512]), MUL)
+    tc(R("k2h"), R("k2i"))
+    tc(R("u2h", s_[0:64]), R("u2i", s_[0:64, :, 0:32:2]))
+    ts(R("u2b", s_[0:64]), R("u2h", s_[0:64]), 0.5, MUL, 1023.75, ADD)
+    mm(R("B0", s_[:, 0, 0]), R("k2h"), R("i16"), True, True)
+    mm(R("B0", s_[:, 0, 1, 0:4]), R("u2h", s_[0:64]), R("i16", s_[0:64, 0:64]), True, True)
+    mm(R("B0", s_[:, 0, 1, 4:8]), R("u2b", s_[0:64]), R("i16", s_[0:64, 0:64]), True, True)
+    tc(R("lkl"), R("B0", s_[:, 0, 0]))
+    ts(R("lkr"), R("B0", s_[:, 0, 0]), 1.0, ADD)
+    tc(R("lup"), R("B0", s_[:, 0, 1, 0:4]))
+    tc(R("lup2"), R("B0", s_[:, 0, 1, 4:8]))
+    inherit(0, 0)
+    expand(0)
+    inherit(0, 1)
+    act(R("tmpn"), IND(R("num", s_[:, 2048:4096]), R("lkl")))
+    act(R("tmpm"), IND(R("num", s_[:, 2048:4096]), R("lkr")))
+    act(R("tmpu"), IND(R("num", s_[:, 0:2048]), R("lup2")))
+    for i in (0, 1):
+        dma("Y", R("num", s_[2 + i::16, 2048:4096]), R("tmpn", s_[i::16, :]))
+        dma("Y", R("num", s_[4 + i::16, 2048:4096]), R("tmpm", s_[i::16, :]))
+        dma("Y", R("num", s_[2 + i::16, 1024:2048]), R("tmpu", s_[i::16, :]))
+    tc(R("g8"), R("ones4", s_[:, 0, :]))
+    for k, n in enumerate(("gl", "gkl", "gkr")):
+        ts(R(n), R("g8"), 0.25, MUL, R("clm", s_[:, k:k + 1]), MUL)
+    for n in ("pk1", "pk0", "pkz", "cb", "cz", "ck2"):
+        ms(R(n), 0.0)
+    for t in (0, 1):
+        tc(R("pkk", s_[:, :, t]), R("g8"))
+    for (n, hf, r, pos, neg) in (("pk1", 0, 0, "gl", None), ("pk1", 0, 1, "gkl", "gl"), ("pk1", 0, 2, "gl", None), ("pk1", 0, 3, "gkr", "gl"),
+                                 ("pk1", 1, 0, "gkr", "gkl"), ("pk1", 1, 1, "gkl", None), ("pk1", 1, 2, None, "gkl"),
+                                 ("pk0", 1, 1, None, "gl"), ("pk0", 1, 2, "gkl", None), ("pk0", 1, 3, "gl", None), ("pkz", 0, 0, "gkl", None)):
+        o = R(n, s_[:, hf, :, r])
+        if neg is None:
+            tc(o, R(pos))
+        elif pos is None:
+            ts(o, R(neg), -1.0, MUL)
+        else:
+            tt(o, R(pos), R(neg), SUB)
+    tt(R("pkz", s_[:, 0, :, 1]), R("gl"), R("gkr"), ADD)
+    for (hf, r, c) in ((0, 2, 1.0), (0, 3, -1.0), (1, 1, 1.0), (1, 2, -1.0), (1, 3, -1.0)):
+        ms(R("cb", s_[:, hf, :, :, r, :]), c)
+    ms(R("cz", s_[:, 0, :, :, 0, :]), -1.0)
+    ms(R("ck2", s_[:, 0]), 3.0)
+    ms(R("ck2", s_[:, 1, :, :, 0, :]), 3.0)
+    ms(R("ck2", s_[:, 1, :, :, 2, :]), 6.0)
+    for x in "01":
+        ms(R("pa" + x, s_[:, :, :, :, 3]), 0.0)
+        ms(R("pb" + x, s_[:, :, :, :, 0]), 0.0)
+    for h in range(N):
+        if h:
+            inherit(h, 0)
+            inherit(h, 1)
+        gather1(h, 0)
+        gather1(h, 1)
+        if h:
+            msum(h - 1)
+        else:
+            act(R("w1", s_[:, 2048:4096]), IND(R("sm", s_[:, 0:2048]), R("lkl")))
+            act(R("w1", s_[:, 1024:2048]), IND(R("sm", s_[:, 0:2048]), R("lup")))
+            act(R("w2", s_[:, 2048:4096]), IND(R("sm", s_[:, 0:2048]), R("lkr")))
+            act(R("w2", s_[:, 1024:2048]), IND(R("w1", s_[:, 0:2048]), R("lup2")))
+        logic1a(h, 0)
+        logic1a(h, 1)
+        V = {}
+        for H in (0, 1):
+            V[H] = logic1b(h, H)
+            gather2(h, H, *V[H])
+        if h == 0:
+            dist(1)
+        if h + 1 < N:
+            expand(h + 1)
+        logic2(h, 0, *V[0])
+        logic2(h, 1, *V[1])
+        if h + 2 < N:
+            dist(h + 2)
+    dma("Y", ("yc", s_[:, :]), R("fw"))
+    tt(R("ef0"), R("ef0"), R("el1"), ADD)
+    tt(R("ef0"), R("ef0"), R("el2"), ADD)
+    msum(3, True)
+    for H in (0, 1):
+        c = s_[:, 192 * H:192 * H + 192]
+        tt(R("yes", c), R("ef0", c), R("el3" + "ab"[H]), ADD)
+        tt(R("yes", c), R("yes", c), R("av0", c), MUL)
+        dma("Y", ("ye", c), R("yes", c))
+    for i in schedule():
+        issue(prog[i])
+    for s, c in sorted(total.items()):
+        if known["G"].get(s, 0) < c:
+            g.wait_ge(T.sem[s], c)

@@ -1,13 +1,86 @@
 import numpy as np
-from concourse.mybir import dt, AluOpType, ActivationFunctionType
+from concourse.bass import DstId, RemoteDMATransfer
+from concourse.mybir import AluOpType, ActivationFunctionType
 ADD, SUB, MUL, MAX, MIN = AluOpType.add, AluOpType.subtract, AluOpType.mult, AluOpType.max, AluOpType.min
-EQ, GT, LT, GE, AND = AluOpType.is_equal, AluOpType.is_gt, AluOpType.is_lt, AluOpType.is_ge, AluOpType.bitwise_and
-SHR = AluOpType.arith_shift_right
+EQ, NE, GT, LT, GE, AND = AluOpType.is_equal, AluOpType.not_equal, AluOpType.is_gt, AluOpType.is_lt, AluOpType.is_ge, AluOpType.bitwise_and
 ACT = ActivationFunctionType
 F32, F16, BF, I32, U16 = "float32", "float16", "bfloat16", "int32", "uint16"
 N = 4
-D5 = [128, 2, 8, 4, 4]
-U4 = [128, 2, 8, 4]
+BIG = float(2 ** 22)
+AK, A0, B0, V, U, P, U2, C, D, L, Q, F, BA, BB, BC = 0, 1, 2, 3, 4, 5, 6, 8, 9, 10, 11, 12, 13, 14, 15
+
+
+def lin(*terms):
+    c = np.zeros(16)
+    for k, x in terms:
+        c += k * x
+    return c
+
+
+def fld(f):
+    return np.eye(16)[f]
+
+
+ONE, FCD, FS = fld(U) / 128, fld(F) / 128, (fld(V) - fld(F)) / 128
+nA, nB, nC, nD, nP, nQ, nL = fld(AK) + fld(A0), fld(AK) + fld(B0), fld(C), fld(D), fld(P), fld(Q), fld(L)
+bA, bB, bC = fld(BA), fld(BB), fld(BC)
+bD = 6 * ONE - bA - bB - bC
+Z = np.zeros(16)
+COLS, OFF = {"a": [], "b": [], "c": []}, {}
+
+
+def mat(name, cols, buf="b"):
+    OFF[name] = (buf, len(COLS[buf]))
+    if buf == "b":
+        COLS[buf].extend(cols)
+    else:
+        COLS[buf].append([Z] * (16 - len(cols)) + cols)
+
+
+for _q in range(4):
+    mat("z%d" % _q, [8192.0 * (np.arange(16) // 4 == _q)], "a")
+PAIRS = ((0, 1), (1, 2), (2, 3), (0, 2), (1, 3), (0, 3))
+mat("sel", [fld(f) * (f in (AK, P)) for f in range(16)], "c")
+mat("kb", [bA - bD, bC - 4 * FCD - bD, bB - bD + BIG * (fld(U2) / 128 - FS), bB - bD, bA + bB - 2 * bD + 4 * FCD, bC - bD, 3.5 * ONE - bD + BIG * FS, 3.5 * ONE - bD])
+mat("pr", [bC - bD - 8 * (ONE - FCD), BIG * (FS - ONE), bA - bD - 8 * FCD, bB - bD - 8 * FCD, bA - bB, bA - bC - 4 * ONE + 8 * FCD, nD, nP])
+mat("d0", [nL - nP, nL + ONE - nD, nQ - nC, nP - nQ, -2048 * ONE - nL, 2 * bD - bA - bB - 4 * FCD, Z, nD - nP])
+mat("d1", [nC - nD, FCD - FS, bD - bA, bA - bB, bB - bC, bC - bD, nC - nP, bA + bB - bD - bC + 8 * FCD])
+mat("mix", [nA, nL, nP, nB, nL + ONE, nC, nQ, nD], "c")
+mat("mg", [fld(A0), fld(B0), nC, nD], "c")
+mat("ml", [fld(AK), fld(AK), Z, Z], "c")
+mat("mr", [nA, nB, nC, nD], "c")
+mat("my", [nA + 2048 * bA, nB + 2048 * bB, nC + 2048 * bC, nD + 2048 * bD], "c")
+mat("st", [(np.arange(16) // 4 == j // 4) * (j % 4 == 3) * 1.0 for j in range(16)], "c")
+NM = {b: len(COLS[b]) for b in "ac"}
+for _b_ in "ac":
+    COLS[_b_] = [m[j] for j in range(16) for m in COLS[_b_]]
+TAB = {b: np.stack(COLS[b], axis=1) for b in COLS}
+
+
+def paints(buf):
+    out, KC = [], len(COLS[buf])
+    for a in range(4):
+        t = TAB[buf][4 * a:4 * a + 4].copy()
+        while t.any():
+            b, c = [int(x[0]) for x in np.nonzero(t)]
+            x, best = t[b, c], None
+            for rs in (1, 2, 3):
+                rows = [b]
+                while rows[-1] + rs < 4 and t[rows[-1] + rs, c] == x:
+                    rows.append(rows[-1] + rs)
+                for nr in range(1, len(rows) + 1):
+                    ok = np.all(t[rows[:nr]] == x, axis=0)
+                    for cs in range(1, KC):
+                        n = 1
+                        while c + n * cs < KC and ok[c + n * cs]:
+                            n += 1
+                        if best is None or n * nr > best[0]:
+                            best = (n * nr, slice(b, rows[nr - 1] + 1, rs), slice(c, c + (n - 1) * cs + 1, cs))
+            out.append((a, best[1], best[2], float(x)))
+            t[best[1], best[2]] = 0
+    return out
+
+
 SCRATCH = {}
 ALIAS = {}
 
@@ -24,81 +97,61 @@ def _b(names, shape, dtype, where="sbuf"):
         SCRATCH[n] = (where, shape, dtype)
 
 
-_b("A0 B0 K0 A1 B1 K1", [128, 2, 2, 8, 4, 4], F32, "psum")
-_b("fb", [128, 512], F32, "psum")
-_b("mb", [128, 4, 2, 8, 2, 4], F32, "psum")
+_b("Oa Ob K D0 D1 PR", [128, 16, 4, 8], F32, "psum")
+_b("X1", [128, 256, 2], F32, "psum")
+_b("X2", [128, 32, 16], F32, "psum")
 _b("av0 av1 av2 av3 ak0", [128, 384], BF)
-_b("lku0 lku1 lku2 lku3", [128, 96], U16)
-_b("lki", [128, 96], I32)
-_b("aexp0 aexp1", [128, 4, 1536], BF)
-_b("aexq0 aexq1", [128, 2, 1536], BF)
-_b("st mt sm", [128, 2048], BF)
-_b("w1 w2 num", [128, 4096], BF)
-_m("tmp2", "tmpn tmpm", [128, 2048], BF)
-_b("tmpu", [128, 1024], BF)
-_b("kidi upi", [128, 128], I32)
-_b("khi klo kmk", [128, 128], BF)
-_b("uhi ulo usg", [128, 64], BF)
-_b("upe ubit", [128, 64], I32)
-_b("km8", [128, 2048], BF)
-_b("k2i", [128, 8, 16], I32)
-_b("u2i", [128, 8, 32], I32)
-_b("k2h", [128, 128], F16)
-_b("u2h u2b", [128, 8, 16], F16)
-_m("lk2", "lkl lkr", [128, 128], U16)
-_m("lu2", "lup lup2", [128, 64], U16)
+_b("own0 own1 own2 own3 ownx lku xl", [128, 96], U16)
+_b("lki oi oj", [128, 96], I32)
+_b("koff lkf yd2", [128, 96], F32)
+_b("kw", [128, 32, 12], F32)
+_b("yd", [128, 16, 12], F32)
+_b("dif absd", [128, 1536], F16)
+_b("bd0 bd1", [128, 8, 384], BF)
+_b("st mt sm km8", [128, 2048], BF)
+_b("num", [128, 2048], I32)
+_b("kidi", [128, 128], I32)
+_b("kmk g8i ib", [128, 128], BF)
+for _h in COLS:
+    _b("row" + _h, [128, 4, len(COLS[_h])], F16)
+    _b("pk" + _h, [128, 8, len(COLS[_h])] if _h == "b" else [128, 144, NM[_h]], F16)
+_b("xs", [128, 8, 4, 4], F16)
+_b("md", [128, 4, 8, 4, 4], F16)
+_m("idt", "p1 n1 p2 n2 p4 n4 p128 n128 p2048 n2048", [128, 32, 4], F16)
+_b("keep", [128, 8, 16], F16)
+_b("w", [128, 8, 8], F32)
 _b("cuti", [128, 384], I32)
-_b("fw", [128, 384], F32)
-_b("fu", [128, 384], U16)
-_b("mg", [128, 6144], BF)
-_m("ef", "ef0 ef1 ef2 yes", [128, 384], F32)
+_b("cf hf", [128, 384], F16)
+_b("ct", [128, 16, 4, 4], F16)
+_b("on", [128, 16, 4], F16)
+_b("ns fr", [128, 8, 4, 4, 4], F16)
+_b("fl", [128, 8, 4, 4, 2], F16)
+_b("il", [128, 288], U16)
+_b("rt0 rt", [128, 4, 4, 8, 16], F16)
+_b("rec", [128, 1536], F32)
+_b("r16", [128, 4, 384], F16)
+_b("lk0 lk1", [128, 1536], F16)
+_b("mg", [128, 6144], F16)
+_b("mu", [128, 384], U16)
+_m("ef", "ef0 ef1 ef2 yes ycf", [128, 384], F32)
 _b("el1 el2", [128, 384], F32)
-_b("el3a el3b", [128, 192], F32)
-_m("eh", "ef3a ef3b", [128, 192], F32)
-_m("idt", "i16 n1 n2 n3 n4", [128, 128], F16)
-_b("ib nb", [128, 128], BF)
-_b("i32", [128, 128], F32)
-_b("ones4", [128, 2, 8], F32)
-_b("g8", [128, 8], F32)
-_b("g8i", [128, 128], BF)
-_b("pkk", [128, 8, 2], F32)
-_b("pick", [128, 4, 8, 4], F32)
-_b("qb", [128, 32], BF)
-_b("gx", [128, 32], F32)
-_b("r2", [128, 48], F16)
-_b("pi", [128, 5], I32)
-_b("pc", [128, 5], F32)
-_b("io16 clm clx", [128, 16], F32)
-_b("koff", [128, 96], F32)
-_m("gms", "gl gkl gkr", [128, 8], BF)
-_m("pks", "pk1 pk0 pkz", [128, 2, 8, 4], BF)
-_b("bias1", [128, 64, 4], BF)
-_m("cks", "cb cz ck2", [128, 2, 2, 8, 4, 4], BF)
-_b("lkf", [128, 96], F32)
-_b("lkx", [128, 4, 24, 16], F32)
-_b("absd dif", [128, 1536], BF)
-_b("dcp", [128, 256], F32)
-_b("dm2", [128, 2, 128], F32)
-_b("owi owk", [128, 16, 8], I32)
-_b("owp", [128, 16, 2, 8], F16)
-_b("owl0 owl1", [128, 96], U16)
+_b("el3a el3b ef3a ef3b", [128, 192], F32)
+_m("yr", "y0 y1 y2 y3 z1 z2", [128, 384], F16)
+_b("pi", [128, 2], I32)
+_b("pc", [128, 1], F32)
 for _h in "01":
-    _b("G" + _h, [128, 768], F32)
-    _m("qd" + _h, " ".join(n + _h for n in "cs h16 e v v1 v2 fm px pa pb pd".split()), D5, F16)
-    _b("kf" + _h, D5, F32)
-    _b("l1" + _h, [128, 2, 96], U16)
-    _b("xl" + _h, [128, 96], U16)
-    _b("sq%s pm%s" % (_h, _h), [128, 2, 2, 8, 4, 4], BF)
-    _b("ph" + _h, [128, 2, 2, 8, 4, 4], F16)
-    _b("prA%s prB%s" % (_h, _h), [128, 1536], F32)
-    _b("kc%s m2%s" % (_h, _h), [128, 2, 8, 4, 2], F32)
-    _b("mx" + _h, U4, F32)
-    _b("pr" + _h, [128, 8, 2, 2, 4, 4], F16)
-    _b("ng" + _h, [128, 1536], BF)
-    _b("uw" + _h, [128, 24, 2, 8, 4], F16)
-    _b("uf" + _h, [128, 4, 2, 8, 4], F32)
-SEMAPHORES = ["cV", "cS", "cP", "cG", "lsem"] + ["ar%d" % h for h in (1, 2, 3)] + ["er%d" % h for h in (1, 2, 3, 4)] + ["d%d" % i for i in range(60)]
+    _b("ga%s gb%s" % (_h, _h), [128, 768], F16)
+    _b("sl" + _h, [128, 384], U16)
+    _b("sg" + _h, [128, 6144], BF)
+    _b("os" + _h, [128, 24, 4, 8], F32)
+    _b("y" + _h + "f", [128, 16, 4, 8], F32)
+    _b("yp" + _h, [128, 16, 4, 3], F32)
+    _b("e" + _h, [128, 16, 4, 8], F16)
+    _b("u" + _h, [128, 32, 16, 4], F16)
+SEMAPHORES = ["cV", "cS", "cP", "cG", "lsem", "ar", "ao"] + ["er%d" % h for h in (1, 2, 3, 4)] + ["d%d" % i for i in range(40)]
 WHOLE = np.s_[:]
+CYC, GATH, PEC, WAKE, OV = 0.95, 1.35, 0.48, 120, 25
+MEMO = {}
 
 
 def rank_program(g, core, T, topo):
@@ -110,7 +163,8 @@ def rank_program(g, core, T, topo):
     total = {}
     known = {e: {} for e in ENG}
     ops = []
-    wr, rd, cache, bank = {}, {}, {}, {}
+    wr, rd, bank = {}, {}, {}
+    cache = MEMO.setdefault("cols", {})
     ndma = [0]
     prog = []
 
@@ -132,18 +186,17 @@ def rank_program(g, core, T, topo):
         return SCRATCH[r[0]][0] == "psum"
 
     def size(n):
-        return 16 * 4096 if n == "num" else int(np.prod(SCRATCH[n][1][1:]))
+        return int(np.prod(SCRATCH[n][1][1:])) * (4 if n[:3] == "row" else 1)
 
     def cols(r):
         key = (r[0], repr(r[1]))
         if key not in cache:
             ix = r[1] if isinstance(r[1], tuple) else (r[1],)
-            if r[0] == "num":
-                rows = np.unique(np.arange(128)[ix[0]] % 16)
-                c = np.arange(16 * 4096).reshape(16, 4096)[rows][:, ix[1] if len(ix) > 1 else WHOLE]
-            else:
-                c = np.arange(size(r[0])).reshape(SCRATCH[r[0]][1][1:])[ix[1:]]
-            cache[key] = np.unique(c.reshape(-1))
+            shape = SCRATCH[r[0]][1][1:]
+            c = np.arange(int(np.prod(shape))).reshape(shape)[ix[1:]].reshape(-1)
+            if r[0][:3] == "row":
+                c = np.concatenate([c + size(r[0]) // 4 * b for b in np.unique(np.arange(128)[ix[0]] // 32)])
+            cache[key] = np.unique(c)
         return cache[key]
 
     def parts(rs):
@@ -155,16 +208,14 @@ def rank_program(g, core, T, topo):
                 out.append(r)
         return out
 
-    def hazards(W, L, outs, ins, skip):
+    def hazards(W, Lr, outs, ins, skip):
         need = set()
         for r in list(ins) + list(outs):
-            if not psum(r) and r[0] in W:
+            if r[0] in W:
                 need.update(np.unique(W[r[0]][cols(r)]).tolist())
         for r in outs:
-            if psum(r):
-                continue
             c, keep = cols(r), []
-            for (o, m) in L.get(r[0], []):
+            for (o, m) in Lr.get(r[0], []):
                 if m[c].any():
                     if not skip(o):
                         need.add(o)
@@ -172,24 +223,27 @@ def rank_program(g, core, T, topo):
                     if not m.any():
                         continue
                 keep.append((o, m))
-            L[r[0]] = keep
+            Lr[r[0]] = keep
         need.discard(-1)
         return need
 
-    def note(W, L, o, outs, ins):
+    def note(W, Lr, o, outs, ins):
         for r in outs:
-            if not psum(r):
-                if r[0] not in W:
-                    W[r[0]] = np.full(size(r[0]), -1)
-                W[r[0]][cols(r)] = o
+            if r[0] not in W:
+                W[r[0]] = np.full(size(r[0]), -1)
+            W[r[0]][cols(r)] = o
+        by = {}
         for r in ins:
-            if not psum(r):
-                m = np.zeros(size(r[0]), bool)
-                m[cols(r)] = True
-                L.setdefault(r[0], []).append((o, m))
+            if r[0] not in by:
+                by[r[0]] = np.zeros(size(r[0]), bool)
+            by[r[0]][cols(r)] = True
+        for n, m in by.items():
+            Lr.setdefault(n, []).append((o, m))
 
     def waits(e, outs, ins, queued):
-        need = hazards(wr, rd, outs, ins, lambda o: queued and ops[o][0] == e)
+        need = hazards(wr, rd, outs, ins, lambda o: False)
+        if e == "P":
+            need = set(o for o in need if ops[o][0] != "P")
         for r in outs + ins:
             if psum(r):
                 need.update(o for e2, o in bank.get(r[0], {}).items() if e2 != e)
@@ -217,566 +271,508 @@ def rank_program(g, core, T, topo):
             if psum(r):
                 bank.setdefault(r[0], {})[e] = len(ops) - 1
 
-    def issue(o):
-        e, outs, ins, a = o["e"], o["o"], o["i"], o["a"]
+    def issue(o, e):
+        outs, ins, a = o["o"], o["i"], o["a"]
         if o["k"] == "arr":
             issued(None, a[0], a[1], {}, outs, [])
             return
         if o["k"] == "send":
             waits("G", [], ins, False)
-            src, dst, dstname, s = a
-            rid, pid = topo.addr(dst, core)
-            g.remote_dma(T[dstname][:], ap(src), T.sem[s], T.sem.lsem, pid, rid, topo.mask(core, dst))
-            total["lsem"] = total.get("lsem", 0) + len(topo.engines(core, dst))
+            src, dsts, s = a
+            m = -1
+            for c, _ in dsts:
+                m &= topo.mask(core, c)
+            if len(dsts) == 1:
+                rid, pid = topo.addr(dsts[0][0], core)
+                g.remote_dma(T[dsts[0][1]][:], ap(src), T.sem[s], T.sem.lsem, pid, rid, m)
+            else:
+                ids = [DstId(rid=topo.addr(c, core)[0], pnc=topo.addr(c, core)[1]) for c, _ in dsts]
+                g.remote_dma_fused([RemoteDMATransfer(dst_ids=ids, dma_engine_mask=m, remote_sem=T.sem[s], srcs=[ap(src)], dsts=[T[n][:] for _, n in dsts])], local_sem=T.sem.lsem)
+            total["lsem"] = total.get("lsem", 0) + bin(m).count("1")
             return
         waits(e, outs, ins, o["k"] == "op")
         if o["k"] == "dma":
             s = "d%d" % ndma[0]
             ndma[0] += 1
-            ENG[e].dma_start(ap(a[0]), ap(a[1])).then_inc(T.sem[s], 16)
-            issued(None, s, 16, dict(known[e]), outs, ins)
+            for x, y in a:
+                ENG[e].dma_start(ap(x), ap(y)).then_inc(T.sem[s], 16)
+            issued(None, s, 16 * len(a), dict(known[e]), outs, ins)
         else:
             s = "c" + e
-            cnt[s] += 1
-            a().then_inc(T.sem[s], 1)
+            for fn in a[e]:
+                cnt[s] += 1
+                fn().then_inc(T.sem[s], 1)
             issued(e, s, cnt[s], dict(known[e]), outs, ins)
 
-    def op(e, outs, ins, fn):
-        o, i = parts(outs), parts(ins)
-        ind = any(r[0] == "@" for r in list(outs) + list(ins))
-        if ind:
-            d = 60 + 1.7 * len(cols(outs[0]))
-        elif e == "P":
-            d = 0.52 * max(min(64, len(cols(ins[0]))), len(cols(ins[1]))) * (4 if SCRATCH[ins[0][0]][2] == F32 else 1)
-        else:
-            n = max(len(cols(r)) // (16 if r[0] == "num" else 1) for r in o + i)
-            d = 200 + 2 * n if e == "G" else max(64, n * (2 if e == "V" and len(ins) == 2 and not any(psum(r) for r in i) else 1))
-        prog.append({"k": "op", "e": e, "o": o, "i": i, "a": fn, "d": d, "lat": 0})
+    def two(r):
+        return SCRATCH[r[0]][2] in (F16, BF, U16)
 
-    def dma(e, out, in_):
-        prog.append({"k": "dma", "e": e, "o": parts([out]), "i": parts([in_]), "a": (out, in_), "d": 60, "lat": 2200})
+    def op(outs, ins, fns, both=False, lab=0):
+        o, i = parts(outs), parts(ins)
+        n = len(cols(outs[0]))
+        d = {}
+        for e in fns:
+            if any(r[0] == "@" for r in ins):
+                d[e] = 60 + CYC * GATH * n
+            elif e == "G":
+                d[e] = 190 + 2 * CYC * n
+            elif e == "S":
+                d[e] = CYC * max(64, n)
+            else:
+                d[e] = CYC * max(64, n * (2 if both else 0.5 if all(two(r) for r in o + i[:1]) else 1))
+        prog.append({"k": "op", "o": o, "i": i, "a": {e: [f] for e, f in fns.items()}, "d": d, "lat": 0, "lab": lab})
+
+    def dma(e, pairs, after=()):
+        prog.append({"k": "dma", "o": parts([x for x, _ in pairs]), "i": parts([y for _, y in pairs]) + list(after), "a": pairs, "d": {e: 60 * len(pairs)}, "lat": 2200, "lab": 0})
 
     def arrival(names, s, c, lat):
-        prog.append({"k": "arr", "e": "X", "o": [R(n) for n in names.split()], "i": [], "a": (s, c), "d": 0, "lat": lat})
+        prog.append({"k": "arr", "o": [R(n) for n in names], "i": [], "a": (s, c), "d": {"X": 0}, "lat": lat, "lab": 0})
 
-    def send(src, dst, dstname, s):
-        prog.append({"k": "send", "e": "G", "o": [R(dstname)], "i": [R(src)], "a": (R(src), dst, dstname, s), "d": 1200, "lat": 0})
+    def send(src, dsts, s, lat):
+        prog.append({"k": "send", "o": [R(n) for _, n in dsts], "i": [R(src)], "a": (R(src), dsts, s), "d": {"G": 1200}, "lat": 0, "lab": 0})
+        arrival([n for _, n in dsts], s, sum(len(topo.engines(c, core)) for c, _ in dsts), lat)
 
     def schedule():
         n = len(prog)
-        W, L, hist, pre = {}, {}, {}, []
+        W, Lr, hist, pre = {}, {}, {}, []
         for i, o in enumerate(prog):
-            S = hazards(W, L, o["o"], o["i"], lambda j: False)
-            note(W, L, i, o["o"], o["i"])
+            S = hazards(W, Lr, o["o"], o["i"], lambda j: False)
+            note(W, Lr, i, o["o"], o["i"])
+            es = "".join(o["d"])
             for b in set(r[0] for r in o["o"] + o["i"] if psum(r)):
                 hb = hist.setdefault(b, {"P": [], "V": [], "S": []})
-                if o["e"] == "P":
+                if es == "P":
                     S.update(hb["P"][-1:] + hb["V"] + hb["S"])
                     hb["V"], hb["S"] = [], []
+                    hb["P"].append(i)
                 else:
-                    S.update(hb["P"][-1:] + hb["S" if o["e"] == "V" else "V"][-1:])
-                hb[o["e"]].append(i)
+                    S.update(hb["P"][-1:] + hb["S"] + (hb["V"] if es != "V" else []))
+                    if es == "V":
+                        hb["V"].append(i)
+                    else:
+                        hb["V"], hb["S"] = [], [i]
             S.discard(i)
             pre.append(S)
         suc = [[] for _ in range(n)]
         for i, S in enumerate(pre):
             for j in S:
                 suc[j].append(i)
-        WAKE, OV = 130, 35
-        gap = lambda i, j: 0 if prog[i]["e"] == prog[j]["e"] == "P" else WAKE
+        pe = ["P" in o["d"] for o in prog]
+        gap = lambda i, j: 0 if pe[i] and pe[j] else WAKE
         prio = [0.0] * n
         for i in range(n - 1, -1, -1):
-            prio[i] = max([prio[j] + gap(i, j) for j in suc[i]] + [0.0]) + prog[i]["d"] + prog[i]["lat"]
+            prio[i] = max([prio[j] + gap(i, j) for j in suc[i]] + [0.0]) + min(prog[i]["d"].values()) + prog[i]["lat"]
         left, ready = [len(S) for S in pre], [0.0] * n
-        avail, t = {e: [] for e in "XYGPSV"}, {e: 0.0 for e in "XYGPSV"}
+        ES = "XYGPSV"
+        avail, t = {e: set() for e in ES}, {e: 0.0 for e in ES}
+
+        def free(i):
+            for e in prog[i]["d"]:
+                avail[e].add(i)
         for i in range(n):
             if not left[i]:
-                avail[prog[i]["e"]].append(i)
+                free(i)
         order = []
         while len(order) < n:
             pick = None
-            for e in "XYGPSV":
+            for e in ES:
                 if avail[e]:
                     now = max(t[e], min(ready[i] for i in avail[e]))
                     if pick is None or now < pick[0]:
-                        pick = (now, max((i for i in avail[e] if ready[i] <= now), key=lambda i: (prio[i], -i)), e)
+                        only = lambda i: 300 if e == "V" and len(prog[i]["d"]) == 1 else 0
+                        pick = (now, max((i for i in avail[e] if ready[i] <= now), key=lambda i: (prio[i] + only(i), -i)), e)
             now, c, e = pick
-            avail[e].remove(c)
-            end = now + prog[c]["d"] + OV
+            for e2 in prog[c]["d"]:
+                avail[e2].remove(c)
+            end = now + prog[c]["d"][e] + (0 if e == "P" else OV)
             if e != "X":
                 t[e] = end
-            order.append(c)
+            order.append((c, e))
             for j in suc[c]:
                 ready[j] = max(ready[j], end + prog[c]["lat"] + gap(c, j))
                 left[j] -= 1
                 if not left[j]:
-                    avail[prog[j]["e"]].append(j)
+                    free(j)
         return order
 
     def tt(out, a, b, o):
-        op("V", [out], [a, b], lambda: g.vector.tensor_tensor(ap(out), ap(a), ap(b), o))
-
-    def tc(out, a):
-        op("V", [out], [a], lambda: g.vector.tensor_copy(ap(out), ap(a)))
+        op([out], [a, b], {"V": lambda: g.vector.tensor_tensor(ap(out), ap(a), ap(b), o)}, a[0] != "@" and not psum(a) and not psum(b))
 
     def ts(out, a, s1, o1, s2=None, o2=None):
         v = lambda x: ap(x) if isinstance(x, tuple) else x
         ins = [a] + [x for x in (s1, s2) if isinstance(x, tuple)]
         if o2 is None:
-            op("V", [out], ins, lambda: g.vector.tensor_scalar(ap(out), ap(a), v(s1), None, o1))
+            op([out], ins, {"V": lambda: g.vector.tensor_scalar(ap(out), ap(a), v(s1), None, o1)})
         else:
-            op("V", [out], ins, lambda: g.vector.tensor_scalar(ap(out), ap(a), v(s1), v(s2), o1, o2))
+            op([out], ins, {"V": lambda: g.vector.tensor_scalar(ap(out), ap(a), v(s1), v(s2), o1, o2)})
 
     def ms(out, c):
-        op("V", [out], [], lambda: g.vector.memset(ap(out), c))
+        op([out], [], {"V": lambda: g.vector.memset(ap(out), c)})
 
-    def act(out, a, f=ACT.Copy, bias=0.0, scale=1.0):
-        col = isinstance(scale, tuple)
-        op("S", [out], [a] + ([scale] if col else []), lambda: g.scalar.activation(ap(out), ap(a), f, bias=bias, scale=ap(scale) if col else scale))
+    def cp(out, a, es="VS"):
+        f = {"V": lambda: g.vector.tensor_copy(ap(out), ap(a)), "S": lambda: g.scalar.activation(ap(out), ap(a), ACT.Copy)}
+        op([out], [a], {e: f[e] for e in es})
 
-    def mm(out, l, r, start, stop):
-        op("P", [out], [l, r], lambda: g.tensor.matmul(ap(out), ap(l), ap(r), start, stop))
+    def aff(out, a, scale, bias, es="VS"):
+        f = {"V": lambda: g.vector.tensor_scalar(ap(out), ap(a), scale, bias, MUL, ADD),
+             "S": lambda: g.scalar.activation(ap(out), ap(a), ACT.Identity, bias=bias, scale=scale)}
+        op([out], [a], {e: f[e] for e in es})
 
-    def group(lst):
+    def relu(out, a, scale=1.0, bias=0.0, es="VS"):
+        f = {"V": lambda: g.vector.tensor_scalar(ap(out), ap(a), bias if scale == 1.0 else scale, 0.0, ADD if scale == 1.0 else MUL, MAX),
+             "S": lambda: g.scalar.activation(ap(out), ap(a), ACT.Relu, bias=bias, scale=scale)}
+        op([out], [a], {e: f[e] for e in es})
+
+    def pe(lst, group=True):
+        fns, d = [], 0.0
         for i, (o, l, r) in enumerate(lst):
-            mm(o, l, r, i == 0, i == len(lst) - 1)
+            fns.append(lambda o=o, l=l, r=r, i=i: g.tensor.matmul(ap(o), ap(l), ap(r), i == 0 or not group, i == len(lst) - 1 or not group))
+            d += PEC * max(min(64, len(cols(l))), len(cols(r))) * (4 if SCRATCH[l[0]][2] == F32 else 1)
+        prog.append({"k": "op", "o": [o for o, _, _ in lst], "i": [x for _, l, r in lst for x in (l, r)], "a": {"P": fns}, "d": {"P": d}, "lat": 0, "lab": 0})
+
+    def pe_open(lst, first, last):
+        fns, d = [], 0.0
+        for i, (o, l, r) in enumerate(lst):
+            fns.append(lambda o=o, l=l, r=r, i=i: g.tensor.matmul(ap(o), ap(l), ap(r), first and i == 0, last and i == len(lst) - 1))
+            d += PEC * max(min(64, len(cols(l))), len(cols(r))) * (4 if SCRATCH[l[0]][2] == F32 else 1)
+        prog.append({"k": "op", "o": [o for o, _, _ in lst], "i": [x for _, l, r in lst for x in (l, r)], "a": {"P": fns}, "d": {"P": d}, "lat": 0, "lab": 0})
 
     def sel(out, in_, pattern, cmp, fill, base, cm):
-        op("G", [out], [in_], lambda: g.affine_select(ap(out), ap(in_), pattern, cmp, fill, base, cm))
+        op([out], [in_], {"G": lambda: g.affine_select(ap(out), ap(in_), pattern, cmp, fill, base, cm)})
 
     def iota(out, pattern, base, cm):
         if SCRATCH[out[0]][2] == I32:
-            op("G", [out], [], lambda: g.iota(ap(out), pattern, base, cm))
+            op([out], [], {"G": lambda: g.iota(ap(out), pattern, base, cm)})
         else:
-            op("G", [out], [], lambda: g.iota(ap(out), pattern, base, cm, allow_small_or_imprecise_dtypes=True))
+            op([out], [], {"G": lambda: g.iota(ap(out), pattern, base, cm, allow_small_or_imprecise_dtypes=True)})
 
     s_ = np.s_
     P96 = slice(0, 96)
-    I96 = lambda n: R(n, s_[0:96, 0:96])
+    I = lambda n: R(n, s_[0:96, 0:24])
+    PK = lambda n, a, k: R("pk" + OFF[n][0], s_[:, :, OFF[n][1] + a:OFF[n][1] + a + k])
+    ST = lambda n, a: R("pk" + OFF[n][0], s_[:, a:a + 128, OFF[n][1]])
+    slot = lambda b, k: R(b, s_[P96, :, :, k])
     cores = list(T.cores)
     nxt = lambda h: cores[(rank + h) % N]
 
-    dma("Y", R("av0"), ("a", s_[:, :]))
-    dma("S", R("lki"), ("lk", s_[:, :]))
-    dma("Y", R("ak0"), ("a0", s_[:, :]))
-    dma("S", R("kidi"), ("kid", s_[:, :]))
-    dma("Y", R("cuti"), ("cut0", s_[:, :]))
-    dma("S", R("upi"), ("up", s_[:, :]))
-    dma("Y", R("st"), ("s", s_[:, :]))
-    ms(R("i16"), 1.0)
-    sel(R("i16"), R("i16"), [[-1, 128]], EQ, 0.0, 0, 1)
-    ms(R("qb"), 2048.0)
-    ms(R("gx"), 1.0)
-    sel(R("qb"), R("qb"), [[-16, 8], [-4, 4]], GE, 0.0, 0, 1)
-    sel(R("qb"), R("qb"), [[16, 8], [4, 4]], GE, 0.0, 3, -1)
-    iota(R("pi", s_[:, 0:1]), [[0, 1]], 0, 1)
-    sel(R("gx"), R("gx"), [[-16, 8], [0, 4]], GE, 0.0, 0, 1)
-    sel(R("gx"), R("gx"), [[16, 8], [0, 4]], GE, 0.0, 15, -1)
-    iota(R("koff"), [[512, 4], [0, 24]], 0, 0)
-    iota(R("io16"), [[1, 16]], 0, 0)
-    ms(R("r2"), 1.0)
-    sel(R("r2"), R("r2"), [[-2, 48]], GE, 0.0, 0, 1)
-    sel(R("r2"), R("r2"), [[2, 48]], GE, 0.0, 1, -1)
-    ms(R("pick"), 1.0)
-    sel(R("pick"), R("pick"), [[-4, 4], [-16, 8], [-1, 4]], EQ, 0.0, 0, 1)
-    ms(R("ones4"), 4.0)
-    sel(R("ones4"), R("ones4"), [[0, 2], [-16, 8]], GE, 0.0, 0, 1)
-    sel(R("ones4"), R("ones4"), [[0, 2], [16, 8]], GE, 0.0, 15, -1)
-    iota(R("bias1"), [[0, 64], [-1, 4]], 3, 0)
-    tc(R("lku0"), R("lki"))
-    for h in (1, 2, 3):
-        send("av0", nxt(h), "av%d" % h, "ar%d" % h)
-        send("lku0", nxt(h), "lku%d" % h, "ar%d" % h)
-        arrival("av%d lku%d" % (h, h), "ar%d" % h, 2 * len(topo.engines(nxt(-h), core)), 8000)
-    ts(R("pi", s_[:, 1:2]), R("pi", s_[:, 0:1]), 1, AND)
-    ts(R("pi", s_[:, 2:3]), R("pi", s_[:, 0:1]), 1, SHR, 7, AND)
-    ts(R("pi", s_[:, 3:4]), R("pi", s_[:, 0:1]), 2, SHR, 1, AND)
-    ts(R("pi", s_[:, 4:5]), R("pi", s_[:, 0:1]), 15, AND)
-    tc(R("pc", s_[:, 0:1]), R("pi", s_[:, 1:2]))
-    ts(R("pc", s_[:, 1:2]), R("pi", s_[:, 1:2]), -1.0, MUL, 1.0, ADD)
-    tc(R("pc", s_[:, 2:3]), R("pi", s_[:, 2:3]))
-    ts(R("pc", s_[:, 3:4]), R("pi", s_[:, 3:4]), 2048.0, MUL)
-    tc(R("pc", s_[:, 4:5]), R("pi", s_[:, 4:5]))
-    ts(R("clm"), R("io16"), R("pc", s_[:, 2:3]), EQ)
-    ts(R("clx"), R("io16"), R("pc", s_[:, 4:5]), EQ)
-
-    def dist(h):
-        av, lku, ow = "av%d" % h, "lku%d" % h, "owl%d" % (h % 2)
-        ak = "ak0" if h == 0 else "av%d" % (h - 1)
-        for k in range(4):
-            c = s_[:, 384 * k:384 * k + 384]
-            i = IND(R(ak, s_[:, 0:384]), R(lku, s_[:, 24 * k:24 * k + 24]))
-            if h == 0:
-                tt(R("dif", c), i, R(av), SUB)
-                act(R("absd", c), R("dif", c), ACT.Abs)
-            else:
-                act(R("dif", c), i)
-        for k in range(4 if h else 0):
-            c = s_[:, 384 * k:384 * k + 384]
-            group([(R("fb", s_[:, 0:384]), R("ib"), R("dif", c)), (R("fb", s_[:, 0:384]), R("nb"), R(av))])
-            act(R("absd", c), R("fb", s_[:, 0:384]), ACT.Abs)
-        ts(R("lkf"), R(lku), 1.0, MUL)
-        tt(R("lkf"), R("lkf"), R("koff"), ADD)
-        for cl in range(16):
-            act(R("lkx", s_[:, :, :, cl]), R("lkf"), ACT.Copy, 0.0, R("clx", s_[:, cl:cl + 1]))
-        for k in range(4):
-            for H in (0, 1):
-                for bl in (0, 1):
-                    o = R("mb", s_[0:96, k, H, :, bl, :])
-                    j = 2 * H + bl
-                    group([(o, R("absd", s_[:, 384 * k + 96 * j:384 * k + 96 * j + 96]), R("qb")),
-                           (o, R("lkx", s_[:, k, 6 * j:6 * j + 6, :]), R("gx"))])
-        act(R("dcp", s_[P96, :]), R("mb", s_[P96, 2:4, :, :, :, :]))
-        tt(R("dm2", s_[P96, :, :]), R("mb", s_[P96, 0:2, :, :, :, :]), R("dcp", s_[P96, :]), MIN)
-        tt(R("owi", s_[P96]), R("dm2", s_[P96, 0, :]), R("dm2", s_[P96, 1, :]), MIN)
-        ts(R("owk", s_[P96]), R("owi", s_[P96]), 511, AND)
-        for b in (0, 1):
-            ts(R("owp", s_[P96, :, b, :]), R("owk", s_[P96]), R("pc", s_[P96, 1 - b:2 - b]), MUL)
-        for H in (0, 1):
-            mm(R("mb", s_[:, 0, H, 0:6, :, :]), R("owp", s_[P96, 8 * H:8 * H + 8, :, :]), R("r2", s_[P96, :]), True, True)
-        tc(R(ow), R("mb", s_[:, 0, :, 0:6, :, :]))
-
-    def inherit(h, H):
-        x = str(H)
-        A, G = "A" + x, "G" + x
-        act(R(G), IND(R("fw", s_[:, 0:384]), R("owl%d" % (h % 2), s_[:, 48 * H:48 * H + 48])))
-        for bl in (0, 1):
-            for q in range(4):
-                mm(R(A, s_[P96, 0, bl, :, q, :]), R(G, s_[:, 4 * bl + q::8]), R("pick", s_[:, q, :, :]), True, True)
-        tc(R("cs" + x, s_[P96]), R(A, s_[P96, 0]))
-        for bl in (0, 1):
-            mm(R(A, s_[:, 1, bl, 0:6, :, :]), R("cs" + x, s_[P96, bl]), I96("i16"), True, True)
-        tc(R("l1" + x), R(A, s_[:, 1, :, 0:6, :, :]))
-
-    def gather1(h, H):
-        x = str(H)
-        A, B, K = "A" + x, "B" + x, "K" + x
-        ax, h16 = "aexp%d" % (h % 2), "h16" + x
-        for bl, pr in ((0, "prA" + x), (1, "prB" + x)):
-            tt(R(pr), IND(R("sm", s_[:, 0:2048]), R("l1" + x, s_[:, bl, :])), R(ax, s_[:, 2 * H + bl, :]), MUL)
-        ts(R(h16, s_[P96]), R("cs" + x, s_[P96]), 0.5, MUL, 1023.75, ADD)
-        ends = ((R(B, s_[P96, 0, :, :, :, 0:3]), R(A, s_[P96, 1, :, :, :, 0:3]), 3, 1), (R(B, s_[P96, 0, :, :, :, 3:4]), R(A, s_[P96, 1, :, :, :, 3:4]), 1, 3),
-                (R(B, s_[P96, 1, :, :, :, 0:2]), R(B, s_[P96, 1, :, :, :, 2:4]), 2, 2))
-        for (o, o2, n, dl) in ends:
-            group([(o, I96("i16"), R(h16, s_[P96, :, :, :, 0:n])), (o, I96("n1"), R(h16, s_[P96, :, :, :, dl:dl + n]))])
-        for (o, o2, n, dl) in ends:
-            mm(o2, I96("i16"), R(h16, s_[P96, :, :, :, 0:n]), True, True)
-        for i in (s_[P96, 0], s_[P96, 1, :, :, :, 0:2]):
-            act(R("sq" + x, i), R(B, i), ACT.Square)
-            act(R("pm" + x, i), R("sq" + x, i), ACT.Relu, 1.0, -1.0)
-        tt(R("ph" + x, s_[P96, 0]), R(A, s_[P96, 1]), R("pm" + x, s_[P96, 0]), MUL)
-        tt(R("ph" + x, s_[P96, 1, :, :, :, 0:2]), R(B, s_[P96, 1, :, :, :, 2:4]), R("pm" + x, s_[P96, 1, :, :, :, 0:2]), MUL)
-        lst = [(R(K, s_[P96, 0]), I96("ib"), R("bias1", s_[P96]))]
-        for bl, pr in ((0, "prA" + x), (1, "prB" + x)):
-            for q in range(4):
-                for t in range(4):
-                    lst.append((R(K, s_[P96, 0, bl, :, q, t]), R(pr, s_[:, 4 * q + t::16]), R("ones4", s_[:, 0, :])))
-        group(lst)
-        sl = (((0, 1), 0, 0), ((1, 2), 0, 1), ((2, 3), 0, 2), ((0, 3), 0, 3), ((0, 2), 1, 0), ((1, 3), 1, 1))
-        for t in range(4):
-            group([(R(B, s_[P96, 0, :, :, :, t]), I96("i16"), R("ph" + x, s_[P96, i, :, :, :, j])) for tu, i, j in sl if t not in tu])
-
-    def logic1a(h, H):
-        x = str(H)
-        A, B, K = "A" + x, "B" + x, "K" + x
-        e, pr = "e" + x, "pr" + x
-        tc(R("kc" + x, s_[P96]), R(K, s_[P96, 0, :, :, :, 2:4]))
-        tt(R("m2" + x, s_[P96]), R(K, s_[P96, 0, :, :, :, 0:2]), R("kc" + x, s_[P96]), MAX)
-        tt(R("mx" + x, s_[P96]), R("m2" + x, s_[P96, :, :, :, 0]), R("m2" + x, s_[P96, :, :, :, 1]), MAX)
-        for t in range(4):
-            tt(R(e, s_[P96, :, :, :, t]), R(K, s_[P96, 0, :, :, :, t]), R("mx" + x, s_[P96]), EQ)
-        for l, src in ((0, B), (1, A)):
-            for bl in (0, 1):
-                tt(R(pr, s_[P96, :, bl, l, :, :]), R(src, s_[P96, 0, bl]), R(e, s_[P96, bl]), MUL)
-        o = R(B, s_[:, 1, 0, 0:6, :, :])
-        group([(o, R(pr, s_[P96, :, :, :, :, t]), I96("i16")) for t in range(4)])
-        for bl in (0, 1):
-            group([(R(A, s_[P96, 1, bl, :, 0:2, :]), I96("i16"), R(pr, s_[P96, :, bl, :, :, t])) for t in range(4)])
-        ts(R("xl" + x), o, R("pc", s_[:, 3:4]), ADD)
-
-    def uw(x, i):
-        return R("uw" + x, s_[P96, i])
-
-    def logic1b(h, H):
-        x = str(H)
-        A, K = "A" + x, "K" + x
-        U = lambda n, t: R(n + x, s_[P96, :, :, :, t])
-        for t in range(4):
-            tt(U("v", t), R(A, s_[P96, 1, :, :, 0, :]), U("h16", t), EQ)
-        ts(uw(x, 0), R(A, s_[P96, 1, :, :, 0, :]), -1024.0, ADD)
-        tc(uw(x, 1), R(A, s_[P96, 1, :, :, 1, :]))
-        tt(U("v2", 1), U("v", 1), U("v", 0), MUL)
-        tt(U("v2", 2), U("v", 2), U("v", 3), GT)
-        tt(U("v1", 1), U("v", 1), U("v", 0), GT)
-        tt(U("v1", 2), U("v", 2), U("v", 3), MUL)
-        cf = R(K, s_[P96, 1, :, :, 3, :])
-        group([(cf, I96("ib"), R("cz", s_[P96, 0, :, :, 0, :]))] + [(cf, I96("i16"), U("cs", t)) for t in range(4)] + [(cf, I96("n1"), uw(x, 1)), (cf, I96("n4"), uw(x, 0))])
-        V1 = {0: U("v", 0), 1: U("v1", 1), 2: U("v1", 2)}
-        V2 = {1: U("v2", 1), 2: U("v2", 2), 3: U("v", 3)}
-        for t in (1, 2, 3):
-            tt(uw(x, 2 + t), R(A, s_[P96, 0, :, :, :, t]), V2[t], MUL)
-        tc(uw(x, 2), cf)
-        for t in range(4):
-            tt(U("fm", t), cf, U("cs", t), EQ)
-        tt(R("kf" + x, s_[P96]), R(K, s_[P96, 0]), R("fm" + x, s_[P96]), MUL)
-        return V1, V2
-
-    def gather2(h, H, V1, V2):
-        x = str(H)
-        A, B, K = "A" + x, "B" + x, "K" + x
-        ax, ng = "aexq%d" % (h % 2), "ng" + x
-        U = lambda n, t: R(n + x, s_[P96, :, :, :, t])
-        for w, pr in (("w1", "prA" + x), ("w2", "prB" + x)):
-            tt(R(pr), IND(R(w, s_[:, 0:4096]), R("xl" + x)), R(ax, s_[:, H, :]), MUL)
-        act(R(ng), IND(R("num", s_[:, 0:4096]), R("xl" + x)))
-        reg = lambda hf, r: R(K, s_[P96, hf, :, :, r, :])
-        sc = ["i16", "n1", "n2", "n3"]
-        lst = [(R(K, s_[P96]), I96("ib"), R("ck2", s_[P96]))]
-        for t in (1, 2, 3):
-            lst += [(reg(0, 2), I96(sc[t]), U("e", t)), (reg(0, 3), I96(sc[t]), V2[t]), (reg(1, 2), I96(sc[t]), U("e", t)), (reg(1, 2), I96(sc[t]), V2[t])]
-        for t in (1, 2):
-            lst += [(reg(0, 1), I96(sc[t]), V1[t]), (reg(1, 2), I96(["", "n2", "n4"][t]), V1[t])]
-        for t in range(4):
-            lst.append((reg(1, 1), I96("i32"), R("kf" + x, s_[P96, :, :, :, t])))
-        for w, pr in ((0, "prA" + x), (1, "prB" + x)):
-            for bl in (0, 1):
-                for q in range(4):
-                    if w == 0:
-                        lst.append((R(K, s_[P96, 0, bl, :, 0:2, q]), R(pr, s_[:, 8 * bl + q::16]), R("pkk")))
-                    else:
-                        lst.append((R(K, s_[P96, 1, bl, :, 0, q]), R(pr, s_[:, 8 * bl + q::16]), R("ones4", s_[:, 0, :])))
-                    lst.append((R(K, s_[P96, 0, bl, :, 2 + w, q]), R(pr, s_[:, 8 * bl + 4 + q::16]), R("ones4", s_[:, 0, :])))
-        lb = [(R(B, s_[P96]), I96("ib"), R("cb", s_[P96]))]
-        for bl in (0, 1):
-            for q in range(4):
-                o = R(B, s_[P96, :, bl, :, :, q])
-                lb += [(o, R(ng, s_[:, 8 * bl + 4 + q::16]), R("pk1")), (o, R(ng, s_[:, 8 * bl + q::16]), R("pk0"))]
-        rb = lambda hf, r: R(B, s_[P96, hf, :, :, r, :])
-        lb += [(rb(0, 0), I96("n1"), uw(x, 1)), (rb(1, 3), I96("n4"), uw(x, 0))]
-        for i in (3, 4, 5):
-            lb += [(rb(1, 3), I96("i16"), uw(x, i)), (rb(0, 2), I96("n1"), uw(x, i))]
-        group(lb)
-        la = [(R(A, s_[P96, 1, :, :, 2:4, :]), I96("ib"), R("cz", s_[P96, 1, :, :, 2:4, :]))]
-        for bl in (0, 1):
-            for q in range(4):
-                la.append((R(A, s_[P96, 1, bl, :, 2:4, q]), R(ng, s_[:, 8 * bl + q::16]), R("pkz", s_[:, 0, :, 0:2])))
-        for r in (2, 3):
-            la.append((R(A, s_[P96, 1, :, :, r, :]), I96("n1"), uw(x, 2)))
-        group(la)
-        group(lst)
-
-    def logic2(h, H, V1, V2):
-        x = str(H)
-        A, B, K = "A" + x, "B" + x, "K" + x
-        U = lambda n, t: R(n + x, s_[P96, :, :, :, t])
-        kr = lambda hf, r: R(K, s_[P96, hf, :, :, r, :])
-        rb = lambda hf, r: R(B, s_[P96, hf, :, :, r, :])
-        ra = lambda r: R(A, s_[P96, 1, :, :, r, :])
-        uf = lambda i: R("uf" + x, s_[P96, i])
-        G1, G2, W, O, P2, GW, GN, WKD, Q, OQ = 6, 7, 8, 9, 10, 11, 12, 13, 14, 15
-        ts(uw(x, P2), ra(3), 0.0, EQ)
-        ts(uw(x, O), kr(1, 2), 0.0, GT)
-        tc(uf(0), kr(0, 1))
-        tc(uf(1), kr(0, 2))
-        tt(uw(x, G1), kr(0, 0), R("mx" + x, s_[P96]), LT)
-        tt(uf(2), kr(1, 1), uf(0), MAX)
-        tt(uf(3), kr(0, 3), uf(1), MAX)
-        tt(uw(x, W), kr(0, 3), uf(1), GT)
-        tt(uf(0), kr(1, 0), uf(2), MAX)
-        tt(uw(x, P2), uw(x, P2), uw(x, G1), MUL)
-        tt(uw(x, WKD), rb(1, 0), uw(x, W), MUL)
-        tt(uw(x, G2), uf(3), uf(0), GT)
-        tt(uw(x, Q), rb(1, 2), uw(x, WKD), SUB)
-        tt(uw(x, G2), uw(x, G2), uw(x, P2), MUL)
-        tt(uw(x, OQ), uw(x, O), uw(x, Q), MUL)
-        tt(uw(x, GW), uw(x, G2), uw(x, W), MUL)
-        tt(uf(1), uw(x, WKD), uw(x, OQ), ADD)
-        tt(uw(x, GN), uw(x, G2), uw(x, GW), SUB)
-        tt(uw(x, 16), ra(2), uw(x, OQ), SUB)
-        tt(uw(x, 17), rb(1, 1), uf(1), ADD)
-        tt(uw(x, 18), rb(0, 0), uw(x, G1), MUL)
-        tt(uw(x, 19), rb(0, 2), uw(x, G1), MUL)
-        tt(uw(x, 20), rb(1, 3), uw(x, G1), MUL)
-        tt(uw(x, 21), rb(0, 1), uw(x, GN), MUL)
-        tt(uw(x, 22), rb(0, 3), uw(x, GW), MUL)
-        tt(uw(x, 16), uw(x, 16), uw(x, G2), MUL)
-        tt(uw(x, 17), uw(x, 17), uw(x, G2), MUL)
-        go = lambda r: R(A, s_[P96, 0, :, :, r, :])
-        group([(go(0), I96("i16"), uw(x, 18)), (go(0), I96("i16"), uw(x, 21))])
-        group([(go(2), I96("i16"), uw(x, 19)), (go(2), I96("i16"), uw(x, 22))])
-        mm(go(3), I96("i16"), uw(x, 16), True, True)
-        group([(go(1), I96("i16"), uw(x, 20)), (go(1), I96("i16"), uw(x, 17))])
-        for t in range(4):
-            tt(U("px", t), go(0), U("e", t), MUL)
-        for t in (1, 2, 3):
-            tt(U("pb", t), go(2), V2[t], MUL)
-        for t in range(4):
-            tt(U("pd", t), go(3), U("fm", t), MUL)
-        for t in (0, 1, 2):
-            tt(U("pa", t), go(1), V1[t], MUL)
-        for bl in (0, 1):
-            o = R("fb", s_[:, 192 * H + 96 * bl:192 * H + 96 * bl + 96])
-            group([(o, R(n + x, s_[P96, bl]), I96("i16")) for n in ("cs", "px", "pb", "pd", "pa")])
-        c = s_[:, 192 * H:192 * H + 192]
-        act(R("fw", c), R("fb", c))
-        tc(R("fu", c), R("fb", c))
-
-    def out_half(h, H):
-        n = "3" + "ab"[H]
-        act(R("ef" + n), R("mb", s_[:, 2 * H:2 * H + 2, :, 0:6, :, :]))
-        send("ef" + n, nxt(-h), "el" + n, "er%d" % (3 + H))
-        arrival("el" + n, "er%d" % (3 + H), len(topo.engines(nxt(h), core)), 4000)
-
-    def msum(h, last=False):
-        for b in range(4):
-            o = R("mg", s_[:, 1536 * b:1536 * b + 1536])
-            i = IND(R("mt", s_[:, 0:2048]), R("fu", s_[:, 96 * b:96 * b + 96]))
-            if last and b % 2 == 0:
-                tc(o, i)
-            else:
-                act(o, i)
-        for b in range(4):
-            if last and b == 2:
-                out_half(h, 0)
-            group([(R("mb", s_[:, b, :, 0:6, :, :]), R("ib"), R("mg", s_[:, 1536 * b + t:1536 * b + 1536:16])) for t in range(16)])
-        if last:
-            out_half(h, 1)
-            return
-        act(R("ef%d" % h), R("mb", s_[:, :, :, 0:6, :, :]))
-        if h:
-            send("ef%d" % h, nxt(-h), "el%d" % h, "er%d" % h)
-            arrival("el%d" % h, "er%d" % h, len(topo.engines(nxt(h), core)), 4000)
-
-    def expand(h):
-        for t in range(16):
-            if h == 0:
-                tc(R("aexp0", s_[:, :, t::16]), R("av0"))
-            else:
-                sel(R("aexp%d" % (h % 2), s_[:, :, t::16]), R("av%d" % h), [[0, 384]], EQ, 0.0, 0, 0)
-        for H in (0, 1):
-            for t in range(16):
-                j = 192 * H + 96 * (t // 8)
-                sel(R("aexq%d" % (h % 2), s_[:, H, t::16]), R("av%d" % h, s_[:, j:j + 96]), [[0, 96]], EQ, 0.0, 0, 0)
-
-    ts(R("fw"), R("cuti"), 1.0, MUL)
-    dist(0)
-    ts(R("kmk"), R("kidi"), 0.0, GE)
-    dma("Y", R("km8", s_[0:8, :]), R("kmk"))
-    for gg in range(8):
-        dma("Y", R("k2i", s_[:, gg, :]), ("kid", s_[gg, :]))
-        dma("S", R("u2i", s_[0:64, gg, :]), ("up", s_[gg, :]))
-    dma("Y", R("mt"), ("m", s_[:, :]))
-    tc(R("khi"), R("kidi"))
-    ms(R("num"), 0.0)
-    ms(R("w1", s_[:, 0:1024]), 255.0)
-    ms(R("w2", s_[:, 0:1024]), 255.0)
-    tt(R("klo"), R("kidi"), R("khi"), SUB)
-    tc(R("uhi"), R("upi", s_[:, 0:128:2]))
-    tc(R("upe"), R("upi", s_[:, 0:128:2]))
-    tt(R("ulo"), R("upi", s_[:, 0:128:2]), R("uhi"), SUB)
-    ts(R("ubit"), R("upe"), 1, AND)
-    ts(R("usg"), R("ubit"), -2.0, MUL, 1.0, ADD)
-    dma("Y", R("num", s_[0::16, 2048:4096]), R("khi"))
-    dma("S", R("num", s_[1::16, 2048:4096]), R("klo"))
-    dma("Y", R("num", s_[0::16, 1024:2048]), R("uhi"))
-    dma("S", R("num", s_[1::16, 1024:2048]), R("ulo"))
-    dma("Y", R("num", s_[4::16, 1024:2048]), R("usg"))
-    for k, n in enumerate(("n1", "n2", "n3", "n4")):
-        ts(R(n, s_[P96, :]), R("i16", s_[P96, :]), -1.0 - k, MUL)
-    tc(R("ib"), R("i16"))
-    tc(R("i32"), R("i16"))
-    ts(R("nb"), R("i16"), -1.0, MUL)
+    dma("Y", [(R("cuti"), ("cut0", s_[:, :]))])
+    dma("S", [(R("lki"), ("lk", s_[:, :]))])
+    dma("Y", [(R("av0"), ("a", s_[:, :])), (R("ak0"), ("a0", s_[:, :]))])
+    dma("S", [(R("kidi"), ("kid", s_[:, :]))])
+    for b in COLS:
+        ms(R("row" + b), 0.0)
+        ms(R("pk" + b), 0.0)
+        if b not in MEMO:
+            MEMO[b] = paints(b)
+        for a, rows, cs, x in MEMO[b]:
+            o = R("row" + b, s_[32 * a:32 * a + 1, rows, cs])
+            op([o], [o], {"V": lambda o=o, x=x: g.vector.memset(ap(o), x), "S": lambda o=o, x=x: g.scalar.activation(ap(o), ap(o), ACT.Identity, bias=x)})
+        dma("Y", [(R("pk" + b, s_[16 * gg:16 * gg + 16, gg if b == "b" else slice(16 * gg, 16 * gg + 16), :]), R("row" + b, s_[0::32])) for gg in range(8)])
+    dma("Y", [(R("st"), ("s", s_[:, :]))], [R("pka")])
+    ms(R("p1"), 1.0)
+    sel(R("p1"), R("p1"), [[-1, 128]], EQ, 0.0, 0, 1)
+    iota(R("koff"), [[2048, 4], [0, 24]], 0, 0)
+    iota(R("num"), [[1, 2048]], 0, 0)
+    dma("Y", [(R("num", s_[0::16, :]), ("kid", s_[:, :])), (R("num", s_[1::16, :]), ("up", s_[:, :]))])
+    send("av0", [(nxt(h), "av%d" % h) for h in (1, 2, 3)], "ar", 20000)
+    for n, x in (("n1", -1.0), ("n2048", -2048.0), ("p2048", 2048.0), ("p4", 4.0), ("n4", -4.0), ("p128", 128.0), ("p2", 2.0), ("n2", -2.0), ("n128", -128.0)):
+        ts(R(n), R("p1"), x, MUL)
+    for t in range(4):
+        ms(R("ct", s_[:, :, :, t]), 0.375 - 0.25 * t)
+    ms(R("on"), 1.0)
+    ms(R("rt0", s_[:, :, :, :, 7]), 0.0)
+    ms(R("bd0"), 0.0)
+    dma("Y", [(R("bd0", s_[16 * gg:16 * gg + 16, gg, :]), ("a", s_[16 * gg:16 * gg + 16, :])) for gg in range(8)])
+    ts(R("kmk"), R("kidi"), 0.0, LT, -256.0, MUL)
+    dma("S", [(R("km8", s_[0:8, :]), R("kmk"))])
+    cp(R("ib"), R("p1"), "V")
     ms(R("g8i"), 1.0)
     sel(R("g8i"), R("g8i"), [[1, 128]], GE, 0.0, 0, -16)
     sel(R("g8i"), R("g8i"), [[-1, 128]], GE, 0.0, 15, 16)
-    for i, bk in enumerate(("A1", "B1", "K1", "K0")):
-        mm(R(bk), R("g8i", s_[0:8, :]), R("km8", s_[0:8, 512 * i:512 * i + 512]), True, True)
-        tt(R("sm", s_[:, 512 * i:512 * i + 512]), R(bk), R("st", s_[:, 512 * i:512 * i + 512]), MUL)
-    tc(R("k2h"), R("k2i"))
-    tc(R("u2h", s_[0:64]), R("u2i", s_[0:64, :, 0:32:2]))
-    ts(R("u2b", s_[0:64]), R("u2h", s_[0:64]), 0.5, MUL, 1023.75, ADD)
-    mm(R("B0", s_[:, 0, 0]), R("k2h"), R("i16"), True, True)
-    mm(R("B0", s_[:, 0, 1, 0:4]), R("u2h", s_[0:64]), R("i16", s_[0:64, 0:64]), True, True)
-    mm(R("B0", s_[:, 0, 1, 4:8]), R("u2b", s_[0:64]), R("i16", s_[0:64, 0:64]), True, True)
-    tc(R("lkl"), R("B0", s_[:, 0, 0]))
-    ts(R("lkr"), R("B0", s_[:, 0, 0]), 1.0, ADD)
-    tc(R("lup"), R("B0", s_[:, 0, 1, 0:4]))
-    tc(R("lup2"), R("B0", s_[:, 0, 1, 4:8]))
-    inherit(0, 0)
-    expand(0)
-    inherit(0, 1)
-    act(R("tmpn"), IND(R("num", s_[:, 2048:4096]), R("lkl")))
-    act(R("tmpm"), IND(R("num", s_[:, 2048:4096]), R("lkr")))
-    act(R("tmpu"), IND(R("num", s_[:, 0:2048]), R("lup2")))
-    for i in (0, 1):
-        dma("Y", R("num", s_[2 + i::16, 2048:4096]), R("tmpn", s_[i::16, :]))
-        dma("Y", R("num", s_[4 + i::16, 2048:4096]), R("tmpm", s_[i::16, :]))
-        dma("Y", R("num", s_[2 + i::16, 1024:2048]), R("tmpu", s_[i::16, :]))
-    tc(R("g8"), R("ones4", s_[:, 0, :]))
-    for k, n in enumerate(("gl", "gkl", "gkr")):
-        ts(R(n), R("g8"), 0.25, MUL, R("clm", s_[:, k:k + 1]), MUL)
-    for n in ("pk1", "pk0", "pkz", "cb", "cz", "ck2"):
-        ms(R(n), 0.0)
-    for t in (0, 1):
-        tc(R("pkk", s_[:, :, t]), R("g8"))
-    for (n, hf, r, pos, neg) in (("pk1", 0, 0, "gl", None), ("pk1", 0, 1, "gkl", "gl"), ("pk1", 0, 2, "gl", None), ("pk1", 0, 3, "gkr", "gl"),
-                                 ("pk1", 1, 0, "gkr", "gkl"), ("pk1", 1, 1, "gkl", None), ("pk1", 1, 2, None, "gkl"),
-                                 ("pk0", 1, 1, None, "gl"), ("pk0", 1, 2, "gkl", None), ("pk0", 1, 3, "gl", None), ("pkz", 0, 0, "gkl", None)):
-        o = R(n, s_[:, hf, :, r])
-        if neg is None:
-            tc(o, R(pos))
-        elif pos is None:
-            ts(o, R(neg), -1.0, MUL)
+    ms(R("w"), 0.0)
+    sel(R("w"), R("w"), [[-8, 8], [-1, 8]], NE, 4.0, 0, 1)
+    sel(R("w"), R("w"), [[-8, 8], [0, 8]], NE, -4.0, -7, 1)
+    sel(R("w", s_[:, :, 7]), R("w", s_[:, :, 7]), [[-8, 8]], NE, 4.0, -2, 1)
+    cp(R("keep"), R("p1"), "V")
+    ms(R("keep", s_[:, :, AK:P + 1:P - AK]), 0.0)
+
+    def dist(ak, ow):
+        for k in range(4):
+            c = s_[:, 384 * k:384 * k + 384]
+            tt(R("dif", c), IND(R(ak, s_[:, 0:384]), R("lku", s_[:, 24 * k:24 * k + 24])), R("av0"), SUB)
+            op([R("absd", c)], [R("dif", c)], {"S": lambda c=c: g.scalar.activation(ap(R("absd", c)), ap(R("dif", c)), ACT.Abs)})
+        for q in range(4):
+            pe([(R("X2", s_[:, q::4, 0:12]), ST("z%d" % q, 15 - r), R("absd", s_[:, r::16])) for r in range(16)])
+        dk = lambda a, b: R("X2", s_[:, a:b, 0:12])
+        tt(R("yd"), dk(0, 16), R("kw", s_[:, 0:16]), ADD)
+        tt(dk(16, 32), dk(16, 32), R("kw", s_[:, 16:32]), ADD)
+        tt(dk(0, 8), dk(16, 24), R("yd", s_[:, 0:8]), MIN)
+        tt(R("yd2"), dk(24, 32), R("yd", s_[:, 8:16]), MIN)
+        tt(R("oi"), dk(0, 8), R("yd2"), MIN)
+        ts(R("oj"), R("oi"), 2047, AND)
+        cp(R(ow), R("oj"), "V")
+
+    cp(R("lku"), R("lki"), "V")
+    tt(R("lkf"), R("lki"), R("koff"), ADD)
+    for q in range(4):
+        aff(R("kw", s_[:, q::4, :]), R("lkf"), 1.0, 384.0 * q)
+    dist("ak0", "own0")
+
+    cp(R("cf"), R("cuti"), "V")
+    aff(R("hf"), R("cf"), 0.5, 1023.75, "V")
+    half = lambda n, H, k: R(n, s_[P96, :, 2 * H:2 * H + 2, :, k])
+    for H, (be, bk) in enumerate((("D0", "K"), ("D1", "PR"))):
+        x = str(H)
+        blk = lambda n, r: R(n, s_[:, 192 * H + 96 * r:192 * H + 96 * r + 96])
+        pe([(R(be, s_[P96, r::2, :, a:a + n]), blk("hf", r), R(m, s_[:, :, o:o + n])) for r in (0, 1) for a, n, d in ((0, 3, 1), (3, 2, 2), (5, 1, 3)) for m, o in (("p1", 0), ("n1", d))])
+        ts(slot("e" + x, s_[0:6]), slot(be, s_[0:6]), 0.0, EQ)
+        pe_open([(R(bk, s_[P96, r::2, :, 0:4]), blk("cf", r), R("p1")) for r in (0, 1)] + [(slot(bk, s_[0:4]), I("p1"), R("ct", s_[P96]))], True, False)
+        pe_open([(slot(bk, t), I("n2048"), slot("e" + x, j)) for j, tu in enumerate(PAIRS) for t in tu], False, True)
+        y = lambda k: slot("y" + x + "f", k)
+        k_ = lambda k: slot(bk, k)
+        cp(y(s_[0:2]), k_(s_[1:4:2]), "V")
+        tt(k_(4), k_(0), y(0), MIN)
+        tt(k_(5), k_(0), y(0), MAX)
+        tt(y(2), k_(2), y(1), MIN)
+        tt(y(3), k_(2), y(1), MAX)
+        tt(k_(6), k_(4), y(2), MAX)
+        tt(y(4), k_(5), y(3), MIN)
+        tt(k_(0), k_(4), y(2), MIN)
+        tt(k_(3), k_(5), y(3), MAX)
+        tt(k_(2), k_(6), y(4), MAX)
+        tt(k_(1), k_(6), y(4), MIN)
+        ts(half("ns", H, s_[0:4]), k_(s_[0:4]), 12582912.0, ADD, -12582912.0, ADD)
+        ts(half("fl", H, s_[0:2]), half("ns", H, s_[0:4:2]), 0.0, LT)
+        tt(half("fr", H, s_[0:4]), k_(s_[0:4]), half("ns", H, s_[0:4]), SUB)
+        aff(slot("e" + x, s_[6:8]), half("ns", H, s_[2:4]), 0.5, 1023.75, "V")
+    for i, (role, f) in enumerate(((0, 0), (2, 1), (3, 1))):
+        pe([(R("X1", s_[:, 48 * i:48 * i + 48, :]), R("ns", s_[P96, :, :, :, role]), I("p1")), (R("X1", s_[:, 48 * i:48 * i + 48, :]), R("fl", s_[P96, :, :, :, f]), I("p2048"))])
+    cp(R("il"), R("X1", s_[:, 0:144, :]), "V")
+    for i in range(3):
+        for j in (0, 1):
+            cp(R("mg", s_[:, 1536 * i + 768 * j:1536 * i + 768 * j + 768]), IND(R("num", s_[:, 0:2048]), R("il", s_[:, 96 * i + 48 * j:96 * i + 48 * j + 48])))
+    for H, (be, b1, b2) in enumerate((("D0", "Oa", "K"), ("D1", "Ob", "PR"))):
+        x = str(H)
+        u = lambda k: R("u" + x, s_[P96, k])
+        ON = R("on", s_[P96])
+        lst = []
+        for r in (0, 1):
+            for q in range(4):
+                for i, (a, k) in enumerate(((0, 1), (1, 2), (3, 2))):
+                    lst.append((R(be, s_[P96, r::2, q, a:a + k]), R("mg", s_[:, 1536 * i + 8 * H + 4 * r + q:1536 * i + 1536:16]), R("p1", s_[:, 0::4, 2 - k:2])))
+        ns, fr, fAB, fCD = (lambda k: half("ns", H, k)), (lambda k: half("fr", H, k)), half("fl", H, 0), half("fl", H, 1)
+        lst += [(slot(be, k), I("n1"), ON) for k in (0, 2, 4)]
+        lst += [(slot(be, 5), I("p1"), ns(0)), (slot(be, 5), I("p2048"), fAB), (slot(be, 5), I("p1"), ON), (slot(be, 6), I("p1"), ns(3)), (slot(be, 6), I("n1"), ns(2)),
+                (slot(be, 7), I("p4"), fr(3)), (slot(be, 7), I("n4"), fr(2))]
+        pe(lst)
+        zP, z, zl1, hP, sw, s3, t3, zq2, zq3, zl2, zl3, zs, zb = [u(k) for k in range(13)]
+        tt(zP, slot(be, 0), fAB, MUL)
+        aff(hP, zP, 0.5, 1024.25, "V")
+        tt(z, slot(be, 5), fAB, MUL)
+        tt(zl1, slot(be, 5), fCD, MUL)
+        tt(sw, slot("e" + x, 6), hP, EQ)
+        tt(s3, slot("e" + x, 7), hP, EQ)
+        tt(t3, s3, fCD, ADD)
+        for o, m, k in ((zq2, sw, 2), (zl2, s3, 1), (zl3, sw, 3), (zs, sw, 6), (zb, sw, 7), (zq3, t3, 4)):
+            tt(o, slot(be, k), m, MUL)
+        CT = R("ct", s_[P96, :, :, 0])
+        sums = {AK: [("p1", z), ("n1", ON)], A0: [("p1", ns(0)), ("p2048", fAB), ("p1", ON), ("n1", z)], B0: [("p1", ns(1)), ("p2048", fAB), ("p1", ON), ("n1", z)],
+                V: [("p128", t3), ("p128", sw)], U: [("p128", ON)], U2: [("p128", ON)], L: [("p1", zl1), ("n1", fCD), ("p1", zl2), ("p1", zl3)],
+                C: [("p1", ns(2)), ("p2048", fCD), ("p1", zs)], D: [("p1", ns(3)), ("p2048", fCD), ("n1", zs)], P: [("p1", ON), ("p1", zP)],
+                Q: [("p1", ON), ("p1", zq2), ("p1", zq3)], F: [("p128", fCD)], BA: [("p4", fr(0)), ("p4", CT)], BB: [("p4", fr(1)), ("p4", CT)],
+                BC: [("p4", fr(2)), ("p4", CT), ("p1", zb)]}
+        for b, f0, n in ((b1, 0, 7), (b2, 8, 8)):
+            pe([(slot(b, f - f0), I(m), src) for f in range(f0, f0 + n) for m, src in sums[f]])
+            for r in (0, 1):
+                for q in range(4):
+                    cp(R("rt0", s_[P96, 2 * H + r, q, :, f0:f0 + n]), R(b, s_[P96, r::2, q, 0:n]))
+    dma("Y", [(R("mt"), ("m", s_[:, :]))], [R("il")])
+    RB = ("Oa", "Ob", "D0", "D1")
+    for q in range(4):
+        pe([(R(RB[q], s_[:, 3 * r:3 * r + 3]), R("rt0", s_[P96, r, q]), I("p1")) for r in range(4)], False)
+        cp(R("rec", s_[:, 384 * q:384 * q + 384]), R(RB[q], s_[:, 0:12]))
+    for i, bk in enumerate(("X1", "K", "PR", "X2")):
+        c = s_[:, 512 * i:512 * i + 512]
+        pe([(R(bk), R("ib"), R("st", c)), (R(bk), R("g8i", s_[0:8, :]), R("km8", s_[0:8, 512 * i:512 * i + 512]))])
+        relu(R("sm", c), R(bk))
+    ms(R("sm", s_[:, 1:2]), 255.0)
+    ms(R("rt", s_[:, :, :, :, 0:8]), 0.0)
+    ms(R("md", s_[:, :, :, :, 0:2]), 0.0)
+    iota(R("bd1"), [[0, 3072]], 0, 0)
+    iota(R("pi", s_[:, 0:1]), [[0, 1]], 0, 1)
+    ts(R("pi", s_[:, 1:2]), R("pi", s_[:, 0:1]), 3, AND)
+    ts(R("pc"), R("pi", s_[:, 1:2]), -2048.0, MUL)
+
+    def front(h, H):
+        x, G = str(H), "g" + "ab"[h % 2] + str(H)
+        cp(R(G), IND(R("rec", s_[:, 0:1536]), R("own%d" % h, s_[:, 48 * H:48 * H + 48])))
+        for q2 in (0, 1):
+            pe([(R("X1", s_[:, 0:192, q2]), ST("mix", 8 - 8 * b), R(G, s_[:, 384 * q2 + 192 * b:384 * q2 + 192 * b + 192])) for b in (0, 1)])
+        cp(R("sl" + x), R("X1", s_[:, 0:192, :]), "V")
+        for c in range(8):
+            cp(R("sg" + x, s_[:, 768 * c:768 * c + 768]), IND(R("sm", s_[:, 0:2048]), R("sl" + x, s_[:, 48 * c:48 * c + 48])))
+
+    def picks(b, name, G, k=slice(0, 8)):
+        return [(R(b, s_[P96, r::2, q, k]), R(G, s_[:, 192 * q + 96 * r:192 * q + 96 * r + 96]), PK(name, k.start, k.stop - k.start)) for r in (0, 1) for q in range(4)]
+
+    R1, Y4, YM, N2, HD = 0, 1, 2, 3, 4
+
+    def prelim(h, H):
+        x, G = str(H), "g" + "ab"[h % 2] + str(H)
+        e = lambda k: slot("e" + x, k)
+        pe(picks("PR", "pr", G), False)
+        cp(slot("yp" + x, s_[0:2]), slot("PR", s_[0:2]), "V")
+        relu(e(s_[0:2]), slot("PR", s_[4:6]), es="V")
+        aff(e(HD), slot("PR", 6), 0.5, 1023.75, "V")
+        tt(slot("yp" + x, 2), slot("PR", 2), slot("yp" + x, 0), MAX)
+        tt(e(YM), slot("PR", 3), slot("yp" + x, 2), MAX)
+        relu(e(N2), e(YM), -1.0, es="V")
+
+    def errs(h, H):
+        x, G, bd = str(H), "g" + "ab"[h % 2] + str(H), "bd%d" % (h % 2)
+        e = lambda k: slot("e" + x, k)
+        for c in (0, 4, 1, 5, 2, 6, 3, 7):
+            lst = []
+            for v in range(24 * c, 24 * c + 24):
+                r, uu = v // 96, v % 96
+                lst.append((R("Oa" if uu < 64 else "Ob", s_[32 * r:32 * r + 32, uu % 64 // 4, uu % 4, :]), R("sg" + x, s_[:, 32 * v:32 * v + 32]), R(bd, s_[:, :, 192 * H + v])))
+            pe(lst, False)
+        cp(R("os" + x, s_[0:64, 0:16]), R("Oa", s_[0:64]))
+        cp(R("os" + x, s_[0:64, 16:24]), R("Ob", s_[0:64, 0:8]))
+        pe_open(picks("K", "kb", G) + [(slot("K", k), I(m), e(j)) for k, m, j in ((1, "p1", Y4), (2, "p1", R1), (4, "n1", Y4), (4, "n1", YM))], True, False)
+        pe_open([(R("K", s_[P96, 2 * gg:2 * gg + 2]), R("os" + x, s_[0:64, :, :, gg]), R("w", s_[0:64])) for gg in range(8)], False, True)
+        pe(picks("D0", "d0", G) + [(slot("D0", k), I(m), e(j)) for k, m, j in ((4, "p2", HD), (5, "p1", Y4), (5, "p1", YM), (5, "n1", N2), (6, "p1", N2))])
+        pe(picks("D1", "d1", G) + [(slot("D1", k), I(m), e(j)) for k, m, j in ((3, "n1", R1), (4, "p1", R1), (7, "n2", Y4), (7, "n1", YM))])
+
+    def logic(h, H):
+        x, G = str(H), "g" + "ab"[h % 2] + str(H)
+        k, y, u = (lambda j: slot("K", j)), (lambda j: slot("y" + x + "f", j)), (lambda j: R("u" + x, s_[P96, j]))
+        tau, eC, eDs, g2, mu, w = [u(j) for j in range(6)]
+        cp(y(s_[0:2]), k(s_[3:5]), "V")
+        relu(y(3), k(5), es="V")
+        relu(y(2), k(6), 1.0, -BIG, "V")
+        tt(y(s_[4:6]), k(s_[0:2]), y(s_[0:2]), MAX)
+        tt(k(0), k(5), slot("yp" + x, 1), LT)
+        ts(k(5), k(5), 0.0, GT)
+        tt(k(1), k(1), y(1), LT)
+        tt(k(2), k(2), y(2), MAX)
+        tt(k(s_[6:8]), k(s_[6:8]), y(s_[3:5]), MAX)
+        tt(k(4), k(2), y(5), LT)
+        tt(tau, k(7), y(3), LT)
+        tt(k(3), k(6), y(4), LT)
+        tt(eC, k(5), tau, MUL)
+        tt(eDs, k(0), tau, MUL)
+        pr = {}
+
+        def prod(m, b, j, out=None):
+            pr[(b, j, m[1])] = o = out or u(6 + len(pr))
+            tt(o, slot(b, j), m, MUL)
+            return o
+        tDP, tCD = prod(tau, "D0", 7), prod(tau, "D1", 0)
+        tt(g2, k(4), eC, MUL)
+        cCD = prod(eC, "D1", 0)
+        tphi = prod(tau, "D1", 1)
+        tt(mu, k(3), g2, ADD)
+        gCP = prod(g2, "D1", 6)
+        tbA = prod(tau, "D1", 2)
+        tt(w, k(1), mu, MUL)
+        mLP = prod(mu, "D0", 0)
+        rest = [prod(mu, "D0", j) for j in (1, 2, 3)]
+        pe(picks("PR", "pr", G, slice(7, 8)) + [(slot("PR", 7), I(m), s) for m, s in (("p1", tDP), ("p1", cCD), ("n1", gCP), ("p1", w), ("p1", mLP))])
+        cp(R("xs", s_[P96, :, 2 * H:2 * H + 2, :]), slot("PR", 7))
+        mRD, mQC, mPQ = rest
+        mL = prod(mu, "D0", 4)
+        sCP, tbB, tbC, sbC, cbA, wb, mbB, mbC = (prod(eDs, "D1", 6), prod(tau, "D1", 3), prod(tau, "D1", 4), prod(eDs, "D1", 4), prod(eC, "D1", 5), prod(w, "D1", 7),
+                                                 prod(mu, "D0", 5), prod(mu, "D0", 6))
+        sums = ((0, (("p1", mQC), ("n1", tDP), ("n1", tCD), ("p1", gCP), ("p1", sCP))), (1, (("p1", mRD), ("n1", w), ("p1", tCD), ("n1", cCD), ("n1", sCP))),
+                (2, (("p1", mL),)), (3, (("p1", mPQ), ("p1", gCP))), (4, (("n128", mu), ("n128", tphi), ("n128", eDs))), (5, (("p1", tbA), ("p1", cbA), ("p1", wb))),
+                (6, (("p1", tbB), ("p1", mbB))), (7, (("p1", tbC), ("n1", sbC), ("p1", mbC))))
+        pe([(slot("PR", j), I(m), s) for j, terms in sums for m, s in terms])
+        for r in (0, 1):
+            for q in range(4):
+                cp(R("rt", s_[P96, 2 * H + r, q, :, 8:16]), R("PR", s_[P96, r::2, q, :]))
+        for r in (0, 1):
+            if h < 3:
+                cp(R("md", s_[P96, 2 * H + r, :, :, 2:4]), R("PR", s_[P96, r::2, :, 0:2]))
+
+    def back(h):
+        G, lk = "g" + "ab"[h % 2], "lk%d" % (h % 2)
+        pe([(R("X1", s_[:, 0:48, :]), R("xs", s_[P96]), I("p1"))])
+        cp(R("xl"), R("X1", s_[:, 0:48, :]), "V")
+        for j in (0, 1):
+            cp(R(lk, s_[:, 768 * j:768 * j + 768]), IND(R("num", s_[:, 0:2048]), R("xl", s_[:, 48 * j:48 * j + 48])))
+        for q in range(4):
+            pe_open([(R(RB[q], s_[:, 6 * H:6 * H + 6]), R("keep"), R(G + str(H), s_[:, 192 * q:192 * q + 192])) for H in (0, 1)]
+                    + [(R(RB[q], s_[:, 3 * r:3 * r + 3]), R("rt", s_[P96, r, q]), I("p1")) for r in range(4)], True, False)
+        for q in range(4):
+            pe_open([(R(RB[q], s_[:, 3 * r:3 * r + 3]), ST("sel", 0), R(lk, s_[:, 4 * r + q::16])) for r in range(4)], False, True)
+            cp(R("rec", s_[:, 384 * q:384 * q + 384]) if h < 3 else R("r16", s_[:, q]), R(RB[q], s_[:, 0:12]))
+
+    def msum(h):
+        G, lk, av = "g" + "ab"[h % 2], "lk%d" % (h % 2), "av%d" % h
+        if h < 3:
+            pe([(R("X2", s_[:, 12 * H:12 * H + 12]), ST("mg", 12 - 4 * q), R(G + str(H), s_[:, 192 * q:192 * q + 192])) for H in (0, 1) for q in range(4)]
+               + [(R("X2", s_[:, 6 * r:6 * r + 6]), R("md", s_[P96, r]), I("p1")) for r in range(4)]
+               + [(R("X2", s_[:, 6 * r:6 * r + 6]), ST("ml", 12 - 4 * q), R(lk, s_[:, 4 * r + q::16])) for r in range(4) for q in range(4)])
         else:
-            tt(o, R(pos), R(neg), SUB)
-    tt(R("pkz", s_[:, 0, :, 1]), R("gl"), R("gkr"), ADD)
-    for (hf, r, c) in ((0, 2, 1.0), (0, 3, -1.0), (1, 1, 1.0), (1, 2, -1.0), (1, 3, -1.0)):
-        ms(R("cb", s_[:, hf, :, :, r, :]), c)
-    ms(R("cz", s_[:, 0, :, :, 0, :]), -1.0)
-    ms(R("ck2", s_[:, 0]), 3.0)
-    ms(R("ck2", s_[:, 1, :, :, 0, :]), 3.0)
-    ms(R("ck2", s_[:, 1, :, :, 2, :]), 6.0)
-    for x in "01":
-        ms(R("pa" + x, s_[:, :, :, :, 3]), 0.0)
-        ms(R("pb" + x, s_[:, :, :, :, 0]), 0.0)
-    for h in range(N):
-        if h:
-            inherit(h, 0)
-            inherit(h, 1)
-        gather1(h, 0)
-        gather1(h, 1)
-        if h:
-            msum(h - 1)
-        else:
-            act(R("w1", s_[:, 2048:4096]), IND(R("sm", s_[:, 0:2048]), R("lkl")))
-            act(R("w1", s_[:, 1024:2048]), IND(R("sm", s_[:, 0:2048]), R("lup")))
-            act(R("w2", s_[:, 2048:4096]), IND(R("sm", s_[:, 0:2048]), R("lkr")))
-            act(R("w2", s_[:, 1024:2048]), IND(R("w1", s_[:, 0:2048]), R("lup2")))
-        logic1a(h, 0)
-        logic1a(h, 1)
-        V = {}
+            pe([(R("X2", s_[:, 0:24]), ST("mr", 12 - 4 * q), R("r16", s_[:, q])) for q in range(4)])
+        cp(R("mu"), R("X2", s_[:, 0:24]), "V")
+        for c in range(8):
+            cp(R("mg", s_[:, 768 * c:768 * c + 768]), IND(R("mt", s_[:, 0:2048]), R("mu", s_[:, 48 * c:48 * c + 48])))
         for H in (0, 1):
-            V[H] = logic1b(h, H)
-            gather2(h, H, *V[H])
+            bk = "X2" if h < 3 or H == 0 else "X1"
+            o = lambda a, b: R("X2", s_[:, 6 * a:6 * b]) if bk == "X2" else R("X1", s_[:, 48 * a:48 * b, :])
+            for r in (2 * H, 2 * H + 1):
+                pe([(o(r, r + 1), R("p1"), R("mg", s_[:, 1536 * r + t:1536 * r + 1536:16])) for t in range(16)])
+            if h == 3:
+                n = "3" + "ab"[H]
+                tt(R("ef" + n), o(2 * H, 2 * H + 2), R(av, s_[:, 192 * H:192 * H + 192]), MUL)
+                send("ef" + n, [(nxt(-h), "el" + n)], "er%d" % (3 + H), 4000)
+        if h < 3:
+            tt(R("ef%d" % h), R("X2", s_[:, 0:24]), R(av), MUL)
+            if h:
+                send("ef%d" % h, [(nxt(-h), "el%d" % h)], "er%d" % h, 4000)
+
+    def cut_out():
+        bk = R("K", s_[:, 0:12])
+        pe([(bk, ST("my", 12 - 4 * q), R("r16", s_[:, q])) for q in range(4)])
+        ts(R("y0"), bk, 2048.0, MIN)
+        for c, n in ((1, "z1"), (2, "z2"), (3, "y3")):
+            relu(R(n), bk, 1.0, -2048.0 * c)
+        for c in (1, 2):
+            ts(R("y%d" % c), R("z%d" % c), 2048.0, MIN)
+        pe([(R("PR", s_[:, 0:12]), ST("st", c), R("y%d" % c)) for c in range(4)])
+        ts(R("ycf"), R("PR", s_[:, 0:12]), R("pc"), ADD)
+        dma("Y", [(("yc", s_[:, :]), R("ycf"))])
+
+    for h in range(N):
+        for H in (0, 1):
+            front(h, H)
         if h == 0:
-            dist(1)
+            dist("av3", "ownx")
+            send("ownx", [(nxt(j), "own%d" % j) for j in (1, 2, 3)], "ao", 5000)
+        else:
+            msum(h - 1)
         if h + 1 < N:
-            expand(h + 1)
-        logic2(h, 0, *V[0])
-        logic2(h, 1, *V[1])
-        if h + 2 < N:
-            dist(h + 2)
-    dma("Y", ("yc", s_[:, :]), R("fw"))
+            dma("Y", [(R("bd%d" % ((h + 1) % 2), s_[16 * gg:16 * gg + 16, gg, :]), R("av%d" % (h + 1), s_[16 * gg:16 * gg + 16, :])) for gg in range(8)])
+        for H in (0, 1):
+            prelim(h, H)
+        for H in (0, 1):
+            errs(h, H)
+            logic(h, H)
+        back(h)
     tt(R("ef0"), R("ef0"), R("el1"), ADD)
     tt(R("ef0"), R("ef0"), R("el2"), ADD)
-    msum(3, True)
+    msum(3)
+    cut_out()
     for H in (0, 1):
         c = s_[:, 192 * H:192 * H + 192]
         tt(R("yes", c), R("ef0", c), R("el3" + "ab"[H]), ADD)
-        tt(R("yes", c), R("yes", c), R("av0", c), MUL)
-        dma("Y", ("ye", c), R("yes", c))
-    for i in schedule():
-        issue(prog[i])
+        dma("Y", [(("ye", c), R("yes", c))])
+    if "order" not in MEMO:
+        MEMO["order"] = schedule()
+    for i, e in MEMO["order"]:
+        issue(prog[i], e)
     for s, c in sorted(total.items()):
         if known["G"].get(s, 0) < c:
             g.wait_ge(T.sem[s], c)

@@ -43,11 +43,11 @@ PAIRS = ((0, 1), (1, 2), (2, 3), (0, 2), (1, 3), (0, 3))
 mat("sel", [fld(f) * (f in (AK, P)) for f in range(16)], "c")
 mat("kb", [bA - bD, bC - 4 * FCD - bD, bB - bD + BIG * (fld(U2) / 128 - FS), bB - bD, bA + bB - 2 * bD + 4 * FCD, bC - bD, 3.5 * ONE - bD + BIG * FS, 3.5 * ONE - bD])
 mat("pr", [bC - bD - 8 * (ONE - FCD), BIG * (FS - ONE), bA - bD - 8 * FCD, bB - bD - 8 * FCD, bA - bB, bA - bC - 4 * ONE + 8 * FCD, nD, nP])
-mat("d0", [nL - nP, nL + ONE - nD, nQ - nC, nP - nQ, -2048 * ONE - nL, 2 * bD - bA - bB - 4 * FCD, Z, nD - nP])
-mat("d1", [nC - nD, FCD - FS, bD - bA, bA - bB, bB - bC, bC - bD, nC - nP, bA + bB - bD - bC + 8 * FCD])
+mat("d0", [nD - nP, nL - nP, bA - bB, -2048 * ONE - nL, FCD - FS, nQ - nC, bD - bA, nP - nQ])
+mat("d1", [nC - nD, nL + ONE - nD, bC - bD, bB - bC, 2 * bD - bA - bB - 4 * FCD, Z, nC - nP, bA + bB - bD - bC + 8 * FCD])
 mat("mix", [nA, nL, nP, nB, nL + ONE, nC, nQ, nD], "c")
-mat("mg", [fld(A0), fld(B0), nC, nD], "c")
-mat("ml", [fld(AK), fld(AK), Z, Z], "c")
+mat("mg", [x for role in (fld(A0), fld(B0), nC, nD) for x in (Z, Z, Z, role)], "c")
+mat("ml", [x for role in (fld(AK), fld(AK), Z, Z) for x in (Z, Z, Z, role)], "c")
 mat("mr", [nA, nB, nC, nD], "c")
 mat("my", [nA + 2048 * bA, nB + 2048 * bB, nC + 2048 * bC, nD + 2048 * bD], "c")
 mat("st", [(np.arange(16) // 4 == j // 4) * (j % 4 == 3) * 1.0 for j in range(16)], "c")
@@ -115,8 +115,11 @@ _b("kmk g8i ib", [128, 128], BF)
 for _h in COLS:
     _b("row" + _h, [128, 4, len(COLS[_h])], F16)
     _b("pk" + _h, [128, 8, len(COLS[_h])] if _h == "b" else [128, 144, NM[_h]], F16)
-_b("xs", [128, 8, 4, 4], F16)
+_b("xw0 xw1", [128, 17, 8, 26], F16)
 _b("md", [128, 4, 8, 4, 4], F16)
+_b("mr32", [128, 144], F32)
+CHAIN = (3,)
+DUE = 1500.0
 _m("idt", "p1 n1 p2 n2 p4 n4 p128 n128 p2048 n2048", [128, 32, 4], F16)
 _b("keep", [128, 8, 16], F16)
 _b("w", [128, 8, 8], F32)
@@ -127,10 +130,10 @@ _b("on", [128, 16, 4], F16)
 _b("ns fr", [128, 8, 4, 4, 4], F16)
 _b("fl", [128, 8, 4, 4, 2], F16)
 _b("il", [128, 288], U16)
-_b("rt0 rt", [128, 4, 4, 8, 16], F16)
+_b("rt0 rt", [128, 2, 8, 16, 8], F16)
 _b("rec", [128, 1536], F32)
 _b("r16", [128, 4, 384], F16)
-_b("lk0 lk1", [128, 1536], F16)
+_b("lk0 lk1", [128, 768], F16)
 _b("mg", [128, 6144], F16)
 _b("mu", [128, 384], U16)
 _m("ef", "ef0 ef1 ef2 yes ycf", [128, 384], F32)
@@ -148,9 +151,14 @@ for _h in "01":
     _b("yp" + _h, [128, 16, 4, 3], F32)
     _b("e" + _h, [128, 16, 4, 8], F16)
     _b("u" + _h, [128, 32, 16, 4], F16)
-SEMAPHORES = ["cV", "cS", "cP", "cG", "lsem", "ar", "ao"] + ["er%d" % h for h in (1, 2, 3, 4)] + ["d%d" % i for i in range(40)]
+SEMAPHORES = ["cV", "cS", "cP", "cG", "lsem", "ar", "as", "ao", "ap"] + ["er%d" % h for h in (1, 2, 3, 4)] + ["d%d" % i for i in range(40)]
 WHOLE = np.s_[:]
-CYC, GATH, PEC, WAKE, OV = 0.95, 1.35, 0.48, 120, 25
+BIAS = {"": 300, "mg": 2500}
+CYC, GATH, PEC, WAKE, OV = 0.85, 1.56, 0.44, 130, 35
+JIT, TRIES, SEED, STRETCH = 0.5, 1500, 1, 300
+CASES = ((0.75, 1.1, 0, 160, 0.9), (1.0, 1.0, 0, 130, 1.0), (1.25, 1.0, -15, 100, 1.12))
+WIDE = False
+LIST = "VS"
 MEMO = {}
 
 
@@ -167,6 +175,7 @@ def rank_program(g, core, T, topo):
     cache = MEMO.setdefault("cols", {})
     ndma = [0]
     prog = []
+    due, fill, soon = {}, [], []
 
     def R(name, idx=WHOLE):
         if name in ALIAS:
@@ -307,38 +316,42 @@ def rank_program(g, core, T, topo):
     def two(r):
         return SCRATCH[r[0]][2] in (F16, BF, U16)
 
-    def op(outs, ins, fns, both=False, lab=0):
+    def op(outs, ins, fns, both=False):
         o, i = parts(outs), parts(ins)
         n = len(cols(outs[0]))
-        d = {}
+        d, lab = {}, any(r[0] == "@" for r in ins)
         for e in fns:
-            if any(r[0] == "@" for r in ins):
+            if lab:
                 d[e] = 60 + CYC * GATH * n
             elif e == "G":
                 d[e] = 190 + 2 * CYC * n
             elif e == "S":
-                d[e] = CYC * max(64, n)
+                d[e] = OV + CYC * max(64, n)
             else:
-                d[e] = CYC * max(64, n * (2 if both else 0.5 if all(two(r) for r in o + i[:1]) else 1))
+                d[e] = OV + CYC * max(64, n * (2 if both else 0.5 if all(two(r) for r in o + i[:1]) else 1))
         prog.append({"k": "op", "o": o, "i": i, "a": {e: [f] for e, f in fns.items()}, "d": d, "lat": 0, "lab": lab})
 
-    def dma(e, pairs, after=()):
-        prog.append({"k": "dma", "o": parts([x for x, _ in pairs]), "i": parts([y for _, y in pairs]) + list(after), "a": pairs, "d": {e: 60 * len(pairs)}, "lat": 2200, "lab": 0})
+    def dma(e, pairs, after=(), lat=2500):
+        prog.append({"k": "dma", "o": parts([x for x, _ in pairs]), "i": parts([y for _, y in pairs]) + list(after), "a": pairs, "d": {e: 60 * len(pairs)}, "lat": lat, "lab": 0})
 
     def arrival(names, s, c, lat):
         prog.append({"k": "arr", "o": [R(n) for n in names], "i": [], "a": (s, c), "d": {"X": 0}, "lat": lat, "lab": 0})
 
-    def send(src, dsts, s, lat):
-        prog.append({"k": "send", "o": [R(n) for _, n in dsts], "i": [R(src)], "a": (R(src), dsts, s), "d": {"G": 1200}, "lat": 0, "lab": 0})
+    def send(src, dsts, s, lat, after=()):
+        prog.append({"k": "send", "o": [R(n) for _, n in dsts], "i": [R(src)] + list(after), "a": (R(src), dsts, s), "d": {"G": 1200}, "lat": 0, "lab": 0})
         arrival([n for _, n in dsts], s, sum(len(topo.engines(c, core)) for c, _ in dsts), lat)
 
     def schedule():
         n = len(prog)
-        W, Lr, hist, pre = {}, {}, {}, []
+        W, Lr, hist, pre, data = {}, {}, {}, [], []
         for i, o in enumerate(prog):
             S = hazards(W, Lr, o["o"], o["i"], lambda j: False)
+            data.append(set(S))
             note(W, Lr, i, o["o"], o["i"])
             es = "".join(o["d"])
+            if es == "G":
+                S.update(hist.setdefault("G", [])[-1:])
+                hist["G"].append(i)
             for b in set(r[0] for r in o["o"] + o["i"] if psum(r)):
                 hb = hist.setdefault(b, {"P": [], "V": [], "S": []})
                 if es == "P":
@@ -357,43 +370,65 @@ def rank_program(g, core, T, topo):
         for i, S in enumerate(pre):
             for j in S:
                 suc[j].append(i)
-        pe = ["P" in o["d"] for o in prog]
-        gap = lambda i, j: 0 if pe[i] and pe[j] else WAKE
-        prio = [0.0] * n
-        for i in range(n - 1, -1, -1):
-            prio[i] = max([prio[j] + gap(i, j) for j in suc[i]] + [0.0]) + min(prog[i]["d"].values()) + prog[i]["lat"]
-        left, ready = [len(S) for S in pre], [0.0] * n
-        ES = "XYGPSV"
-        avail, t = {e: set() for e in ES}, {e: 0.0 for e in ES}
+        def ready(c, e, done, eng, wake=WAKE):
+            t = 0.0
+            for j in pre[c]:
+                x = done[j] if eng[j] == e and (e == "P" or j not in data[c]) else done[j] + wake
+                if x > t:
+                    t = x
+            return t
 
-        def free(i):
-            for e in prog[i]["d"]:
-                avail[e].add(i)
-        for i in range(n):
-            if not left[i]:
-                free(i)
-        order = []
-        while len(order) < n:
-            pick = None
-            for e in ES:
-                if avail[e]:
-                    now = max(t[e], min(ready[i] for i in avail[e]))
-                    if pick is None or now < pick[0]:
-                        only = lambda i: 300 if e == "V" and len(prog[i]["d"]) == 1 else 0
-                        pick = (now, max((i for i in avail[e] if ready[i] <= now), key=lambda i: (prio[i] + only(i), -i)), e)
-            now, c, e = pick
-            for e2 in prog[c]["d"]:
-                avail[e2].remove(c)
-            end = now + prog[c]["d"][e] + (0 if e == "P" else OV)
-            if e != "X":
-                t[e] = end
-            order.append((c, e))
-            for j in suc[c]:
-                ready[j] = max(ready[j], end + prog[c]["lat"] + gap(c, j))
-                left[j] -= 1
-                if not left[j]:
-                    free(j)
-        return order
+        def place(jit, bias):
+            prio = [0.0] * n
+            for i in range(n - 1, -1, -1):
+                prio[i] = max([prio[j] for j in suc[i]] + [prio[due[i]] + DUE if i in due else 0.0]) + (min(prog[i]["d"].values()) + 60) * jit[i] + prog[i]["lat"]
+            busy, done, eng, order = {e: [(1e18, 1e18)] for e in "XYGPSV"}, [0.0] * n, [""] * n, []
+            for c in sorted(range(n), key=lambda i: (-prio[i], i)):
+                pick = None
+                for e, d in prog[c]["d"].items():
+                    t, bz = ready(c, e, done, eng), busy[e]
+                    at, hi = 0, len(bz) - 1
+                    while at < hi:
+                        mid = (at + hi) // 2
+                        at, hi = (mid + 1, hi) if bz[mid][1] <= t else (at, mid)
+                    while bz[at][0] < t + d:
+                        t, at = max(t, bz[at][1]), at + 1
+                    key = t + d + (bias[c] if e == "V" else 0)
+                    if pick is None or key < pick[0]:
+                        pick = (key, t, d, at, e)
+                _, t, d, at, eng[c] = pick
+                if eng[c] != "X":
+                    busy[eng[c]].insert(at, (t, t + d))
+                done[c] = t + d + prog[c]["lat"]
+                order.append((t, len(order), c, eng[c]))
+            return [(c, e) for _, _, c, e in sorted(order)]
+
+        def span(order, kg, kp, ov, wake, _):
+            t, done, eng = {e: 0.0 for e in "XYGPSV"}, [0.0] * n, [""] * n
+            for c, e in order:
+                eng[c] = e
+                end = max(ready(c, e, done, eng, wake), t[e] if e != "X" else 0.0) + prog[c]["d"][e] * (kg if prog[c]["lab"] else kp if e == "P" else 1) + (ov if e in "VS" else 0)
+                t[e], done[c] = end, end + prog[c]["lat"]
+            return max(done)
+        state = [SEED]
+
+        def rng():
+            state[0] = (state[0] * 1103515245 + 12345) % 2 ** 31
+            return state[0] / 2 ** 31
+        best = None
+        jit, bias = [1.0] * n, [BIAS.get(o["o"][0][0], BIAS[""]) if o["o"] else 0 for o in prog]
+        for _ in range(TRIES):
+            j2, b2, a = list(jit), list(bias), int(rng() * n)
+            for i in range(a, min(n, a + int(rng() * STRETCH))):
+                if best and rng() < 0.3:
+                    j2[i] = 1 + JIT * (2 * rng() - 1)
+                    b2[i] = bias[i] + 1000 * (rng() - 0.5)
+            o = place(j2, b2)
+            cost = sum(span(o, *m) / m[4] for m in CASES)
+            if best is None or cost <= best[0]:
+                best, jit, bias = (cost, o), j2, b2
+        MEMO["span"] = best[0] / len(CASES)
+        return best[1]
 
     def tt(out, a, b, o):
         op([out], [a, b], {"V": lambda: g.vector.tensor_tensor(ap(out), ap(a), ap(b), o)}, a[0] != "@" and not psum(a) and not psum(b))
@@ -452,14 +487,17 @@ def rank_program(g, core, T, topo):
     PK = lambda n, a, k: R("pk" + OFF[n][0], s_[:, :, OFF[n][1] + a:OFF[n][1] + a + k])
     ST = lambda n, a: R("pk" + OFF[n][0], s_[:, a:a + 128, OFF[n][1]])
     slot = lambda b, k: R(b, s_[P96, :, :, k])
+    fslot = lambda b, k: R(b, s_[P96, k // 4::2, k % 4, :])
     cores = list(T.cores)
     nxt = lambda h: cores[(rank + h) % N]
 
-    dma("Y", [(R("cuti"), ("cut0", s_[:, :]))])
+    dma("S", [(R("cuti"), ("cut0", s_[:, :]))])
+    cp(R("cf"), R("cuti"), "V")
     dma("S", [(R("lki"), ("lk", s_[:, :]))])
-    dma("Y", [(R("av0"), ("a", s_[:, :])), (R("ak0"), ("a0", s_[:, :]))])
-    dma("S", [(R("kidi"), ("kid", s_[:, :]))])
-    for b in COLS:
+    dma("Y", [(R("av0"), ("a", s_[:, :])), (R("ak0"), ("a0", s_[:, :]))], lat=3200)
+    dma("Y", [(R("kidi"), ("kid", s_[:, :]))], lat=3500)
+    for b in "cb":
+        soon.extend((len(prog), len(prog) + 1))
         ms(R("row" + b), 0.0)
         ms(R("pk" + b), 0.0)
         if b not in MEMO:
@@ -467,22 +505,25 @@ def rank_program(g, core, T, topo):
         for a, rows, cs, x in MEMO[b]:
             o = R("row" + b, s_[32 * a:32 * a + 1, rows, cs])
             op([o], [o], {"V": lambda o=o, x=x: g.vector.memset(ap(o), x), "S": lambda o=o, x=x: g.scalar.activation(ap(o), ap(o), ACT.Identity, bias=x)})
-        dma("Y", [(R("pk" + b, s_[16 * gg:16 * gg + 16, gg if b == "b" else slice(16 * gg, 16 * gg + 16), :]), R("row" + b, s_[0::32])) for gg in range(8)])
-    dma("Y", [(R("st"), ("s", s_[:, :]))], [R("pka")])
+        dma("Y", [(R("pk" + b, s_[16 * gg:16 * gg + 16, gg if b == "b" else slice(16 * gg, 16 * gg + 16), :]), R("row" + b, s_[0::32])) for gg in range(8)], lat=4000)
     ms(R("p1"), 1.0)
     sel(R("p1"), R("p1"), [[-1, 128]], EQ, 0.0, 0, 1)
-    iota(R("koff"), [[2048, 4], [0, 24]], 0, 0)
     iota(R("num"), [[1, 2048]], 0, 0)
     dma("Y", [(R("num", s_[0::16, :]), ("kid", s_[:, :])), (R("num", s_[1::16, :]), ("up", s_[:, :]))])
-    send("av0", [(nxt(h), "av%d" % h) for h in (1, 2, 3)], "ar", 20000)
+    dma("Y", [(R("st"), ("s", s_[:, :]))], [R("cf")], 5000)
+    ms(R("pka"), 0.0)
+    zc = R("pka", s_[:, 15::16, :])
+    ms(zc, 8192.0)
+    sel(zc, zc, [[-16, 9], [-4, 4]], GE, 0.0, 0, 1)
+    sel(zc, zc, [[16, 9], [4, 4]], GE, 0.0, 3, -1)
+    iota(R("koff"), [[2048, 4], [0, 24]], 0, 0)
+    send("av0", [(nxt(3), "av3")], "ar", 14000)
+    send("av0", [(nxt(h), "av%d" % h) for h in (1, 2)], "as", 20000)
     for n, x in (("n1", -1.0), ("n2048", -2048.0), ("p2048", 2048.0), ("p4", 4.0), ("n4", -4.0), ("p128", 128.0), ("p2", 2.0), ("n2", -2.0), ("n128", -128.0)):
         ts(R(n), R("p1"), x, MUL)
     for t in range(4):
         ms(R("ct", s_[:, :, :, t]), 0.375 - 0.25 * t)
     ms(R("on"), 1.0)
-    ms(R("rt0", s_[:, :, :, :, 7]), 0.0)
-    ms(R("bd0"), 0.0)
-    dma("Y", [(R("bd0", s_[16 * gg:16 * gg + 16, gg, :]), ("a", s_[16 * gg:16 * gg + 16, :])) for gg in range(8)])
     ts(R("kmk"), R("kidi"), 0.0, LT, -256.0, MUL)
     dma("S", [(R("km8", s_[0:8, :]), R("kmk"))])
     cp(R("ib"), R("p1"), "V")
@@ -493,6 +534,8 @@ def rank_program(g, core, T, topo):
     sel(R("w"), R("w"), [[-8, 8], [-1, 8]], NE, 4.0, 0, 1)
     sel(R("w"), R("w"), [[-8, 8], [0, 8]], NE, -4.0, -7, 1)
     sel(R("w", s_[:, :, 7]), R("w", s_[:, :, 7]), [[-8, 8]], NE, 4.0, -2, 1)
+    iota(R("bd0"), [[0, 3072]], 0, 0)
+    dma("Y", [(R("bd0", s_[16 * gg:16 * gg + 16, gg, :]), ("a", s_[16 * gg:16 * gg + 16, :])) for gg in range(8)])
     cp(R("keep"), R("p1"), "V")
     ms(R("keep", s_[:, :, AK:P + 1:P - AK]), 0.0)
 
@@ -513,12 +556,15 @@ def rank_program(g, core, T, topo):
         cp(R(ow), R("oj"), "V")
 
     cp(R("lku"), R("lki"), "V")
+    ts(R("yd2"), R("lki"), 192.0, GE, 576.0, MUL)
     tt(R("lkf"), R("lki"), R("koff"), ADD)
+    tt(R("lkf"), R("lkf"), R("yd2"), ADD)
     for q in range(4):
-        aff(R("kw", s_[:, q::4, :]), R("lkf"), 1.0, 384.0 * q)
+        aff(R("kw", s_[:, q::4, :]), R("lkf"), 1.0, 192.0 * q)
     dist("ak0", "own0")
 
-    cp(R("cf"), R("cuti"), "V")
+    for i in soon:
+        due[i] = len(prog)
     aff(R("hf"), R("cf"), 0.5, 1023.75, "V")
     half = lambda n, H, k: R(n, s_[P96, :, 2 * H:2 * H + 2, :, k])
     for H, (be, bk) in enumerate((("D0", "K"), ("D1", "PR"))):
@@ -550,21 +596,19 @@ def rank_program(g, core, T, topo):
     cp(R("il"), R("X1", s_[:, 0:144, :]), "V")
     for i in range(3):
         for j in (0, 1):
-            cp(R("mg", s_[:, 1536 * i + 768 * j:1536 * i + 768 * j + 768]), IND(R("num", s_[:, 0:2048]), R("il", s_[:, 96 * i + 48 * j:96 * i + 48 * j + 48])))
+            cp(R("mg", s_[:, 1536 * i + 768 * j:1536 * i + 768 * j + 768]), IND(R("num", s_[:, 0:2048]), R("il", s_[:, 96 * i + 48 * j:96 * i + 48 * j + 48])), "VS"[j])
     for H, (be, b1, b2) in enumerate((("D0", "Oa", "K"), ("D1", "Ob", "PR"))):
         x = str(H)
         u = lambda k: R("u" + x, s_[P96, k])
         ON = R("on", s_[P96])
-        lst = []
-        for r in (0, 1):
-            for q in range(4):
-                for i, (a, k) in enumerate(((0, 1), (1, 2), (3, 2))):
-                    lst.append((R(be, s_[P96, r::2, q, a:a + k]), R("mg", s_[:, 1536 * i + 8 * H + 4 * r + q:1536 * i + 1536:16]), R("p1", s_[:, 0::4, 2 - k:2])))
         ns, fr, fAB, fCD = (lambda k: half("ns", H, k)), (lambda k: half("fr", H, k)), half("fl", H, 0), half("fl", H, 1)
-        lst += [(slot(be, k), I("n1"), ON) for k in (0, 2, 4)]
+        lst = []
         lst += [(slot(be, 5), I("p1"), ns(0)), (slot(be, 5), I("p2048"), fAB), (slot(be, 5), I("p1"), ON), (slot(be, 6), I("p1"), ns(3)), (slot(be, 6), I("n1"), ns(2)),
                 (slot(be, 7), I("p4"), fr(3)), (slot(be, 7), I("n4"), fr(2))]
-        pe(lst)
+        pe_open(lst, True, False)
+        for i, (a, k) in enumerate(((0, 1), (1, 2), (3, 2))):
+            pe_open([(R(be, s_[P96, r::2, q, a:a + k]), R("mg", s_[:, 1536 * i + 8 * H + 4 * r + q:1536 * i + 1536:16]), R("p1", s_[:, 0::4, 2 - k:2]))
+                     for r in (0, 1) for q in range(4)] + [(slot(be, 2 * i), I("n1"), ON)], False, i == 2)
         zP, z, zl1, hP, sw, s3, t3, zq2, zq3, zl2, zl3, zs, zb = [u(k) for k in range(13)]
         tt(zP, slot(be, 0), fAB, MUL)
         aff(hP, zP, 0.5, 1024.25, "V")
@@ -581,24 +625,28 @@ def rank_program(g, core, T, topo):
                 C: [("p1", ns(2)), ("p2048", fCD), ("p1", zs)], D: [("p1", ns(3)), ("p2048", fCD), ("n1", zs)], P: [("p1", ON), ("p1", zP)],
                 Q: [("p1", ON), ("p1", zq2), ("p1", zq3)], F: [("p128", fCD)], BA: [("p4", fr(0)), ("p4", CT)], BB: [("p4", fr(1)), ("p4", CT)],
                 BC: [("p4", fr(2)), ("p4", CT), ("p1", zb)]}
-        for b, f0, n in ((b1, 0, 7), (b2, 8, 8)):
-            pe([(slot(b, f - f0), I(m), src) for f in range(f0, f0 + n) for m, src in sums[f]])
-            for r in (0, 1):
-                for q in range(4):
-                    cp(R("rt0", s_[P96, 2 * H + r, q, :, f0:f0 + n]), R(b, s_[P96, r::2, q, 0:n]))
-    dma("Y", [(R("mt"), ("m", s_[:, :]))], [R("il")])
-    RB = ("Oa", "Ob", "D0", "D1")
-    for q in range(4):
-        pe([(R(RB[q], s_[:, 3 * r:3 * r + 3]), R("rt0", s_[P96, r, q]), I("p1")) for r in range(4)], False)
-        cp(R("rec", s_[:, 384 * q:384 * q + 384]), R(RB[q], s_[:, 0:12]))
+        sums[7] = sums[U]
+        for b, f0 in ((b1, 0), (b2, 8)):
+            pe([(fslot(b, f - f0), I(m), src) for f in range(f0, f0 + 8) for m, src in sums[f]])
+            cp(R("rt0", s_[P96, H, :, f0:f0 + 8, :]), R(b, s_[P96]))
+    for H in (0, 1):
+        for j in (0, 1):
+            bk = (("Oa", "K"), ("Ob", "PR"))[H][j]
+            pe([(R(bk, s_[:, 6 * i + 3 * r:6 * i + 3 * r + 3]), R("rt0", s_[P96, H, :, :, 4 * r + 2 * j + i]), I("p1")) for i in (0, 1) for r in (0, 1)], False)
+            cp(R("rec", s_[:, 768 * H + 384 * j:768 * H + 384 * j + 384]), R(bk, s_[:, 0:12]))
+    dma("Y", [(R("mt"), ("m", s_[:, :]))], [R("rec")], 6000)
     for i, bk in enumerate(("X1", "K", "PR", "X2")):
         c = s_[:, 512 * i:512 * i + 512]
         pe([(R(bk), R("ib"), R("st", c)), (R(bk), R("g8i", s_[0:8, :]), R("km8", s_[0:8, 512 * i:512 * i + 512]))])
         relu(R("sm", c), R(bk))
     ms(R("sm", s_[:, 1:2]), 255.0)
-    ms(R("rt", s_[:, :, :, :, 0:8]), 0.0)
-    ms(R("md", s_[:, :, :, :, 0:2]), 0.0)
+    for n in ("xw0", "xw1"):
+        iota(R(n, s_[:, 0::2, :, 3:9]), [[0, 432]], 0, 0)
+        iota(R(n, s_[:, 0::2, :, 20:23]), [[0, 216]], 0, 0)
+    iota(R("rt", s_[:, :, :, 0:8, :]), [[0, 1024]], 0, 0)
+    iota(R("md", s_[:, :, :, 0:2, :]), [[0, 256]], 0, 0)
     iota(R("bd1"), [[0, 3072]], 0, 0)
+    cp(R("mr32"), R("pkc", s_[:, :, OFF["mr"][1]]))
     iota(R("pi", s_[:, 0:1]), [[0, 1]], 0, 1)
     ts(R("pi", s_[:, 1:2]), R("pi", s_[:, 0:1]), 3, AND)
     ts(R("pc"), R("pi", s_[:, 1:2]), -2048.0, MUL)
@@ -608,49 +656,59 @@ def rank_program(g, core, T, topo):
         cp(R(G), IND(R("rec", s_[:, 0:1536]), R("own%d" % h, s_[:, 48 * H:48 * H + 48])))
         for q2 in (0, 1):
             pe([(R("X1", s_[:, 0:192, q2]), ST("mix", 8 - 8 * b), R(G, s_[:, 384 * q2 + 192 * b:384 * q2 + 192 * b + 192])) for b in (0, 1)])
-        cp(R("sl" + x), R("X1", s_[:, 0:192, :]), "V")
-        for c in range(8):
+        cp(R("sl" + x), R("X1", s_[:, 0:192, :]), LIST)
+        for c in (0, 4, 1, 5, 2, 6, 3, 7):
             cp(R("sg" + x, s_[:, 768 * c:768 * c + 768]), IND(R("sm", s_[:, 0:2048]), R("sl" + x, s_[:, 48 * c:48 * c + 48])))
 
     def picks(b, name, G, k=slice(0, 8)):
         return [(R(b, s_[P96, r::2, q, k]), R(G, s_[:, 192 * q + 96 * r:192 * q + 96 * r + 96]), PK(name, k.start, k.stop - k.start)) for r in (0, 1) for q in range(4)]
 
     R1, Y4, YM, N2, HD = 0, 1, 2, 3, 4
+    xt = lambda H, k: R("xw" + str(H), s_[P96, 1:17:2, :, k])
 
     def prelim(h, H):
         x, G = str(H), "g" + "ab"[h % 2] + str(H)
         e = lambda k: slot("e" + x, k)
         pe(picks("PR", "pr", G), False)
-        cp(slot("yp" + x, s_[0:2]), slot("PR", s_[0:2]), "V")
-        relu(e(s_[0:2]), slot("PR", s_[4:6]), es="V")
-        aff(e(HD), slot("PR", 6), 0.5, 1023.75, "V")
+        cp(slot("yp" + x, s_[0:2]), slot("PR", s_[0:2]))
+        relu(e(s_[0:2]), slot("PR", s_[4:6]))
+        aff(e(HD), slot("PR", 6), 0.5, 1023.75)
+        cp(xt(H, 6), slot("PR", 7))
         tt(slot("yp" + x, 2), slot("PR", 2), slot("yp" + x, 0), MAX)
         tt(e(YM), slot("PR", 3), slot("yp" + x, 2), MAX)
-        relu(e(N2), e(YM), -1.0, es="V")
+        relu(e(N2), e(YM), -1.0)
 
     def errs(h, H):
         x, G, bd = str(H), "g" + "ab"[h % 2] + str(H), "bd%d" % (h % 2)
         e = lambda k: slot("e" + x, k)
-        for c in (0, 4, 1, 5, 2, 6, 3, 7):
+        for c in (0, 4, 1, 5, 2, 6, 3, 7) if not WIDE else ():
             lst = []
             for v in range(24 * c, 24 * c + 24):
                 r, uu = v // 96, v % 96
                 lst.append((R("Oa" if uu < 64 else "Ob", s_[32 * r:32 * r + 32, uu % 64 // 4, uu % 4, :]), R("sg" + x, s_[:, 32 * v:32 * v + 32]), R(bd, s_[:, :, 192 * H + v])))
             pe(lst, False)
-        cp(R("os" + x, s_[0:64, 0:16]), R("Oa", s_[0:64]))
-        cp(R("os" + x, s_[0:64, 16:24]), R("Ob", s_[0:64, 0:8]))
+        if not WIDE:
+            cp(R("os" + x, s_[0:64, 0:16]), R("Oa", s_[0:64]))
+            cp(R("os" + x, s_[0:64, 16:24]), R("Ob", s_[0:64, 0:8]))
+        for c in range(4 if WIDE else 0):
+            bk, r = ("Oa", "Ob")[c % 2], c // 2
+            for j in (0, 6):
+                pe([(R(bk, s_[:, y]), R("sg" + x, s_[:, 1536 * c + 128 * y:1536 * c + 128 * y + 128]), R(bd, s_[:, :, 192 * H + 48 * c + 4 * y:192 * H + 48 * c + 4 * y + 4]))
+                    for y in range(j, j + 6)], False)
+            for i in range(4):
+                cp(R("os" + x, s_[32 * r:32 * r + 32, 12 * (c % 2):12 * (c % 2) + 12, i, :]), R(bk, s_[32 * i:32 * i + 32, 0:12, :, i::4]))
         pe_open(picks("K", "kb", G) + [(slot("K", k), I(m), e(j)) for k, m, j in ((1, "p1", Y4), (2, "p1", R1), (4, "n1", Y4), (4, "n1", YM))], True, False)
         pe_open([(R("K", s_[P96, 2 * gg:2 * gg + 2]), R("os" + x, s_[0:64, :, :, gg]), R("w", s_[0:64])) for gg in range(8)], False, True)
-        pe(picks("D0", "d0", G) + [(slot("D0", k), I(m), e(j)) for k, m, j in ((4, "p2", HD), (5, "p1", Y4), (5, "p1", YM), (5, "n1", N2), (6, "p1", N2))])
-        pe(picks("D1", "d1", G) + [(slot("D1", k), I(m), e(j)) for k, m, j in ((3, "n1", R1), (4, "p1", R1), (7, "n2", Y4), (7, "n1", YM))])
+        pe(picks("D0", "d0", G) + [(slot("D0", k), I(m), e(j)) for k, m, j in ((2, "n1", R1), (3, "p2", HD))])
+        pe(picks("D1", "d1", G) + [(slot("D1", k), I(m), e(j)) for k, m, j in ((3, "p1", R1), (4, "p1", Y4), (4, "p1", YM), (4, "n1", N2), (5, "p1", N2), (7, "n2", Y4), (7, "n1", YM))])
 
     def logic(h, H):
         x, G = str(H), "g" + "ab"[h % 2] + str(H)
-        k, y, u = (lambda j: slot("K", j)), (lambda j: slot("y" + x + "f", j)), (lambda j: R("u" + x, s_[P96, j]))
-        tau, eC, eDs, g2, mu, w = [u(j) for j in range(6)]
-        cp(y(s_[0:2]), k(s_[3:5]), "V")
-        relu(y(3), k(5), es="V")
-        relu(y(2), k(6), 1.0, -BIG, "V")
+        k, y, u = (lambda j: slot("K", j)), (lambda j: slot("y" + x + "f", j)), (lambda j: xt(H, j))
+        tau, mu, g2, w, eC, eDs = [u(j) for j in range(6)]
+        cp(y(s_[0:2]), k(s_[3:5]))
+        relu(y(3), k(5))
+        relu(y(2), k(6), 1.0, -BIG)
         tt(y(s_[4:6]), k(s_[0:2]), y(s_[0:2]), MAX)
         tt(k(0), k(5), slot("yp" + x, 1), LT)
         ts(k(5), k(5), 0.0, GT)
@@ -662,76 +720,74 @@ def rank_program(g, core, T, topo):
         tt(k(3), k(6), y(4), LT)
         tt(eC, k(5), tau, MUL)
         tt(eDs, k(0), tau, MUL)
-        pr = {}
-
-        def prod(m, b, j, out=None):
-            pr[(b, j, m[1])] = o = out or u(6 + len(pr))
-            tt(o, slot(b, j), m, MUL)
-            return o
-        tDP, tCD = prod(tau, "D0", 7), prod(tau, "D1", 0)
+        prod = lambda o, n, b, j, m: tt(u(s_[o:o + n]), slot(b, j), u(s_[m:m + n]), MUL)
+        add = lambda terms, first, last: pe_open([(fslot("PR", f - C), I(m), u(j)) for f, m, j in terms], first, last)
         tt(g2, k(4), eC, MUL)
-        cCD = prod(eC, "D1", 0)
-        tphi = prod(tau, "D1", 1)
+        prod(22, 2, "D1", s_[0:7:6], 4)
         tt(mu, k(3), g2, ADD)
-        gCP = prod(g2, "D1", 6)
-        tbA = prod(tau, "D1", 2)
+        prod(24, 2, "D1", s_[2:4], 4)
         tt(w, k(1), mu, MUL)
-        mLP = prod(mu, "D0", 0)
-        rest = [prod(mu, "D0", j) for j in (1, 2, 3)]
-        pe(picks("PR", "pr", G, slice(7, 8)) + [(slot("PR", 7), I(m), s) for m, s in (("p1", tDP), ("p1", cCD), ("n1", gCP), ("p1", w), ("p1", mLP))])
-        cp(R("xs", s_[P96, :, 2 * H:2 * H + 2, :]), slot("PR", 7))
-        mRD, mQC, mPQ = rest
-        mL = prod(mu, "D0", 4)
-        sCP, tbB, tbC, sbC, cbA, wb, mbB, mbC = (prod(eDs, "D1", 6), prod(tau, "D1", 3), prod(tau, "D1", 4), prod(eDs, "D1", 4), prod(eC, "D1", 5), prod(w, "D1", 7),
-                                                 prod(mu, "D0", 5), prod(mu, "D0", 6))
-        sums = ((0, (("p1", mQC), ("n1", tDP), ("n1", tCD), ("p1", gCP), ("p1", sCP))), (1, (("p1", mRD), ("n1", w), ("p1", tCD), ("n1", cCD), ("n1", sCP))),
-                (2, (("p1", mL),)), (3, (("p1", mPQ), ("p1", gCP))), (4, (("n128", mu), ("n128", tphi), ("n128", eDs))), (5, (("p1", tbA), ("p1", cbA), ("p1", wb))),
-                (6, (("p1", tbB), ("p1", mbB))), (7, (("p1", tbC), ("n1", sbC), ("p1", mbC))))
-        pe([(slot("PR", j), I(m), s) for j, terms in sums for m, s in terms])
-        for r in (0, 1):
-            for q in range(4):
-                cp(R("rt", s_[P96, 2 * H + r, q, :, 8:16]), R("PR", s_[P96, r::2, q, :]))
-        for r in (0, 1):
-            if h < 3:
-                cp(R("md", s_[P96, 2 * H + r, :, :, 2:4]), R("PR", s_[P96, r::2, :, 0:2]))
+        prod(7, 2, "D0", s_[0:2], 0)
+        prod(19, 3, "D1", s_[5:8], 1)
+        add([(C, "p1", 23), (D, "n1", 22), (D, "n1", 23), (BA, "p1", 24), (BC, "n1", 25), (F, "n128", 1), (F, "n128", 5), (D, "n1", 3), (C, "n1", 7)], True, False)
+        prod(15, 2, "D1", s_[0:2], 0)
+        prod(17, 2, "D1", s_[3:5], 0)
+        add([(BC, "p1", 19), (C, "p1", 20), (Q, "p1", 20), (BA, "p1", 21), (C, "n1", 15), (D, "p1", 15), (D, "p1", 16), (BC, "p1", 17), (BB, "p1", 18)], False, False)
+        for j in (2, 4, 6):
+            prod(7 + j, 2, "D0", s_[j:j + 2], 0)
+        add([(BB, "p1", 9), (L, "p1", 10), (F, "n128", 11), (C, "p1", 12), (BA, "p1", 13), (Q, "p1", 14)], False, True)
+        cp(R("rt", s_[P96, H, :, 8:16, :]), R("PR", s_[P96]))
+        for r in range(2 if h == 3 else 0):
+            cp(R("md", s_[P96, 2 * H + r, :, 2:4, :]), R("PR", s_[P96, 0::2, 0:2, 4 * r:4 * r + 4]))
 
-    def back(h):
-        G, lk = "g" + "ab"[h % 2], "lk%d" % (h % 2)
-        pe([(R("X1", s_[:, 0:48, :]), R("xs", s_[P96]), I("p1"))])
-        cp(R("xl"), R("X1", s_[:, 0:48, :]), "V")
+    def back(h, H):
+        G, lk = "g" + "ab"[h % 2] + str(H), "lk" + str(H)
+        pe([(R("X1", s_[:, 0:24, :]), R("xw" + str(H), s_[P96, 1 - b:17 - b, :, k]), R("n1" if k == 20 else "p1", s_[P96, 0:24, b::2])) for k in (6, 22, 3, 7, 8, 20) for b in (0, 1)])
+        while fill and H:
+            due[fill.pop()] = len(prog)
+        cp(R("xl", s_[:, 48 * H:48 * H + 48]), R("X1", s_[:, 0:24, :]), LIST)
         for j in (0, 1):
-            cp(R(lk, s_[:, 768 * j:768 * j + 768]), IND(R("num", s_[:, 0:2048]), R("xl", s_[:, 48 * j:48 * j + 48])))
-        for q in range(4):
-            pe_open([(R(RB[q], s_[:, 6 * H:6 * H + 6]), R("keep"), R(G + str(H), s_[:, 192 * q:192 * q + 192])) for H in (0, 1)]
-                    + [(R(RB[q], s_[:, 3 * r:3 * r + 3]), R("rt", s_[P96, r, q]), I("p1")) for r in range(4)], True, False)
-        for q in range(4):
-            pe_open([(R(RB[q], s_[:, 3 * r:3 * r + 3]), ST("sel", 0), R(lk, s_[:, 4 * r + q::16])) for r in range(4)], False, True)
-            cp(R("rec", s_[:, 384 * q:384 * q + 384]) if h < 3 else R("r16", s_[:, q]), R(RB[q], s_[:, 0:12]))
+            cp(R(lk, s_[:, 384 * j:384 * j + 384]), IND(R("num", s_[:, 0:2048]), R("xl", s_[:, 48 * H + 24 * j:48 * H + 24 * j + 24])))
+        for j, bk in enumerate(("Oa", "Ob")):
+            o = lambda q, r, c: R(bk, s_[:, 6 * (q % 2) + 3 * r:6 * (q % 2) + 3 * r + 3, :, c])
+            pe_open([(R(bk, s_[:, 0:12]), R("keep"), R(G, s_[:, 384 * j:384 * j + 384]))], True, False)
+            pe_open([(o(q, r, WHOLE), R("rt", s_[P96, H, :, :, 4 * r + q]), I("p1")) for q in (2 * j, 2 * j + 1) for r in (0, 1)], False, False)
+            pe_open([(o(q, r, s_[b::2]), ST("sel", 0), R(lk, s_[:, 8 * b + 4 * r + q::16])) for q in (2 * j, 2 * j + 1) for r in (0, 1) for b in (0, 1)], False, True)
+            cp(R("r16", s_[:, 2 * j:2 * j + 2, 192 * H:192 * H + 192]) if h == 3 else R("rec", s_[:, 768 * H + 384 * j:768 * H + 384 * j + 384]), R(bk, s_[:, 0:12]))
 
     def msum(h):
         G, lk, av = "g" + "ab"[h % 2], "lk%d" % (h % 2), "av%d" % h
+        col = lambda r, q: 768 * (r // 2) + 192 * q + 96 * (r % 2)
+        mg = lambda c: R("mg", s_[:, 768 * c:768 * c + 768])
+        ind = lambda c: IND(R("mt", s_[:, 0:2048]), R("mu", s_[:, 48 * c:48 * c + 48]))
         if h < 3:
-            pe([(R("X2", s_[:, 12 * H:12 * H + 12]), ST("mg", 12 - 4 * q), R(G + str(H), s_[:, 192 * q:192 * q + 192])) for H in (0, 1) for q in range(4)]
-               + [(R("X2", s_[:, 6 * r:6 * r + 6]), R("md", s_[P96, r]), I("p1")) for r in range(4)]
-               + [(R("X2", s_[:, 6 * r:6 * r + 6]), ST("ml", 12 - 4 * q), R(lk, s_[:, 4 * r + q::16])) for r in range(4) for q in range(4)])
-        else:
-            pe([(R("X2", s_[:, 0:24]), ST("mr", 12 - 4 * q), R("r16", s_[:, q])) for q in range(4)])
-        cp(R("mu"), R("X2", s_[:, 0:24]), "V")
-        for c in range(8):
-            cp(R("mg", s_[:, 768 * c:768 * c + 768]), IND(R("mt", s_[:, 0:2048]), R("mu", s_[:, 48 * c:48 * c + 48])))
-        for H in (0, 1):
-            bk = "X2" if h < 3 or H == 0 else "X1"
-            o = lambda a, b: R("X2", s_[:, 6 * a:6 * b]) if bk == "X2" else R("X1", s_[:, 48 * a:48 * b, :])
-            for r in (2 * H, 2 * H + 1):
-                pe([(o(r, r + 1), R("p1"), R("mg", s_[:, 1536 * r + t:1536 * r + 1536:16])) for t in range(16)])
-            if h == 3:
-                n = "3" + "ab"[H]
-                tt(R("ef" + n), o(2 * H, 2 * H + 2), R(av, s_[:, 192 * H:192 * H + 192]), MUL)
-                send("ef" + n, [(nxt(-h), "el" + n)], "er%d" % (3 + H), 4000)
-        if h < 3:
+            for q in range(4):
+                pe([(R("X2", s_[:, 6 * q:6 * q + 6]), R("mr32", s_[:, 12 - 4 * r:140 - 4 * r]), R("rec", s_[:, col(r, q):col(r, q) + 96])) for r in range(4)])
+            cp(R("mu"), R("X2", s_[:, 0:24]), LIST)
+            for c in range(8):
+                fill.append(len(prog))
+                if c // 2 in CHAIN:
+                    tt(mg(c), ind(c), mg(c - 2), ADD)
+                else:
+                    cp(mg(c), ind(c))
+            for r in range(4):
+                pe([(R("X2", s_[:, 6 * r:6 * r + 6]), R("p1"), R("mg", s_[:, 1536 * q + 4 * r + t:1536 * q + 1536:16])) for q in range(4) if q + 1 not in CHAIN for t in range(4)])
             tt(R("ef%d" % h), R("X2", s_[:, 0:24]), R(av), MUL)
             if h:
-                send("ef%d" % h, [(nxt(-h), "el%d" % h)], "er%d" % h, 4000)
+                send("ef%d" % h, [(nxt(-h), "el%d" % h)], "er%d" % h, 9000)
+            return
+        for H in (0, 1):
+            c, n = s_[:, 192 * H:192 * H + 192], "3" + "ab"[H]
+            pe_open([(R("X2", s_[:, 0:12]), ST("mg", 3 - q), R(G + str(H), s_[:, 192 * q:192 * q + 192])) for q in range(4)], True, False)
+            pe_open([(R("X2", s_[:, 6 * r:6 * r + 6]), R("md", s_[P96, 2 * H + r]), I("p1")) for r in (0, 1)], False, False)
+            pe_open([(R("X2", s_[:, 6 * r:6 * r + 6, b::2]), ST("ml", 3 - q), R("lk" + str(H), s_[:, 8 * b + 4 * r + q::16])) for r in (0, 1) for q in range(4) for b in (0, 1)], False, True)
+            cp(R("mu", c), R("X2", s_[:, 0:12]), LIST)
+            for j in range(4 * H, 4 * H + 4):
+                cp(mg(j), ind(j), "VS"[j % 2] if H else "VS")
+            for r in (0, 1):
+                pe([(R("X2", s_[:, 12 + 6 * r:18 + 6 * r]), R("p1"), R("mg", s_[:, 3072 * H + 1536 * r + t:3072 * H + 1536 * r + 1536:16])) for t in range(16)])
+            tt(R("ef" + n), R("X2", s_[:, 12:24]), R(av, c), MUL)
+            send("ef" + n, [(nxt(-h), "el" + n)], "er%d" % (3 + H), 6000)
 
     def cut_out():
         bk = R("K", s_[:, 0:12])
@@ -750,17 +806,20 @@ def rank_program(g, core, T, topo):
             front(h, H)
         if h == 0:
             dist("av3", "ownx")
-            send("ownx", [(nxt(j), "own%d" % j) for j in (1, 2, 3)], "ao", 5000)
+            send("ownx", [(nxt(1), "own1")], "ao", 8000)
+            send("ownx", [(nxt(j), "own%d" % j) for j in (2, 3)], "ap", 12000)
         else:
             msum(h - 1)
         if h + 1 < N:
             dma("Y", [(R("bd%d" % ((h + 1) % 2), s_[16 * gg:16 * gg + 16, gg, :]), R("av%d" % (h + 1), s_[16 * gg:16 * gg + 16, :])) for gg in range(8)])
         for H in (0, 1):
             prelim(h, H)
-        for H in (0, 1):
-            errs(h, H)
-            logic(h, H)
-        back(h)
+        errs(h, 0)
+        logic(h, 0)
+        errs(h, 1)
+        back(h, 0)
+        logic(h, 1)
+        back(h, 1)
     tt(R("ef0"), R("ef0"), R("el1"), ADD)
     tt(R("ef0"), R("ef0"), R("el2"), ADD)
     msum(3)

@@ -102,9 +102,11 @@ _b("X1", [128, 256, 2], F32, "psum")
 _b("X2", [128, 32, 16], F32, "psum")
 _b("av0 av1 av2 av3 ak0", [128, 384], BF)
 _b("own0 own1 own2 own3 ownx lku xl", [128, 96], U16)
-_b("lki oi oj", [128, 96], I32)
+_b("lki oi", [128, 96], I32)
+_b("oj", [128, 4, 24], I32)
 _b("koff lkf yd2", [128, 96], F32)
-_b("kw", [128, 32, 12], F32)
+_b("kw", [128, 4, 4, 24], F32)
+_b("qs", [128, 4, 2, 12, 4], F16)
 _b("yd", [128, 16, 12], F32)
 _b("dif absd", [128, 1536], F16)
 _b("bd0 bd1", [128, 8, 384], BF)
@@ -115,16 +117,17 @@ _b("kmk g8i ib", [128, 128], BF)
 for _h in COLS:
     _b("row" + _h, [128, 4, len(COLS[_h])], F16)
     _b("pk" + _h, [128, 8, len(COLS[_h])] if _h == "b" else [128, 144, NM[_h]], F16)
-_b("xw0 xw1", [128, 17, 8, 26], F16)
+_b("xw0", [128, 17, 8, 26], F16)
+_b("xw1", [128, 35, 4, 26], F16)
 _b("md", [128, 4, 8, 4, 4], F16)
-_b("mr32", [128, 144], F32)
 CHAIN = (3,)
-DUE = 1500.0
+DUE = 0.0
 _m("idt", "p1 n1 p2 n2 p4 n4 p128 n128 p2048 n2048", [128, 32, 4], F16)
 _b("keep", [128, 8, 16], F16)
 _b("w", [128, 8, 8], F32)
 _b("cuti", [128, 384], I32)
-_b("cf hf", [128, 384], F16)
+_b("cf hf a16", [128, 384], F16)
+VIA = (0, 1)
 _b("ct", [128, 16, 4, 4], F16)
 _b("on", [128, 16, 4], F16)
 _b("ns fr", [128, 8, 4, 4, 4], F16)
@@ -133,20 +136,23 @@ _b("il", [128, 288], U16)
 _b("rt0 rt", [128, 2, 8, 16, 8], F16)
 _b("rec", [128, 1536], F32)
 _b("r16", [128, 4, 384], F16)
-_b("lk0 lk1", [128, 768], F16)
-_b("mg", [128, 6144], F16)
-_b("mu", [128, 384], U16)
+_b("mg mg0", [128, 6144], F16)
+_b("mu mu0", [128, 384], U16)
+_b("i32", [128, 128], F32)
 _m("ef", "ef0 ef1 ef2 yes ycf", [128, 384], F32)
 _b("el1 el2", [128, 384], F32)
-_b("el3a el3b ef3a ef3b", [128, 192], F32)
+NV = (256, 128)
+_b("el3a ef3a", [128, 256], F32)
+_b("el3b ef3b", [128, 128], F32)
 _m("yr", "y0 y1 y2 y3 z1 z2", [128, 384], F16)
 _b("pi", [128, 2], I32)
 _b("pc", [128, 1], F32)
 for _h in "01":
-    _b("ga%s gb%s" % (_h, _h), [128, 768], F16)
-    _b("sl" + _h, [128, 384], U16)
-    _b("sg" + _h, [128, 6144], BF)
-    _b("os" + _h, [128, 24, 4, 8], F32)
+    _n = NV[int(_h)]
+    _b("ga%s gb%s lk%s" % (_h, _h, _h), [128, 4 * _n], F16)
+    _b("sl" + _h, [128, 2 * _n], U16)
+    _b("sg" + _h, [128, 32 * _n], BF)
+    _b("os" + _h, [128, 32, 4, 8], F32)
     _b("y" + _h + "f", [128, 16, 4, 8], F32)
     _b("yp" + _h, [128, 16, 4, 3], F32)
     _b("e" + _h, [128, 16, 4, 8], F16)
@@ -155,9 +161,9 @@ SEMAPHORES = ["cV", "cS", "cP", "cG", "lsem", "ar", "as", "ao", "ap"] + ["er%d" 
 WHOLE = np.s_[:]
 BIAS = {"": 300, "mg": 2500}
 CYC, GATH, PEC, WAKE, OV = 0.85, 1.56, 0.44, 130, 35
-JIT, TRIES, SEED, STRETCH = 0.5, 1500, 1, 300
-CASES = ((0.75, 1.1, 0, 160, 0.9), (1.0, 1.0, 0, 130, 1.0), (1.25, 1.0, -15, 100, 1.12))
-WIDE = False
+JIT, TRIES, SEED, STRETCH, MOVES = 0.5, 400, 1, 300, 4000
+CASES = ((0.75, 1.1, 0, 200, 0.92, 0.9), (1.0, 1.0, 0, 130, 1.0, 0.6), (1.25, 1.0, -15, 100, 1.12, 0.4))
+MCH, SCH, LEAD = 48, 32, 2
 LIST = "VS"
 MEMO = {}
 
@@ -175,7 +181,7 @@ def rank_program(g, core, T, topo):
     cache = MEMO.setdefault("cols", {})
     ndma = [0]
     prog = []
-    due, fill, soon = {}, [], []
+    due, fill, soon, behind, first = {}, [], [], {}, [0]
 
     def R(name, idx=WHOLE):
         if name in ALIAS:
@@ -349,6 +355,8 @@ def rank_program(g, core, T, topo):
             data.append(set(S))
             note(W, Lr, i, o["o"], o["i"])
             es = "".join(o["d"])
+            if i in behind:
+                S.add(behind[i])
             if es == "G":
                 S.update(hist.setdefault("G", [])[-1:])
                 hist["G"].append(i)
@@ -403,12 +411,29 @@ def rank_program(g, core, T, topo):
                 order.append((t, len(order), c, eng[c]))
             return [(c, e) for _, _, c, e in sorted(order)]
 
-        def span(order, kg, kp, ov, wake, _):
+        dur, lat, gat = [o["d"] for o in prog], [o["lat"] for o in prog], [o["lab"] for o in prog]
+
+        def span(order, kg, kp, ov, wake, _, kl, link=None):
             t, done, eng = {e: 0.0 for e in "XYGPSV"}, [0.0] * n, [""] * n
-            for c, e in order:
-                eng[c] = e
-                end = max(ready(c, e, done, eng, wake), t[e] if e != "X" else 0.0) + prog[c]["d"][e] * (kg if prog[c]["lab"] else kp if e == "P" else 1) + (ov if e in "VS" else 0)
-                t[e], done[c] = end, end + prog[c]["lat"]
+            last, why, at = {}, [None] * n, [0] * n
+            for k, (c, e) in enumerate(order):
+                eng[c], at[c] = e, k
+                s, by = 0.0, None
+                for j in pre[c]:
+                    x = done[j] if eng[j] == e and (e == "P" or j not in data[c]) else done[j] + wake
+                    if x > s:
+                        s, by = x, j
+                if e != "X" and t[e] > s:
+                    s, by = t[e], last[e]
+                why[c], last[e] = by, c
+                t[e] = end = s + (dur[c][e] * kg if gat[c] else dur[c][e] * kp if e == "P" else dur[c][e] + ov if e in "VS" else dur[c][e])
+                done[c] = end + (lat[c] * kl if e == "X" else lat[c])
+            if link is not None:
+                c = done.index(max(done))
+                while why[c] is not None:
+                    if why[c] not in pre[c]:
+                        link.append((at[why[c]], at[c]))
+                    c = why[c]
             return max(done)
         state = [SEED]
 
@@ -427,6 +452,36 @@ def rank_program(g, core, T, topo):
             cost = sum(span(o, *m) / m[4] for m in CASES)
             if best is None or cost <= best[0]:
                 best, jit, bias = (cost, o), j2, b2
+        for _ in range(MOVES):
+            o, link = list(best[1]), []
+            span(o, *CASES[int(rng() * len(CASES))], link)
+            if not link:
+                break
+            a, b = link[int(rng() * len(link))]
+            x = rng()
+            flex = [k for k in (a, b) if len(prog[o[k][0]]["d"]) == 2]
+            if flex and x < 0.35:
+                k = flex[int(rng() * len(flex))]
+                o[k] = (o[k][0], "V" if o[k][1] == "S" else "S")
+            elif x < 0.7:
+                need, seg = {o[b][0]}, o[a:b + 1]
+                for c, e in reversed(seg):
+                    if c in need:
+                        need.update(pre[c])
+                if o[a][0] in need:
+                    continue
+                o[a:b + 1] = [y for y in seg if y[0] in need] + [y for y in seg if y[0] not in need]
+            else:
+                b = min(n - 1, b + int(rng() * 40))
+                late, seg = {o[a][0]}, o[a:b + 1]
+                for c, e in seg:
+                    if pre[c] & late:
+                        late.add(c)
+                o[a:b + 1] = [y for y in seg if y[0] not in late] + [y for y in seg if y[0] in late]
+            cost = sum(span(o, *m) / m[4] for m in CASES)
+            if cost <= best[0]:
+                best = (cost, o)
+        MEMO["spans"] = [span(best[1], *m) for m in CASES]
         MEMO["span"] = best[0] / len(CASES)
         return best[1]
 
@@ -512,21 +567,20 @@ def rank_program(g, core, T, topo):
     dma("Y", [(R("num", s_[0::16, :]), ("kid", s_[:, :])), (R("num", s_[1::16, :]), ("up", s_[:, :]))])
     dma("Y", [(R("st"), ("s", s_[:, :]))], [R("cf")], 5000)
     ms(R("pka"), 0.0)
-    zc = R("pka", s_[:, 15::16, :])
-    ms(zc, 8192.0)
-    sel(zc, zc, [[-16, 9], [-4, 4]], GE, 0.0, 0, 1)
-    sel(zc, zc, [[16, 9], [4, 4]], GE, 0.0, 3, -1)
+    for j in range(4):
+        zc = R("pka", s_[:, 12 + j::16, :])
+        sel(zc, zc, [[-16, 9], [-4, 4]], NE, 8192.0, -j, 1)
     iota(R("koff"), [[2048, 4], [0, 24]], 0, 0)
     send("av0", [(nxt(3), "av3")], "ar", 14000)
     send("av0", [(nxt(h), "av%d" % h) for h in (1, 2)], "as", 20000)
     for n, x in (("n1", -1.0), ("n2048", -2048.0), ("p2048", 2048.0), ("p4", 4.0), ("n4", -4.0), ("p128", 128.0), ("p2", 2.0), ("n2", -2.0), ("n128", -128.0)):
-        ts(R(n), R("p1"), x, MUL)
+        aff(R(n), R("p1"), x, 0.0)
     for t in range(4):
         ms(R("ct", s_[:, :, :, t]), 0.375 - 0.25 * t)
     ms(R("on"), 1.0)
     ts(R("kmk"), R("kidi"), 0.0, LT, -256.0, MUL)
     dma("S", [(R("km8", s_[0:8, :]), R("kmk"))])
-    cp(R("ib"), R("p1"), "V")
+    cp(R("ib"), R("p1"))
     ms(R("g8i"), 1.0)
     sel(R("g8i"), R("g8i"), [[1, 128]], GE, 0.0, 0, -16)
     sel(R("g8i"), R("g8i"), [[-1, 128]], GE, 0.0, 15, 16)
@@ -536,36 +590,46 @@ def rank_program(g, core, T, topo):
     sel(R("w", s_[:, :, 7]), R("w", s_[:, :, 7]), [[-8, 8]], NE, 4.0, -2, 1)
     iota(R("bd0"), [[0, 3072]], 0, 0)
     dma("Y", [(R("bd0", s_[16 * gg:16 * gg + 16, gg, :]), ("a", s_[16 * gg:16 * gg + 16, :])) for gg in range(8)])
-    cp(R("keep"), R("p1"), "V")
+    cp(R("keep"), R("p1"))
+    cp(R("i32"), R("p1"))
     ms(R("keep", s_[:, :, AK:P + 1:P - AK]), 0.0)
 
-    def dist(ak, ow):
+    def dist(ak, ow, via):
         for k in range(4):
             c = s_[:, 384 * k:384 * k + 384]
-            tt(R("dif", c), IND(R(ak, s_[:, 0:384]), R("lku", s_[:, 24 * k:24 * k + 24])), R("av0"), SUB)
-            op([R("absd", c)], [R("dif", c)], {"S": lambda c=c: g.scalar.activation(ap(R("absd", c)), ap(R("dif", c)), ACT.Abs)})
+            i, d = IND(R(ak, s_[:, 0:384]), R("lku", s_[:, 24 * k:24 * k + 24])), R("dif", c)
+            if k in via:
+                cp(d, i, "S")
+                pe([(R(via[k], s_[:, 0:12]), R("p1"), d), (R(via[k], s_[:, 0:12]), R("n1"), R("a16"))])
+                d = R(via[k], s_[:, 0:12])
+            else:
+                tt(d, i, R("av0"), SUB)
+            op([R("absd", c)], [d], {"S": lambda c=c, d=d: g.scalar.activation(ap(R("absd", c)), ap(d), ACT.Abs)})
+        pe([(R("X2", s_[:, 0:24]), ST("st", 3 - j), R("absd", s_[:, j::4])) for j in range(4)])
+        cp(R("qs"), R("X2", s_[:, 0:24]))
         for q in range(4):
-            pe([(R("X2", s_[:, q::4, 0:12]), ST("z%d" % q, 15 - r), R("absd", s_[:, r::16])) for r in range(16)])
+            for j in (0, 1):
+                pe([(R("X2", s_[:, 2 * q + j::8, 0:12]), ST("z%d" % q, 12 - 4 * i), R("qs", s_[:, :, j, :, i])) for i in range(4)])
         dk = lambda a, b: R("X2", s_[:, a:b, 0:12])
-        tt(R("yd"), dk(0, 16), R("kw", s_[:, 0:16]), ADD)
-        tt(dk(16, 32), dk(16, 32), R("kw", s_[:, 16:32]), ADD)
+        tt(R("yd"), dk(0, 16), R("kw", s_[:, 0:2]), ADD)
+        tt(dk(16, 32), dk(16, 32), R("kw", s_[:, 2:4]), ADD)
         tt(dk(0, 8), dk(16, 24), R("yd", s_[:, 0:8]), MIN)
         tt(R("yd2"), dk(24, 32), R("yd", s_[:, 8:16]), MIN)
         tt(R("oi"), dk(0, 8), R("yd2"), MIN)
         ts(R("oj"), R("oi"), 2047, AND)
-        cp(R(ow), R("oj"), "V")
+        cp(R(ow, s_[:, 0:64]), R("oj", s_[:, :, 0:16]), "V")
+        cp(R(ow, s_[:, 64:96]), R("oj", s_[:, :, 16:24]), "V")
 
     cp(R("lku"), R("lki"), "V")
-    ts(R("yd2"), R("lki"), 192.0, GE, 576.0, MUL)
     tt(R("lkf"), R("lki"), R("koff"), ADD)
-    tt(R("lkf"), R("lkf"), R("yd2"), ADD)
     for q in range(4):
-        aff(R("kw", s_[:, q::4, :]), R("lkf"), 1.0, 192.0 * q)
-    dist("ak0", "own0")
+        aff(R("kw", s_[:, :, q, :]), R("lkf"), 1.0, 384.0 * q)
+    cp(R("a16"), R("av0"))
+    dist("ak0", "own0", {k: ("Oa", "Ob")[k % 2] for k in VIA})
 
-    for i in soon:
-        due[i] = len(prog)
-    aff(R("hf"), R("cf"), 0.5, 1023.75, "V")
+    while soon:
+        due[soon.pop()] = len(prog)
+    aff(R("hf"), R("cuti"), 0.5, 1023.75, "S")
     half = lambda n, H, k: R(n, s_[P96, :, 2 * H:2 * H + 2, :, k])
     for H, (be, bk) in enumerate((("D0", "K"), ("D1", "PR"))):
         x = str(H)
@@ -576,7 +640,7 @@ def rank_program(g, core, T, topo):
         pe_open([(slot(bk, t), I("n2048"), slot("e" + x, j)) for j, tu in enumerate(PAIRS) for t in tu], False, True)
         y = lambda k: slot("y" + x + "f", k)
         k_ = lambda k: slot(bk, k)
-        cp(y(s_[0:2]), k_(s_[1:4:2]), "V")
+        cp(y(s_[0:2]), k_(s_[1:4:2]))
         tt(k_(4), k_(0), y(0), MIN)
         tt(k_(5), k_(0), y(0), MAX)
         tt(y(2), k_(2), y(1), MIN)
@@ -590,10 +654,10 @@ def rank_program(g, core, T, topo):
         ts(half("ns", H, s_[0:4]), k_(s_[0:4]), 12582912.0, ADD, -12582912.0, ADD)
         ts(half("fl", H, s_[0:2]), half("ns", H, s_[0:4:2]), 0.0, LT)
         tt(half("fr", H, s_[0:4]), k_(s_[0:4]), half("ns", H, s_[0:4]), SUB)
-        aff(slot("e" + x, s_[6:8]), half("ns", H, s_[2:4]), 0.5, 1023.75, "V")
+        aff(slot("e" + x, s_[6:8]), half("ns", H, s_[2:4]), 0.5, 1023.75)
     for i, (role, f) in enumerate(((0, 0), (2, 1), (3, 1))):
         pe([(R("X1", s_[:, 48 * i:48 * i + 48, :]), R("ns", s_[P96, :, :, :, role]), I("p1")), (R("X1", s_[:, 48 * i:48 * i + 48, :]), R("fl", s_[P96, :, :, :, f]), I("p2048"))])
-    cp(R("il"), R("X1", s_[:, 0:144, :]), "V")
+    cp(R("il"), R("X1", s_[:, 0:144, :]))
     for i in range(3):
         for j in (0, 1):
             cp(R("mg", s_[:, 1536 * i + 768 * j:1536 * i + 768 * j + 768]), IND(R("num", s_[:, 0:2048]), R("il", s_[:, 96 * i + 48 * j:96 * i + 48 * j + 48])), "VS"[j])
@@ -629,47 +693,57 @@ def rank_program(g, core, T, topo):
         for b, f0 in ((b1, 0), (b2, 8)):
             pe([(fslot(b, f - f0), I(m), src) for f in range(f0, f0 + 8) for m, src in sums[f]])
             cp(R("rt0", s_[P96, H, :, f0:f0 + 8, :]), R(b, s_[P96]))
-    for H in (0, 1):
-        for j in (0, 1):
-            bk = (("Oa", "K"), ("Ob", "PR"))[H][j]
-            pe([(R(bk, s_[:, 6 * i + 3 * r:6 * i + 3 * r + 3]), R("rt0", s_[P96, H, :, :, 4 * r + 2 * j + i]), I("p1")) for i in (0, 1) for r in (0, 1)], False)
-            cp(R("rec", s_[:, 768 * H + 384 * j:768 * H + 384 * j + 384]), R(bk, s_[:, 0:12]))
+    for q, bk in enumerate(("D0", "Oa", "K", "D1")):
+        pe([(R(bk, s_[:, 3 * r:3 * r + 3]), R("rt0", s_[P96, r // 2, :, :, 4 * (r % 2) + q]), I("p1")) for r in range(4)], False)
+        cp(R("rec", s_[:, 384 * q:384 * q + 384]), R(bk, s_[:, 0:12]))
     dma("Y", [(R("mt"), ("m", s_[:, :]))], [R("rec")], 6000)
     for i, bk in enumerate(("X1", "K", "PR", "X2")):
         c = s_[:, 512 * i:512 * i + 512]
         pe([(R(bk), R("ib"), R("st", c)), (R(bk), R("g8i", s_[0:8, :]), R("km8", s_[0:8, 512 * i:512 * i + 512]))])
         relu(R("sm", c), R(bk))
     ms(R("sm", s_[:, 1:2]), 255.0)
-    for n in ("xw0", "xw1"):
-        iota(R(n, s_[:, 0::2, :, 3:9]), [[0, 432]], 0, 0)
-        iota(R(n, s_[:, 0::2, :, 20:23]), [[0, 216]], 0, 0)
+    iota(R("xw0", s_[:, 0::2, :, 3:9]), [[0, 432]], 0, 0)
+    iota(R("xw0", s_[:, 0::2, :, 20:23]), [[0, 216]], 0, 0)
+    iota(R("xw1", s_[:, :, :, 3:9]), [[0, 840]], 0, 0)
+    iota(R("xw1", s_[:, :, :, 20:23]), [[0, 420]], 0, 0)
     iota(R("rt", s_[:, :, :, 0:8, :]), [[0, 1024]], 0, 0)
     iota(R("md", s_[:, :, :, 0:2, :]), [[0, 256]], 0, 0)
     iota(R("bd1"), [[0, 3072]], 0, 0)
-    cp(R("mr32"), R("pkc", s_[:, :, OFF["mr"][1]]))
     iota(R("pi", s_[:, 0:1]), [[0, 1]], 0, 1)
     ts(R("pi", s_[:, 1:2]), R("pi", s_[:, 0:1]), 3, AND)
     ts(R("pc"), R("pi", s_[:, 1:2]), -2048.0, MUL)
 
     def front(h, H):
         x, G = str(H), "g" + "ab"[h % 2] + str(H)
-        cp(R(G), IND(R("rec", s_[:, 0:1536]), R("own%d" % h, s_[:, 48 * H:48 * H + 48])))
+        n = NV[H]
+        for a in range(0, 4 * n, 512):
+            cp(R(G, s_[:, a:a + 512]), IND(R("rec", s_[:, 0:1536]), R("own%d" % h, s_[:, 64 * H + a // 16:64 * H + a // 16 + 32])))
         for q2 in (0, 1):
-            pe([(R("X1", s_[:, 0:192, q2]), ST("mix", 8 - 8 * b), R(G, s_[:, 384 * q2 + 192 * b:384 * q2 + 192 * b + 192])) for b in (0, 1)])
-        cp(R("sl" + x), R("X1", s_[:, 0:192, :]), LIST)
-        for c in (0, 4, 1, 5, 2, 6, 3, 7):
-            cp(R("sg" + x, s_[:, 768 * c:768 * c + 768]), IND(R("sm", s_[:, 0:2048]), R("sl" + x, s_[:, 48 * c:48 * c + 48])))
+            pe([(R("X1", s_[:, 0:n, q2]), ST("mix", 8 - 8 * b), R(G, s_[:, n * (2 * q2 + b):n * (2 * q2 + b + 1)])) for b in (0, 1)])
+        for a, b in ((0, 2 * SCH), (2 * SCH, n)) if H == 0 else ((0, n),):
+            cp(R("sl" + x, s_[:, 2 * a:2 * b]), R("X1", s_[:, a:b, :]), LIST)
+        for v in chunks(H):
+            if H == 0:
+                first[0] = len(prog) - LEAD
+            else:
+                behind[len(prog)] = first[0]
+            cp(R("sg" + x, s_[:, 32 * v:32 * (v + SCH)]), IND(R("sm", s_[:, 0:2048]), R("sl" + x, s_[:, 2 * v:2 * (v + SCH)])))
 
-    def picks(b, name, G, k=slice(0, 8)):
-        return [(R(b, s_[P96, r::2, q, k]), R(G, s_[:, 192 * q + 96 * r:192 * q + 96 * r + 96]), PK(name, k.start, k.stop - k.start)) for r in (0, 1) for q in range(4)]
+    def chunks(H):
+        return sorted(range(0, NV[H], SCH), key=lambda v: (v % 128 >= 64, v))
+
+    def picks(b, name, G, H):
+        return [(R(b, s_[:, r::2, q, :]), R(G, s_[:, NV[H] * q + 128 * r:NV[H] * q + 128 * r + 128]), PK(name, 0, 8)) for r in range(2 - H) for q in range(4)]
 
     R1, Y4, YM, N2, HD = 0, 1, 2, 3, 4
-    xt = lambda H, k: R("xw" + str(H), s_[P96, 1:17:2, :, k])
+    KB = ("K", "Oa")
+    xt = lambda H, k: R("xw0", s_[:, 1:17:2, :, k]) if H == 0 else R("xw1", s_[:, 3:35:4, :, k])
+    slots = lambda H: lambda b, k: R(b, s_[:, 0::1 + H, :, k])
 
     def prelim(h, H):
-        x, G = str(H), "g" + "ab"[h % 2] + str(H)
+        x, G, slot = str(H), "g" + "ab"[h % 2] + str(H), slots(H)
         e = lambda k: slot("e" + x, k)
-        pe(picks("PR", "pr", G), False)
+        pe(picks("PR", "pr", G, H), False)
         cp(slot("yp" + x, s_[0:2]), slot("PR", s_[0:2]))
         relu(e(s_[0:2]), slot("PR", s_[4:6]))
         aff(e(HD), slot("PR", 6), 0.5, 1023.75)
@@ -679,32 +753,30 @@ def rank_program(g, core, T, topo):
         relu(e(N2), e(YM), -1.0)
 
     def errs(h, H):
-        x, G, bd = str(H), "g" + "ab"[h % 2] + str(H), "bd%d" % (h % 2)
+        x, G, bd, slot, I = str(H), "g" + "ab"[h % 2] + str(H), "bd%d" % (h % 2), slots(H), R
         e = lambda k: slot("e" + x, k)
-        for c in (0, 4, 1, 5, 2, 6, 3, 7) if not WIDE else ():
+        for c in chunks(H):
             lst = []
-            for v in range(24 * c, 24 * c + 24):
-                r, uu = v // 96, v % 96
-                lst.append((R("Oa" if uu < 64 else "Ob", s_[32 * r:32 * r + 32, uu % 64 // 4, uu % 4, :]), R("sg" + x, s_[:, 32 * v:32 * v + 32]), R(bd, s_[:, :, 192 * H + v])))
+            for v in range(c, c + SCH):
+                if H and v < 64:
+                    o = R("X1", s_[0:32, 4 * v:4 * v + 4, :])
+                else:
+                    o = R(("Oa", "Ob")[v % 128 // 64], s_[32 * (v // 128):32 * (v // 128) + 32, v % 64 // 4, v % 4, :])
+                lst.append((o, R("sg" + x, s_[:, 32 * v:32 * v + 32]), R(bd, s_[:, :, 256 * H + v])))
             pe(lst, False)
-        if not WIDE:
-            cp(R("os" + x, s_[0:64, 0:16]), R("Oa", s_[0:64]))
-            cp(R("os" + x, s_[0:64, 16:24]), R("Ob", s_[0:64, 0:8]))
-        for c in range(4 if WIDE else 0):
-            bk, r = ("Oa", "Ob")[c % 2], c // 2
-            for j in (0, 6):
-                pe([(R(bk, s_[:, y]), R("sg" + x, s_[:, 1536 * c + 128 * y:1536 * c + 128 * y + 128]), R(bd, s_[:, :, 192 * H + 48 * c + 4 * y:192 * H + 48 * c + 4 * y + 4]))
-                    for y in range(j, j + 6)], False)
-            for i in range(4):
-                cp(R("os" + x, s_[32 * r:32 * r + 32, 12 * (c % 2):12 * (c % 2) + 12, i, :]), R(bk, s_[32 * i:32 * i + 32, 0:12, :, i::4]))
-        pe_open(picks("K", "kb", G) + [(slot("K", k), I(m), e(j)) for k, m, j in ((1, "p1", Y4), (2, "p1", R1), (4, "n1", Y4), (4, "n1", YM))], True, False)
-        pe_open([(R("K", s_[P96, 2 * gg:2 * gg + 2]), R("os" + x, s_[0:64, :, :, gg]), R("w", s_[0:64])) for gg in range(8)], False, True)
-        pe(picks("D0", "d0", G) + [(slot("D0", k), I(m), e(j)) for k, m, j in ((2, "n1", R1), (3, "p2", HD))])
-        pe(picks("D1", "d1", G) + [(slot("D1", k), I(m), e(j)) for k, m, j in ((3, "p1", R1), (4, "p1", Y4), (4, "p1", YM), (4, "n1", N2), (5, "p1", N2), (7, "n2", Y4), (7, "n1", YM))])
+        for j, bk in enumerate((("Oa", "Ob"), ("X1", "Ob"))[H]):
+            cp(R("os" + x, s_[0:64 >> H, 16 * j:16 * j + 16]), R(bk, s_[0:64 >> H]))
+        pe_open(picks(KB[H], "kb", G, H) + [(slot(KB[H], k), I(m), e(j)) for k, m, j in ((1, "p1", Y4), (2, "p1", R1), (4, "n1", Y4), (4, "n1", YM))], True, False)
+        if H == 0:
+            pe_open([(R("K", s_[:, 2 * gg:2 * gg + 2]), R("os0", s_[0:64, :, :, gg]), R("w", s_[0:64])) for gg in range(8)], False, True)
+        else:
+            pe_open([(R("Oa", s_[:, 2 * gg]), R("os1", s_[0:32, :, :, gg]), R("w", s_[0:32, 0:4])) for gg in range(8)], False, True)
+        pe(picks("D0", "d0", G, H) + [(slot("D0", k), I(m), e(j)) for k, m, j in ((2, "n1", R1), (3, "p2", HD))])
+        pe(picks("D1", "d1", G, H) + [(slot("D1", k), I(m), e(j)) for k, m, j in ((3, "p1", R1), (4, "p1", Y4), (4, "p1", YM), (4, "n1", N2), (5, "p1", N2), (7, "n2", Y4), (7, "n1", YM))])
 
     def logic(h, H):
-        x, G = str(H), "g" + "ab"[h % 2] + str(H)
-        k, y, u = (lambda j: slot("K", j)), (lambda j: slot("y" + x + "f", j)), (lambda j: xt(H, j))
+        x, slot = str(H), slots(H)
+        k, y, u = (lambda j: slot(KB[H], j)), (lambda j: slot("y" + x + "f", j)), (lambda j: xt(H, j))
         tau, mu, g2, w, eC, eDs = [u(j) for j in range(6)]
         cp(y(s_[0:2]), k(s_[3:5]))
         relu(y(3), k(5))
@@ -721,7 +793,7 @@ def rank_program(g, core, T, topo):
         tt(eC, k(5), tau, MUL)
         tt(eDs, k(0), tau, MUL)
         prod = lambda o, n, b, j, m: tt(u(s_[o:o + n]), slot(b, j), u(s_[m:m + n]), MUL)
-        add = lambda terms, first, last: pe_open([(fslot("PR", f - C), I(m), u(j)) for f, m, j in terms], first, last)
+        add = lambda terms, first, last: pe_open([(R("PR", s_[:, (f - C) // 4::2, f % 4, 0:8 - 4 * H]), R(m), u(j)) for f, m, j in terms], first, last)
         tt(g2, k(4), eC, MUL)
         prod(22, 2, "D1", s_[0:7:6], 4)
         tt(mu, k(3), g2, ADD)
@@ -736,57 +808,69 @@ def rank_program(g, core, T, topo):
         for j in (2, 4, 6):
             prod(7 + j, 2, "D0", s_[j:j + 2], 0)
         add([(BB, "p1", 9), (L, "p1", 10), (F, "n128", 11), (C, "p1", 12), (BA, "p1", 13), (Q, "p1", 14)], False, True)
-        cp(R("rt", s_[P96, H, :, 8:16, :]), R("PR", s_[P96]))
-        for r in range(2 if h == 3 else 0):
-            cp(R("md", s_[P96, 2 * H + r, :, 2:4, :]), R("PR", s_[P96, 0::2, 0:2, 4 * r:4 * r + 4]))
+        cp(R("rt", s_[:, H, :, 8:16, 0:8 - 4 * H]), R("PR", s_[:, :, :, 0:8 - 4 * H]))
+        for r in range(2 - H if h == 3 else 0):
+            cp(R("md", s_[:, 2 * H + r, :, 2:4, :]), R("PR", s_[:, 0::2, 0:2, 4 * r:4 * r + 4]))
 
     def back(h, H):
-        G, lk = "g" + "ab"[h % 2] + str(H), "lk" + str(H)
-        pe([(R("X1", s_[:, 0:24, :]), R("xw" + str(H), s_[P96, 1 - b:17 - b, :, k]), R("n1" if k == 20 else "p1", s_[P96, 0:24, b::2])) for k in (6, 22, 3, 7, 8, 20) for b in (0, 1)])
+        G, lk, n, nb = "g" + "ab"[h % 2] + str(H), "lk" + str(H), NV[H], 2 + 2 * H
+        for ks in ((6,), (22,), (7, 8), (3, 20)):
+            pe_open([(R("X1", s_[:, 0:n // 8, :]), R("xw" + str(H), s_[:, nb - 1 - b:8 * nb + nb - 1 - b, :, k]), R("n1" if k == 20 else "p1", s_[:, :, b::nb]))
+                     for k in ks for b in range(nb)], ks[0] == 6, ks[0] == 3)
         while fill and H:
             due[fill.pop()] = len(prog)
-        cp(R("xl", s_[:, 48 * H:48 * H + 48]), R("X1", s_[:, 0:24, :]), LIST)
+        cp(R("xl", s_[:, 64 * H:64 * H + n // 4]), R("X1", s_[:, 0:n // 8, :]), LIST)
         for j in (0, 1):
-            cp(R(lk, s_[:, 384 * j:384 * j + 384]), IND(R("num", s_[:, 0:2048]), R("xl", s_[:, 48 * H + 24 * j:48 * H + 24 * j + 24])))
-        for j, bk in enumerate(("Oa", "Ob")):
-            o = lambda q, r, c: R(bk, s_[:, 6 * (q % 2) + 3 * r:6 * (q % 2) + 3 * r + 3, :, c])
-            pe_open([(R(bk, s_[:, 0:12]), R("keep"), R(G, s_[:, 384 * j:384 * j + 384]))], True, False)
-            pe_open([(o(q, r, WHOLE), R("rt", s_[P96, H, :, :, 4 * r + q]), I("p1")) for q in (2 * j, 2 * j + 1) for r in (0, 1)], False, False)
-            pe_open([(o(q, r, s_[b::2]), ST("sel", 0), R(lk, s_[:, 8 * b + 4 * r + q::16])) for q in (2 * j, 2 * j + 1) for r in (0, 1) for b in (0, 1)], False, True)
-            cp(R("r16", s_[:, 2 * j:2 * j + 2, 192 * H:192 * H + 192]) if h == 3 else R("rec", s_[:, 768 * H + 384 * j:768 * H + 384 * j + 384]), R(bk, s_[:, 0:12]))
+            cp(R(lk, s_[:, 2 * n * j:2 * n * j + 2 * n]), IND(R("num", s_[:, 0:2048]), R("xl", s_[:, 64 * H + n // 8 * j:64 * H + n // 8 * (j + 1)])))
+        for bk, qs in ((("Ob", (0, 1)), ("K", (2, 3))), (("Oa", (0, 1)), ("D1", (2, 3))))[H]:
+            a = n // 32
+            o = lambda q, r: R(bk, s_[:, a * (q % 2) + 4 * r:a * (q % 2) + 4 * r + 4])
+            pe_open([(R(bk, s_[:, 0:2 * a]), R("keep"), R(G, s_[:, n * qs[0]:n * qs[0] + 2 * n]))], True, False)
+            pe_open([(o(q, r), R("rt", s_[:, H, :, :, 4 * r + q]), R("p1")) for q in qs for r in range(2 - H)], False, False)
+            pe_open([(o(q, r), ST("sel", 0), R(lk, s_[:, 4 * r + q::8 - 4 * H])) for q in qs for r in range(2 - H)], False, True)
+            if h == 3:
+                cp(R("r16", s_[:, qs[0]:qs[0] + 2, 256 * H:256 * H + n]), R(bk, s_[:, 0:2 * a]))
+            for q in qs if h < 3 else ():
+                cp(R("rec", s_[:, 384 * q + 256 * H:384 * q + 256 * H + n]), R(bk, s_[:, a * (q % 2):a * (q % 2) + a]))
 
     def msum(h):
         G, lk, av = "g" + "ab"[h % 2], "lk%d" % (h % 2), "av%d" % h
-        col = lambda r, q: 768 * (r // 2) + 192 * q + 96 * (r % 2)
-        mg = lambda c: R("mg", s_[:, 768 * c:768 * c + 768])
-        ind = lambda c: IND(R("mt", s_[:, 0:2048]), R("mu", s_[:, 48 * c:48 * c + 48]))
         if h < 3:
+            sel(R("r16"), R("rec"), [[0, 1536]], EQ, 0.0, 0, 0)
             for q in range(4):
-                pe([(R("X2", s_[:, 6 * q:6 * q + 6]), R("mr32", s_[:, 12 - 4 * r:140 - 4 * r]), R("rec", s_[:, col(r, q):col(r, q) + 96])) for r in range(4)])
-            cp(R("mu"), R("X2", s_[:, 0:24]), LIST)
-            for c in range(8):
-                fill.append(len(prog))
-                if c // 2 in CHAIN:
-                    tt(mg(c), ind(c), mg(c - 2), ADD)
-                else:
-                    cp(mg(c), ind(c))
+                pe([(R("X2", s_[:, 6 * q:6 * q + 6]), ST("mr", 12 - 4 * r), R("r16", s_[:, q, 96 * r:96 * r + 96])) for r in range(4)])
+            mu, mb = ("mu", "mu0")[h == 0], ("mg", "mg0")[h == 0]
+            soon.append(len(prog))
+            cp(R(mu), R("X2", s_[:, 0:24]), LIST)
+            for q in range(4):
+                for a in range(96 * q, 96 * q + 96, MCH):
+                    if h:
+                        fill.append(len(prog))
+                    o, i = R(mb, s_[:, 16 * a:16 * (a + MCH)]), IND(R("mt", s_[:, 0:2048]), R(mu, s_[:, a:a + MCH]))
+                    if q in CHAIN and h:
+                        tt(o, i, R(mb, s_[:, 16 * (a - 96):16 * (a + MCH - 96)]), ADD)
+                    else:
+                        cp(o, i)
+            if h == 0:
+                return
             for r in range(4):
                 pe([(R("X2", s_[:, 6 * r:6 * r + 6]), R("p1"), R("mg", s_[:, 1536 * q + 4 * r + t:1536 * q + 1536:16])) for q in range(4) if q + 1 not in CHAIN for t in range(4)])
-            tt(R("ef%d" % h), R("X2", s_[:, 0:24]), R(av), MUL)
-            if h:
-                send("ef%d" % h, [(nxt(-h), "el%d" % h)], "er%d" % h, 9000)
+            cp(R("ef%d" % h), R("X2", s_[:, 0:24]))
+            send("ef%d" % h, [(nxt(-h), "el%d" % h)], "er%d" % h, 9000)
             return
         for H in (0, 1):
-            c, n = s_[:, 192 * H:192 * H + 192], "3" + "ab"[H]
-            pe_open([(R("X2", s_[:, 0:12]), ST("mg", 3 - q), R(G + str(H), s_[:, 192 * q:192 * q + 192])) for q in range(4)], True, False)
-            pe_open([(R("X2", s_[:, 6 * r:6 * r + 6]), R("md", s_[P96, 2 * H + r]), I("p1")) for r in (0, 1)], False, False)
-            pe_open([(R("X2", s_[:, 6 * r:6 * r + 6, b::2]), ST("ml", 3 - q), R("lk" + str(H), s_[:, 8 * b + 4 * r + q::16])) for r in (0, 1) for q in range(4) for b in (0, 1)], False, True)
-            cp(R("mu", c), R("X2", s_[:, 0:12]), LIST)
-            for j in range(4 * H, 4 * H + 4):
-                cp(mg(j), ind(j), "VS"[j % 2] if H else "VS")
-            for r in (0, 1):
-                pe([(R("X2", s_[:, 12 + 6 * r:18 + 6 * r]), R("p1"), R("mg", s_[:, 3072 * H + 1536 * r + t:3072 * H + 1536 * r + 1536:16])) for t in range(16)])
-            tt(R("ef" + n), R("X2", s_[:, 12:24]), R(av, c), MUL)
+            nv = NV[H]
+            c, n = s_[:, 256 * H:256 * H + nv], "3" + "ab"[H]
+            pe_open([(R("X2", s_[:, 0:nv // 16]), ST("mg", 3 - q), R(G + str(H), s_[:, nv * q:nv * q + nv])) for q in range(4)], True, False)
+            pe_open([(R("X2", s_[:, 8 * r:8 * r + 8]), R("md", s_[:, 2 * H + r]), R("p1")) for r in range(2 - H)], False, False)
+            pe_open([(R("X2", s_[:, 8 * r:8 * r + 8]), ST("ml", 3 - q), R("lk" + str(H), s_[:, 4 * r + q::8 - 4 * H])) for r in range(2 - H) for q in range(4)], False, True)
+            cp(R("mu", c), R("X2", s_[:, 0:nv // 16]), LIST)
+            for a in range(256 * H, 256 * H + nv, 64):
+                cp(R("mg", s_[:, 16 * a:16 * a + 1024]), IND(R("mt", s_[:, 0:2048]), R("mu", s_[:, a:a + 64])), "VS"[a // 64 % 2] if H else "VS")
+            for a in range(0, nv, 128 >> H):
+                b = 16 * (256 * H + a)
+                pe([(R("X2", s_[:, 16 + a // 16:16 + (a + (128 >> H)) // 16]), R("p1"), R("mg", s_[:, b + t:b + (2048 >> H):16])) for t in range(16)])
+            tt(R("ef" + n), R("X2", s_[:, 16:16 + nv // 16]), R(av, c), MUL)
             send("ef" + n, [(nxt(-h), "el" + n)], "er%d" % (3 + H), 6000)
 
     def cut_out():
@@ -805,7 +889,7 @@ def rank_program(g, core, T, topo):
         for H in (0, 1):
             front(h, H)
         if h == 0:
-            dist("av3", "ownx")
+            dist("av3", "ownx", {})
             send("ownx", [(nxt(1), "own1")], "ao", 8000)
             send("ownx", [(nxt(j), "own%d" % j) for j in (2, 3)], "ap", 12000)
         else:
@@ -815,17 +899,23 @@ def rank_program(g, core, T, topo):
         for H in (0, 1):
             prelim(h, H)
         errs(h, 0)
+        while soon:
+            due[soon.pop()] = len(prog)
         logic(h, 0)
         errs(h, 1)
         back(h, 0)
         logic(h, 1)
         back(h, 1)
-    tt(R("ef0"), R("ef0"), R("el1"), ADD)
-    tt(R("ef0"), R("ef0"), R("el2"), ADD)
     msum(3)
     cut_out()
     for H in (0, 1):
-        c = s_[:, 192 * H:192 * H + 192]
+        c, bk = s_[:, 192 * H:192 * H + 192], "D%d" % H
+        pe_open([(R(bk, s_[:, 0:6]), R("i32"), R(n, c)) for n in ("el1", "el2")], True, False)
+        for q in range(4):
+            pe_open([(R(bk, s_[:, 3 * r:3 * r + 3]), R("p1"), R("mg0", s_[:, 1536 * q + 8 * H + 4 * r + t:1536 * q + 1536:16])) for r in (0, 1) for t in range(4)], False, q == 3)
+        tt(R("ef0", c), R(bk, s_[:, 0:6]), R("av0", c), MUL)
+    for H in (0, 1):
+        c = s_[:, 256 * H:256 * H + NV[H]]
         tt(R("yes", c), R("ef0", c), R("el3" + "ab"[H]), ADD)
         dma("Y", [(("ye", c), R("yes", c))])
     if "order" not in MEMO:

import numpy as np
from concourse.bass import DstId, RemoteDMATransfer
from concourse.mybir import AluOpType, ActivationFunctionType
ADD, SUB, MUL, MAX, MIN = AluOpType.add, AluOpType.subtract, AluOpType.mult, AluOpType.max, AluOpType.min
EQ, NE, GT, LT, GE, AND = AluOpType.is_equal, AluOpType.not_equal, AluOpType.is_gt, AluOpType.is_lt, AluOpType.is_ge, AluOpType.bitwise_and
ACT = ActivationFunctionType
F32, F16, BF, I32, U16 = "float32", "float16", "bfloat16", "int32", "uint16"
N = 4
BIG = float(2 ** 22)
AK, A0, B0, V, U, P, U2, C, D, L, Q, F, BA, BB, BC = 0, 1, 2, 3, 4, 5, 6, 8, 9, 10, 11, 12, 13, 14, 15


def lin(*terms):
    c = np.zeros(16)
    for k, x in terms:
        c += k * x
    return c


def fld(f):
    return np.eye(16)[f]


ONE, FCD, FS = fld(U) / 128, fld(F) / 128, (fld(V) - fld(F)) / 128
nA, nB, nC, nD, nP, nQ, nL = fld(AK) + fld(A0), fld(AK) + fld(B0), fld(C), fld(D), fld(P), fld(Q), fld(L)
bA, bB, bC = fld(BA), fld(BB), fld(BC)
bD = 6 * ONE - bA - bB - bC
Z = np.zeros(16)
COLS, OFF = {"a": [], "b": [], "c": []}, {}


def mat(name, cols, buf="b"):
    OFF[name] = (buf, len(COLS[buf]))
    if buf == "b":
        COLS[buf].extend(cols)
    else:
        COLS[buf].append([Z] * (16 - len(cols)) + cols)


for _q in range(4):
    mat("z%d" % _q, [8192.0 * (np.arange(16) // 4 == _q)], "a")
PAIRS = ((0, 1), (1, 2), (2, 3), (0, 2), (1, 3), (0, 3))
mat("sel", [fld(f) * (f in (AK, P)) for f in range(16)], "c")
mat("kb", [bA - bD, bC - 4 * FCD - bD, bB - bD + BIG * (fld(U2) / 128 - FS), bB - bD, bA + bB - 2 * bD + 4 * FCD, bC - bD, 3.5 * ONE - bD + BIG * FS, 3.5 * ONE - bD])
mat("pr", [bC - bD - 8 * (ONE - FCD), BIG * (FS - ONE), bA - bD - 8 * FCD, bB - bD - 8 * FCD, bA - bB, bA - bC - 4 * ONE + 8 * FCD, nD, nP])
mat("d0", [nD - nP, nL - nP, bA - bB, -2048 * ONE - nL, FCD - FS, nQ - nC, bD - bA, nP - nQ])
mat("d1", [nC - nD, nL + ONE - nD, bC - bD, bB - bC, 2 * bD - bA - bB - 4 * FCD, Z, nC - nP, bA + bB - bD - bC + 8 * FCD])
mat("mix", [nA, nL, nP, nB, nL + ONE, nC, nQ, nD], "c")
mat("mg", [x for role in (fld(A0), fld(B0), nC, nD) for x in (Z, Z, Z, role)], "c")
mat("ml", [x for role in (fld(AK), fld(AK), Z, Z) for x in (Z, Z, Z, role)], "c")
mat("mr", [nA, nB, nC, nD], "c")
mat("my", [nA + 2048 * bA, nB + 2048 * bB, nC + 2048 * bC, nD + 2048 * bD], "c")
mat("st", [(np.arange(16) // 4 == j // 4) * (j % 4 == 3) * 1.0 for j in range(16)], "c")
NM = {b: len(COLS[b]) for b in "ac"}
for _b_ in "ac":
    COLS[_b_] = [m[j] for j in range(16) for m in COLS[_b_]]
TAB = {b: np.stack(COLS[b], axis=1) for b in COLS}


def paints(buf):
    out, KC = [], len(COLS[buf])
    for a in range(4):
        t = TAB[buf][4 * a:4 * a + 4].copy()
        while t.any():
            b, c = [int(x[0]) for x in np.nonzero(t)]
            x, best = t[b, c], None
            for rs in (1, 2, 3):
                rows = [b]
                while rows[-1] + rs < 4 and t[rows[-1] + rs, c] == x:
                    rows.append(rows[-1] + rs)
                for nr in range(1, len(rows) + 1):
                    ok = np.all(t[rows[:nr]] == x, axis=0)
                    for cs in range(1, KC):
                        n = 1
                        while c + n * cs < KC and ok[c + n * cs]:
                            n += 1
                        if best is None or n * nr > best[0]:
                            best = (n * nr, slice(b, rows[nr - 1] + 1, rs), slice(c, c + (n - 1) * cs + 1, cs))
            out.append((a, best[1], best[2], float(x)))
            t[best[1], best[2]] = 0
    return out


SCRATCH = {}
ALIAS = {}


def _m(buf, names, shape, dtype):
    names = names.split()
    for i, n in enumerate(names):
        ALIAS[n] = (buf, i)
    SCRATCH[buf] = ("sbuf", [128, len(names)] + shape[1:], dtype)


def _b(names, shape, dtype, where="sbuf"):
    for n in names.split():
        SCRATCH[n] = (where, shape, dtype)


_b("Oa Ob K D0 D1 PR", [128, 16, 4, 8], F32, "psum")
_b("X1", [128, 256, 2], F32, "psum")
_b("X2", [128, 32, 16], F32, "psum")
_b("av0 av1 av2 av3 ak0", [128, 384], BF)
_b("own0 own1 own2 own3 ownx lku xl", [128, 96], U16)
_b("lki oi", [128, 96], I32)
_b("oj", [128, 4, 24], I32)
_b("koff lkf yd2", [128, 96], F32)
_b("kw", [128, 4, 4, 24], F32)
_b("qs", [128, 4, 2, 12, 4], F16)
_b("yd", [128, 16, 12], F32)
_b("dif absd", [128, 1536], F16)
_b("bd0 bd1", [128, 8, 384], BF)
_b("st mt sm km8", [128, 2048], BF)
_b("num", [128, 2048], I32)
_b("kidi", [128, 128], I32)
_b("kmk g8i ib", [128, 128], BF)
for _h in COLS:
    _b("row" + _h, [128, 4, len(COLS[_h])], F16)
    _b("pk" + _h, [128, 8, len(COLS[_h])] if _h == "b" else [128, 144, NM[_h]], F16)
_b("xw0", [128, 17, 8, 26], F16)
_b("xw1", [128, 35, 4, 26], F16)
_b("md", [128, 4, 8, 4, 4], F16)
CHAIN = (3,)
DUE = 0.0
_m("idt", "p1 n1 p2 n2 p4 n4 p128 n128 p2048 n2048", [128, 32, 4], F16)
_b("keep", [128, 8, 16], F16)
_b("w", [128, 8, 8], F32)
_b("cuti", [128, 384], I32)
_b("cf hf a16", [128, 384], F16)
VIA = (0, 1)
_b("ct", [128, 16, 4, 4], F16)
_b("on", [128, 16, 4], F16)
_b("ns fr", [128, 8, 4, 4, 4], F16)
_b("fl", [128, 8, 4, 4, 2], F16)
_b("il", [128, 288], U16)
_b("rt0 rt", [128, 2, 8, 16, 8], F16)
_b("rec", [128, 1536], F32)
_b("r16", [128, 4, 384], F16)
_b("mg mg0", [128, 6144], F16)
_b("mu mu0", [128, 384], U16)
_b("i32", [128, 128], F32)
_m("ef", "ef0 ef1 ef2 yes ycf", [128, 384], F32)
_b("el1 el2", [128, 384], F32)
NV = (256, 128)
_b("el3a ef3a", [128, 256], F32)
_b("el3b ef3b", [128, 128], F32)
_m("yr", "y0 y1 y2 y3 z1 z2", [128, 384], F16)
_b("pi", [128, 2], I32)
_b("pc", [128, 1], F32)
for _h in "01":
    _n = NV[int(_h)]
    _b("ga%s gb%s lk%s" % (_h, _h, _h), [128, 4 * _n], F16)
    _b("sl" + _h, [128, 2 * _n], U16)
    _b("sg" + _h, [128, 32 * _n], BF)
    _b("os" + _h, [128, 32, 4, 8], F32)
    _b("y" + _h + "f", [128, 16, 4, 8], F32)
    _b("yp" + _h, [128, 16, 4, 3], F32)
    _b("e" + _h, [128, 16, 4, 8], F16)
    _b("u" + _h, [128, 32, 16, 4], F16)
SEMAPHORES = ["cV", "cS", "cP", "cG", "lsem", "ar", "as", "ao", "ap"] + ["er%d" % h for h in (1, 2, 3, 4)] + ["d%d" % i for i in range(40)]
WHOLE = np.s_[:]
BIAS = {"": 300, "mg": 2500}
CYC, GATH, PEC, WAKE, OV = 0.85, 1.56, 0.44, 130, 35
JIT, TRIES, SEED, STRETCH, MOVES = 0.5, 400, 1, 300, 4000
CASES = ((0.75, 1.1, 0, 200, 0.92, 0.9), (1.0, 1.0, 0, 130, 1.0, 0.6), (1.25, 1.0, -15, 100, 1.12, 0.4))
MCH, SCH, LEAD = 48, 32, 2
LIST = "VS"
MEMO = {}


def rank_program(g, core, T, topo):
    rank = T.rank_of(core)
    if rank is None:
        return
    ENG = {"V": g.vector, "S": g.scalar, "P": g.tensor, "G": g, "Y": g.sync}
    cnt = {"cV": 0, "cS": 0, "cP": 0, "cG": 0}
    total = {}
    known = {e: {} for e in ENG}
    ops = []
    wr, rd, bank = {}, {}, {}
    cache = MEMO.setdefault("cols", {})
    ndma = [0]
    prog = []
    due, fill, soon, behind, first = {}, [], [], {}, [0]

    def R(name, idx=WHOLE):
        if name in ALIAS:
            ix = idx if isinstance(idx, tuple) else (idx,)
            return (ALIAS[name][0], (ix[0], ALIAS[name][1]) + ix[1:])
        return (name, idx)

    def IND(win, off):
        return ("@", win, off)

    def ap(r):
        if r[0] == "@":
            return ap(r[1]).indirect(ap(r[2]))
        return T[r[0]][r[1]]

    def psum(r):
        return SCRATCH[r[0]][0] == "psum"

    def size(n):
        return int(np.prod(SCRATCH[n][1][1:])) * (4 if n[:3] == "row" else 1)

    def cols(r):
        key = (r[0], repr(r[1]))
        if key not in cache:
            ix = r[1] if isinstance(r[1], tuple) else (r[1],)
            shape = SCRATCH[r[0]][1][1:]
            c = np.arange(int(np.prod(shape))).reshape(shape)[ix[1:]].reshape(-1)
            if r[0][:3] == "row":
                c = np.concatenate([c + size(r[0]) // 4 * b for b in np.unique(np.arange(128)[ix[0]] // 32)])
            cache[key] = np.unique(c)
        return cache[key]

    def parts(rs):
        out = []
        for r in rs:
            if r[0] == "@":
                out += [r[1], r[2]]
            elif r[0] in SCRATCH:
                out.append(r)
        return out

    def hazards(W, Lr, outs, ins, skip):
        need = set()
        for r in list(ins) + list(outs):
            if r[0] in W:
                need.update(np.unique(W[r[0]][cols(r)]).tolist())
        for r in outs:
            c, keep = cols(r), []
            for (o, m) in Lr.get(r[0], []):
                if m[c].any():
                    if not skip(o):
                        need.add(o)
                    m[c] = False
                    if not m.any():
                        continue
                keep.append((o, m))
            Lr[r[0]] = keep
        need.discard(-1)
        return need

    def note(W, Lr, o, outs, ins):
        for r in outs:
            if r[0] not in W:
                W[r[0]] = np.full(size(r[0]), -1)
            W[r[0]][cols(r)] = o
        by = {}
        for r in ins:
            if r[0] not in by:
                by[r[0]] = np.zeros(size(r[0]), bool)
            by[r[0]][cols(r)] = True
        for n, m in by.items():
            Lr.setdefault(n, []).append((o, m))

    def waits(e, outs, ins, queued):
        need = hazards(wr, rd, outs, ins, lambda o: False)
        if e == "P":
            need = set(o for o in need if ops[o][0] != "P")
        for r in outs + ins:
            if psum(r):
                need.update(o for e2, o in bank.get(r[0], {}).items() if e2 != e)
        k, want = known[e], {}
        for o in need:
            _, s, c, snap = ops[o]
            if k.get(s, 0) < c and (s not in want or want[s][0] < c):
                want[s] = (c, snap)
        for s in list(want):
            if any(s2 != s and want[s2][1].get(s, 0) >= want[s][0] for s2 in want):
                del want[s]
        for s, (c, snap) in want.items():
            if k.get(s, 0) >= c:
                continue
            ENG[e].wait_ge(T.sem[s], c)
            for s2, c2 in snap.items():
                k[s2] = max(k.get(s2, 0), c2)
            k[s] = max(k.get(s, 0), c)

    def issued(e, s, c, snap, outs, ins):
        total[s] = c
        ops.append((e, s, c, snap))
        note(wr, rd, len(ops) - 1, outs, ins)
        for r in outs + ins:
            if psum(r):
                bank.setdefault(r[0], {})[e] = len(ops) - 1

    def issue(o, e):
        outs, ins, a = o["o"], o["i"], o["a"]
        if o["k"] == "arr":
            issued(None, a[0], a[1], {}, outs, [])
            return
        if o["k"] == "send":
            waits("G", [], ins, False)
            src, dsts, s = a
            m = -1
            for c, _ in dsts:
                m &= topo.mask(core, c)
            if len(dsts) == 1:
                rid, pid = topo.addr(dsts[0][0], core)
                g.remote_dma(T[dsts[0][1]][:], ap(src), T.sem[s], T.sem.lsem, pid, rid, m)
            else:
                ids = [DstId(rid=topo.addr(c, core)[0], pnc=topo.addr(c, core)[1]) for c, _ in dsts]
                g.remote_dma_fused([RemoteDMATransfer(dst_ids=ids, dma_engine_mask=m, remote_sem=T.sem[s], srcs=[ap(src)], dsts=[T[n][:] for _, n in dsts])], local_sem=T.sem.lsem)
            total["lsem"] = total.get("lsem", 0) + bin(m).count("1")
            return
        waits(e, outs, ins, o["k"] == "op")
        if o["k"] == "dma":
            s = "d%d" % ndma[0]
            ndma[0] += 1
            for x, y in a:
                ENG[e].dma_start(ap(x), ap(y)).then_inc(T.sem[s], 16)
            issued(None, s, 16 * len(a), dict(known[e]), outs, ins)
        else:
            s = "c" + e
            for fn in a[e]:
                cnt[s] += 1
                fn().then_inc(T.sem[s], 1)
            issued(e, s, cnt[s], dict(known[e]), outs, ins)

    def two(r):
        return SCRATCH[r[0]][2] in (F16, BF, U16)

    def op(outs, ins, fns, both=False):
        o, i = parts(outs), parts(ins)
        n = len(cols(outs[0]))
        d, lab = {}, any(r[0] == "@" for r in ins)
        for e in fns:
            if lab:
                d[e] = 60 + CYC * GATH * n
            elif e == "G":
                d[e] = 190 + 2 * CYC * n
            elif e == "S":
                d[e] = OV + CYC * max(64, n)
            else:
                d[e] = OV + CYC * max(64, n * (2 if both else 0.5 if all(two(r) for r in o + i[:1]) else 1))
        prog.append({"k": "op", "o": o, "i": i, "a": {e: [f] for e, f in fns.items()}, "d": d, "lat": 0, "lab": lab})

    def dma(e, pairs, after=(), lat=2500):
        prog.append({"k": "dma", "o": parts([x for x, _ in pairs]), "i": parts([y for _, y in pairs]) + list(after), "a": pairs, "d": {e: 60 * len(pairs)}, "lat": lat, "lab": 0})

    def arrival(names, s, c, lat):
        prog.append({"k": "arr", "o": [R(n) for n in names], "i": [], "a": (s, c), "d": {"X": 0}, "lat": lat, "lab": 0})

    def send(src, dsts, s, lat, after=()):
        prog.append({"k": "send", "o": [R(n) for _, n in dsts], "i": [R(src)] + list(after), "a": (R(src), dsts, s), "d": {"G": 1200}, "lat": 0, "lab": 0})
        arrival([n for _, n in dsts], s, sum(len(topo.engines(c, core)) for c, _ in dsts), lat)

    def schedule():
        n = len(prog)
        W, Lr, hist, pre, data = {}, {}, {}, [], []
        for i, o in enumerate(prog):
            S = hazards(W, Lr, o["o"], o["i"], lambda j: False)
            data.append(set(S))
            note(W, Lr, i, o["o"], o["i"])
            es = "".join(o["d"])
            if i in behind:
                S.add(behind[i])
            if es == "G":
                S.update(hist.setdefault("G", [])[-1:])
                hist["G"].append(i)
            for b in set(r[0] for r in o["o"] + o["i"] if psum(r)):
                hb = hist.setdefault(b, {"P": [], "V": [], "S": []})
                if es == "P":
                    S.update(hb["P"][-1:] + hb["V"] + hb["S"])
                    hb["V"], hb["S"] = [], []
                    hb["P"].append(i)
                else:
                    S.update(hb["P"][-1:] + hb["S"] + (hb["V"] if es != "V" else []))
                    if es == "V":
                        hb["V"].append(i)
                    else:
                        hb["V"], hb["S"] = [], [i]
            S.discard(i)
            pre.append(S)
        suc = [[] for _ in range(n)]
        for i, S in enumerate(pre):
            for j in S:
                suc[j].append(i)
        def ready(c, e, done, eng, wake=WAKE):
            t = 0.0
            for j in pre[c]:
                x = done[j] if eng[j] == e and (e == "P" or j not in data[c]) else done[j] + wake
                if x > t:
                    t = x
            return t

        def place(jit, bias):
            prio = [0.0] * n
            for i in range(n - 1, -1, -1):
                prio[i] = max([prio[j] for j in suc[i]] + [prio[due[i]] + DUE if i in due else 0.0]) + (min(prog[i]["d"].values()) + 60) * jit[i] + prog[i]["lat"]
            busy, done, eng, order = {e: [(1e18, 1e18)] for e in "XYGPSV"}, [0.0] * n, [""] * n, []
            for c in sorted(range(n), key=lambda i: (-prio[i], i)):
                pick = None
                for e, d in prog[c]["d"].items():
                    t, bz = ready(c, e, done, eng), busy[e]
                    at, hi = 0, len(bz) - 1
                    while at < hi:
                        mid = (at + hi) // 2
                        at, hi = (mid + 1, hi) if bz[mid][1] <= t else (at, mid)
                    while bz[at][0] < t + d:
                        t, at = max(t, bz[at][1]), at + 1
                    key = t + d + (bias[c] if e == "V" else 0)
                    if pick is None or key < pick[0]:
                        pick = (key, t, d, at, e)
                _, t, d, at, eng[c] = pick
                if eng[c] != "X":
                    busy[eng[c]].insert(at, (t, t + d))
                done[c] = t + d + prog[c]["lat"]
                order.append((t, len(order), c, eng[c]))
            return [(c, e) for _, _, c, e in sorted(order)]

        dur, lat, gat = [o["d"] for o in prog], [o["lat"] for o in prog], [o["lab"] for o in prog]

        def span(order, kg, kp, ov, wake, _, kl, link=None):
            t, done, eng = {e: 0.0 for e in "XYGPSV"}, [0.0] * n, [""] * n
            last, why, at = {}, [None] * n, [0] * n
            for k, (c, e) in enumerate(order):
                eng[c], at[c] = e, k
                s, by = 0.0, None
                for j in pre[c]:
                    x = done[j] if eng[j] == e and (e == "P" or j not in data[c]) else done[j] + wake
                    if x > s:
                        s, by = x, j
                if e != "X" and t[e] > s:
                    s, by = t[e], last[e]
                why[c], last[e] = by, c
                t[e] = end = s + (dur[c][e] * kg if gat[c] else dur[c][e] * kp if e == "P" else dur[c][e] + ov if e in "VS" else dur[c][e])
                done[c] = end + (lat[c] * kl if e == "X" else lat[c])
            if link is not None:
                c = done.index(max(done))
                while why[c] is not None:
                    if why[c] not in pre[c]:
                        link.append((at[why[c]], at[c]))
                    c = why[c]
            return max(done)
        state = [SEED]

        def rng():
            state[0] = (state[0] * 1103515245 + 12345) % 2 ** 31
            return state[0] / 2 ** 31
        best = None
        jit, bias = [1.0] * n, [BIAS.get(o["o"][0][0], BIAS[""]) if o["o"] else 0 for o in prog]
        for _ in range(TRIES):
            j2, b2, a = list(jit), list(bias), int(rng() * n)
            for i in range(a, min(n, a + int(rng() * STRETCH))):
                if best and rng() < 0.3:
                    j2[i] = 1 + JIT * (2 * rng() - 1)
                    b2[i] = bias[i] + 1000 * (rng() - 0.5)
            o = place(j2, b2)
            cost = sum(span(o, *m) / m[4] for m in CASES)
            if best is None or cost <= best[0]:
                best, jit, bias = (cost, o), j2, b2
        for _ in range(MOVES):
            o, link = list(best[1]), []
            span(o, *CASES[int(rng() * len(CASES))], link)
            if not link:
                break
            a, b = link[int(rng() * len(link))]
            x = rng()
            flex = [k for k in (a, b) if len(prog[o[k][0]]["d"]) == 2]
            if flex and x < 0.35:
                k = flex[int(rng() * len(flex))]
                o[k] = (o[k][0], "V" if o[k][1] == "S" else "S")
            elif x < 0.7:
                need, seg = {o[b][0]}, o[a:b + 1]
                for c, e in reversed(seg):
                    if c in need:
                        need.update(pre[c])
                if o[a][0] in need:
                    continue
                o[a:b + 1] = [y for y in seg if y[0] in need] + [y for y in seg if y[0] not in need]
            else:
                b = min(n - 1, b + int(rng() * 40))
                late, seg = {o[a][0]}, o[a:b + 1]
                for c, e in seg:
                    if pre[c] & late:
                        late.add(c)
                o[a:b + 1] = [y for y in seg if y[0] not in late] + [y for y in seg if y[0] in late]
            cost = sum(span(o, *m) / m[4] for m in CASES)
            if cost <= best[0]:
                best = (cost, o)
        MEMO["spans"] = [span(best[1], *m) for m in CASES]
        MEMO["span"] = best[0] / len(CASES)
        return best[1]

    def tt(out, a, b, o):
        op([out], [a, b], {"V": lambda: g.vector.tensor_tensor(ap(out), ap(a), ap(b), o)}, a[0] != "@" and not psum(a) and not psum(b))

    def ts(out, a, s1, o1, s2=None, o2=None):
        v = lambda x: ap(x) if isinstance(x, tuple) else x
        ins = [a] + [x for x in (s1, s2) if isinstance(x, tuple)]
        if o2 is None:
            op([out], ins, {"V": lambda: g.vector.tensor_scalar(ap(out), ap(a), v(s1), None, o1)})
        else:
            op([out], ins, {"V": lambda: g.vector.tensor_scalar(ap(out), ap(a), v(s1), v(s2), o1, o2)})

    def ms(out, c):
        op([out], [], {"V": lambda: g.vector.memset(ap(out), c)})

    def cp(out, a, es="VS"):
        f = {"V": lambda: g.vector.tensor_copy(ap(out), ap(a)), "S": lambda: g.scalar.activation(ap(out), ap(a), ACT.Copy)}
        op([out], [a], {e: f[e] for e in es})

    def aff(out, a, scale, bias, es="VS"):
        f = {"V": lambda: g.vector.tensor_scalar(ap(out), ap(a), scale, bias, MUL, ADD),
             "S": lambda: g.scalar.activation(ap(out), ap(a), ACT.Identity, bias=bias, scale=scale)}
        op([out], [a], {e: f[e] for e in es})

    def relu(out, a, scale=1.0, bias=0.0, es="VS"):
        f = {"V": lambda: g.vector.tensor_scalar(ap(out), ap(a), bias if scale == 1.0 else scale, 0.0, ADD if scale == 1.0 else MUL, MAX),
             "S": lambda: g.scalar.activation(ap(out), ap(a), ACT.Relu, bias=bias, scale=scale)}
        op([out], [a], {e: f[e] for e in es})

    def pe(lst, group=True):
        fns, d = [], 0.0
        for i, (o, l, r) in enumerate(lst):
            fns.append(lambda o=o, l=l, r=r, i=i: g.tensor.matmul(ap(o), ap(l), ap(r), i == 0 or not group, i == len(lst) - 1 or not group))
            d += PEC * max(min(64, len(cols(l))), len(cols(r))) * (4 if SCRATCH[l[0]][2] == F32 else 1)
        prog.append({"k": "op", "o": [o for o, _, _ in lst], "i": [x for _, l, r in lst for x in (l, r)], "a": {"P": fns}, "d": {"P": d}, "lat": 0, "lab": 0})

    def pe_open(lst, first, last):
        fns, d = [], 0.0
        for i, (o, l, r) in enumerate(lst):
            fns.append(lambda o=o, l=l, r=r, i=i: g.tensor.matmul(ap(o), ap(l), ap(r), first and i == 0, last and i == len(lst) - 1))
            d += PEC * max(min(64, len(cols(l))), len(cols(r))) * (4 if SCRATCH[l[0]][2] == F32 else 1)
        prog.append({"k": "op", "o": [o for o, _, _ in lst], "i": [x for _, l, r in lst for x in (l, r)], "a": {"P": fns}, "d": {"P": d}, "lat": 0, "lab": 0})

    def sel(out, in_, pattern, cmp, fill, base, cm):
        op([out], [in_], {"G": lambda: g.affine_select(ap(out), ap(in_), pattern, cmp, fill, base, cm)})

    def iota(out, pattern, base, cm):
        if SCRATCH[out[0]][2] == I32:
            op([out], [], {"G": lambda: g.iota(ap(out), pattern, base, cm)})
        else:
            op([out], [], {"G": lambda: g.iota(ap(out), pattern, base, cm, allow_small_or_imprecise_dtypes=True)})

    s_ = np.s_
    P96 = slice(0, 96)
    I = lambda n: R(n, s_[0:96, 0:24])
    PK = lambda n, a, k: R("pk" + OFF[n][0], s_[:, :, OFF[n][1] + a:OFF[n][1] + a + k])
    ST = lambda n, a: R("pk" + OFF[n][0], s_[:, a:a + 128, OFF[n][1]])
    slot = lambda b, k: R(b, s_[P96, :, :, k])
    fslot = lambda b, k: R(b, s_[P96, k // 4::2, k % 4, :])
    cores = list(T.cores)
    nxt = lambda h: cores[(rank + h) % N]

    dma("S", [(R("cuti"), ("cut0", s_[:, :]))])
    cp(R("cf"), R("cuti"), "V")
    dma("S", [(R("lki"), ("lk", s_[:, :]))])
    dma("Y", [(R("av0"), ("a", s_[:, :])), (R("ak0"), ("a0", s_[:, :]))], lat=3200)
    dma("Y", [(R("kidi"), ("kid", s_[:, :]))], lat=3500)
    for b in "cb":
        soon.extend((len(prog), len(prog) + 1))
        ms(R("row" + b), 0.0)
        ms(R("pk" + b), 0.0)
        if b not in MEMO:
            MEMO[b] = paints(b)
        for a, rows, cs, x in MEMO[b]:
            o = R("row" + b, s_[32 * a:32 * a + 1, rows, cs])
            op([o], [o], {"V": lambda o=o, x=x: g.vector.memset(ap(o), x), "S": lambda o=o, x=x: g.scalar.activation(ap(o), ap(o), ACT.Identity, bias=x)})
        dma("Y", [(R("pk" + b, s_[16 * gg:16 * gg + 16, gg if b == "b" else slice(16 * gg, 16 * gg + 16), :]), R("row" + b, s_[0::32])) for gg in range(8)], lat=4000)
    ms(R("p1"), 1.0)
    sel(R("p1"), R("p1"), [[-1, 128]], EQ, 0.0, 0, 1)
    iota(R("num"), [[1, 2048]], 0, 0)
    dma("Y", [(R("num", s_[0::16, :]), ("kid", s_[:, :])), (R("num", s_[1::16, :]), ("up", s_[:, :]))])
    dma("Y", [(R("st"), ("s", s_[:, :]))], [R("cf")], 5000)
    ms(R("pka"), 0.0)
    for j in range(4):
        zc = R("pka", s_[:, 12 + j::16, :])
        sel(zc, zc, [[-16, 9], [-4, 4]], NE, 8192.0, -j, 1)
    iota(R("koff"), [[2048, 4], [0, 24]], 0, 0)
    send("av0", [(nxt(3), "av3")], "ar", 14000)
    send("av0", [(nxt(h), "av%d" % h) for h in (1, 2)], "as", 20000)
    for n, x in (("n1", -1.0), ("n2048", -2048.0), ("p2048", 2048.0), ("p4", 4.0), ("n4", -4.0), ("p128", 128.0), ("p2", 2.0), ("n2", -2.0), ("n128", -128.0)):
        aff(R(n), R("p1"), x, 0.0)
    for t in range(4):
        ms(R("ct", s_[:, :, :, t]), 0.375 - 0.25 * t)
    ms(R("on"), 1.0)
    ts(R("kmk"), R("kidi"), 0.0, LT, -256.0, MUL)
    dma("S", [(R("km8", s_[0:8, :]), R("kmk"))])
    cp(R("ib"), R("p1"))
    ms(R("g8i"), 1.0)
    sel(R("g8i"), R("g8i"), [[1, 128]], GE, 0.0, 0, -16)
    sel(R("g8i"), R("g8i"), [[-1, 128]], GE, 0.0, 15, 16)
    ms(R("w"), 0.0)
    sel(R("w"), R("w"), [[-8, 8], [-1, 8]], NE, 4.0, 0, 1)
    sel(R("w"), R("w"), [[-8, 8], [0, 8]], NE, -4.0, -7, 1)
    sel(R("w", s_[:, :, 7]), R("w", s_[:, :, 7]), [[-8, 8]], NE, 4.0, -2, 1)
    iota(R("bd0"), [[0, 3072]], 0, 0)
    dma("Y", [(R("bd0", s_[16 * gg:16 * gg + 16, gg, :]), ("a", s_[16 * gg:16 * gg + 16, :])) for gg in range(8)])
    cp(R("keep"), R("p1"))
    cp(R("i32"), R("p1"))
    ms(R("keep", s_[:, :, AK:P + 1:P - AK]), 0.0)

    def dist(ak, ow, via):
        for k in range(4):
            c = s_[:, 384 * k:384 * k + 384]
            i, d = IND(R(ak, s_[:, 0:384]), R("lku", s_[:, 24 * k:24 * k + 24])), R("dif", c)
            if k in via:
                cp(d, i, "S")
                pe([(R(via[k], s_[:, 0:12]), R("p1"), d), (R(via[k], s_[:, 0:12]), R("n1"), R("a16"))])
                d = R(via[k], s_[:, 0:12])
            else:
                tt(d, i, R("av0"), SUB)
            op([R("absd", c)], [d], {"S": lambda c=c, d=d: g.scalar.activation(ap(R("absd", c)), ap(d), ACT.Abs)})
        pe([(R("X2", s_[:, 0:24]), ST("st", 3 - j), R("absd", s_[:, j::4])) for j in range(4)])
        cp(R("qs"), R("X2", s_[:, 0:24]))
        for q in range(4):
            for j in (0, 1):
                pe([(R("X2", s_[:, 2 * q + j::8, 0:12]), ST("z%d" % q, 12 - 4 * i), R("qs", s_[:, :, j, :, i])) for i in range(4)])
        dk = lambda a, b: R("X2", s_[:, a:b, 0:12])
        tt(R("yd"), dk(0, 16), R("kw", s_[:, 0:2]), ADD)
        tt(dk(16, 32), dk(16, 32), R("kw", s_[:, 2:4]), ADD)
        tt(dk(0, 8), dk(16, 24), R("yd", s_[:, 0:8]), MIN)
        tt(R("yd2"), dk(24, 32), R("yd", s_[:, 8:16]), MIN)
        tt(R("oi"), dk(0, 8), R("yd2"), MIN)
        ts(R("oj"), R("oi"), 2047, AND)
        cp(R(ow, s_[:, 0:64]), R("oj", s_[:, :, 0:16]), "V")
        cp(R(ow, s_[:, 64:96]), R("oj", s_[:, :, 16:24]), "V")

    cp(R("lku"), R("lki"), "V")
    tt(R("lkf"), R("lki"), R("koff"), ADD)
    for q in range(4):
        aff(R("kw", s_[:, :, q, :]), R("lkf"), 1.0, 384.0 * q)
    cp(R("a16"), R("av0"))
    dist("ak0", "own0", {k: ("Oa", "Ob")[k % 2] for k in VIA})

    while soon:
        due[soon.pop()] = len(prog)
    aff(R("hf"), R("cuti"), 0.5, 1023.75, "S")
    half = lambda n, H, k: R(n, s_[P96, :, 2 * H:2 * H + 2, :, k])
    for H, (be, bk) in enumerate((("D0", "K"), ("D1", "PR"))):
        x = str(H)
        blk = lambda n, r: R(n, s_[:, 192 * H + 96 * r:192 * H + 96 * r + 96])
        pe([(R(be, s_[P96, r::2, :, a:a + n]), blk("hf", r), R(m, s_[:, :, o:o + n])) for r in (0, 1) for a, n, d in ((0, 3, 1), (3, 2, 2), (5, 1, 3)) for m, o in (("p1", 0), ("n1", d))])
        ts(slot("e" + x, s_[0:6]), slot(be, s_[0:6]), 0.0, EQ)
        pe_open([(R(bk, s_[P96, r::2, :, 0:4]), blk("cf", r), R("p1")) for r in (0, 1)] + [(slot(bk, s_[0:4]), I("p1"), R("ct", s_[P96]))], True, False)
        pe_open([(slot(bk, t), I("n2048"), slot("e" + x, j)) for j, tu in enumerate(PAIRS) for t in tu], False, True)
        y = lambda k: slot("y" + x + "f", k)
        k_ = lambda k: slot(bk, k)
        cp(y(s_[0:2]), k_(s_[1:4:2]))
        tt(k_(4), k_(0), y(0), MIN)
        tt(k_(5), k_(0), y(0), MAX)
        tt(y(2), k_(2), y(1), MIN)
        tt(y(3), k_(2), y(1), MAX)
        tt(k_(6), k_(4), y(2), MAX)
        tt(y(4), k_(5), y(3), MIN)
        tt(k_(0), k_(4), y(2), MIN)
        tt(k_(3), k_(5), y(3), MAX)
        tt(k_(2), k_(6), y(4), MAX)
        tt(k_(1), k_(6), y(4), MIN)
        ts(half("ns", H, s_[0:4]), k_(s_[0:4]), 12582912.0, ADD, -12582912.0, ADD)
        ts(half("fl", H, s_[0:2]), half("ns", H, s_[0:4:2]), 0.0, LT)
        tt(half("fr", H, s_[0:4]), k_(s_[0:4]), half("ns", H, s_[0:4]), SUB)
        aff(slot("e" + x, s_[6:8]), half("ns", H, s_[2:4]), 0.5, 1023.75)
    for i, (role, f) in enumerate(((0, 0), (2, 1), (3, 1))):
        pe([(R("X1", s_[:, 48 * i:48 * i + 48, :]), R("ns", s_[P96, :, :, :, role]), I("p1")), (R("X1", s_[:, 48 * i:48 * i + 48, :]), R("fl", s_[P96, :, :, :, f]), I("p2048"))])
    cp(R("il"), R("X1", s_[:, 0:144, :]))
    for i in range(3):
        for j in (0, 1):
            cp(R("mg", s_[:, 1536 * i + 768 * j:1536 * i + 768 * j + 768]), IND(R("num", s_[:, 0:2048]), R("il", s_[:, 96 * i + 48 * j:96 * i + 48 * j + 48])), "VS"[j])
    for H, (be, b1, b2) in enumerate((("D0", "Oa", "K"), ("D1", "Ob", "PR"))):
        x = str(H)
        u = lambda k: R("u" + x, s_[P96, k])
        ON = R("on", s_[P96])
        ns, fr, fAB, fCD = (lambda k: half("ns", H, k)), (lambda k: half("fr", H, k)), half("fl", H, 0), half("fl", H, 1)
        lst = []
        lst += [(slot(be, 5), I("p1"), ns(0)), (slot(be, 5), I("p2048"), fAB), (slot(be, 5), I("p1"), ON), (slot(be, 6), I("p1"), ns(3)), (slot(be, 6), I("n1"), ns(2)),
                (slot(be, 7), I("p4"), fr(3)), (slot(be, 7), I("n4"), fr(2))]
        pe_open(lst, True, False)
        for i, (a, k) in enumerate(((0, 1), (1, 2), (3, 2))):
            pe_open([(R(be, s_[P96, r::2, q, a:a + k]), R("mg", s_[:, 1536 * i + 8 * H + 4 * r + q:1536 * i + 1536:16]), R("p1", s_[:, 0::4, 2 - k:2]))
                     for r in (0, 1) for q in range(4)] + [(slot(be, 2 * i), I("n1"), ON)], False, i == 2)
        zP, z, zl1, hP, sw, s3, t3, zq2, zq3, zl2, zl3, zs, zb = [u(k) for k in range(13)]
        tt(zP, slot(be, 0), fAB, MUL)
        aff(hP, zP, 0.5, 1024.25, "V")
        tt(z, slot(be, 5), fAB, MUL)
        tt(zl1, slot(be, 5), fCD, MUL)
        tt(sw, slot("e" + x, 6), hP, EQ)
        tt(s3, slot("e" + x, 7), hP, EQ)
        tt(t3, s3, fCD, ADD)
        for o, m, k in ((zq2, sw, 2), (zl2, s3, 1), (zl3, sw, 3), (zs, sw, 6), (zb, sw, 7), (zq3, t3, 4)):
            tt(o, slot(be, k), m, MUL)
        CT = R("ct", s_[P96, :, :, 0])
        sums = {AK: [("p1", z), ("n1", ON)], A0: [("p1", ns(0)), ("p2048", fAB), ("p1", ON), ("n1", z)], B0: [("p1", ns(1)), ("p2048", fAB), ("p1", ON), ("n1", z)],
                V: [("p128", t3), ("p128", sw)], U: [("p128", ON)], U2: [("p128", ON)], L: [("p1", zl1), ("n1", fCD), ("p1", zl2), ("p1", zl3)],
                C: [("p1", ns(2)), ("p2048", fCD), ("p1", zs)], D: [("p1", ns(3)), ("p2048", fCD), ("n1", zs)], P: [("p1", ON), ("p1", zP)],
                Q: [("p1", ON), ("p1", zq2), ("p1", zq3)], F: [("p128", fCD)], BA: [("p4", fr(0)), ("p4", CT)], BB: [("p4", fr(1)), ("p4", CT)],
                BC: [("p4", fr(2)), ("p4", CT), ("p1", zb)]}
        sums[7] = sums[U]
        for b, f0 in ((b1, 0), (b2, 8)):
            pe([(fslot(b, f - f0), I(m), src) for f in range(f0, f0 + 8) for m, src in sums[f]])
            cp(R("rt0", s_[P96, H, :, f0:f0 + 8, :]), R(b, s_[P96]))
    for q, bk in enumerate(("D0", "Oa", "K", "D1")):
        pe([(R(bk, s_[:, 3 * r:3 * r + 3]), R("rt0", s_[P96, r // 2, :, :, 4 * (r % 2) + q]), I("p1")) for r in range(4)], False)
        cp(R("rec", s_[:, 384 * q:384 * q + 384]), R(bk, s_[:, 0:12]))
    dma("Y", [(R("mt"), ("m", s_[:, :]))], [R("rec")], 6000)
    for i, bk in enumerate(("X1", "K", "PR", "X2")):
        c = s_[:, 512 * i:512 * i + 512]
        pe([(R(bk), R("ib"), R("st", c)), (R(bk), R("g8i", s_[0:8, :]), R("km8", s_[0:8, 512 * i:512 * i + 512]))])
        relu(R("sm", c), R(bk))
    ms(R("sm", s_[:, 1:2]), 255.0)
    iota(R("xw0", s_[:, 0::2, :, 3:9]), [[0, 432]], 0, 0)
    iota(R("xw0", s_[:, 0::2, :, 20:23]), [[0, 216]], 0, 0)
    iota(R("xw1", s_[:, :, :, 3:9]), [[0, 840]], 0, 0)
    iota(R("xw1", s_[:, :, :, 20:23]), [[0, 420]], 0, 0)
    iota(R("rt", s_[:, :, :, 0:8, :]), [[0, 1024]], 0, 0)
    iota(R("md", s_[:, :, :, 0:2, :]), [[0, 256]], 0, 0)
    iota(R("bd1"), [[0, 3072]], 0, 0)
    iota(R("pi", s_[:, 0:1]), [[0, 1]], 0, 1)
    ts(R("pi", s_[:, 1:2]), R("pi", s_[:, 0:1]), 3, AND)
    ts(R("pc"), R("pi", s_[:, 1:2]), -2048.0, MUL)

    def front(h, H):
        x, G = str(H), "g" + "ab"[h % 2] + str(H)
        n = NV[H]
        for a in range(0, 4 * n, 512):
            cp(R(G, s_[:, a:a + 512]), IND(R("rec", s_[:, 0:1536]), R("own%d" % h, s_[:, 64 * H + a // 16:64 * H + a // 16 + 32])))
        for q2 in (0, 1):
            pe([(R("X1", s_[:, 0:n, q2]), ST("mix", 8 - 8 * b), R(G, s_[:, n * (2 * q2 + b):n * (2 * q2 + b + 1)])) for b in (0, 1)])
        for a, b in ((0, 2 * SCH), (2 * SCH, n)) if H == 0 else ((0, n),):
            cp(R("sl" + x, s_[:, 2 * a:2 * b]), R("X1", s_[:, a:b, :]), LIST)
        for v in chunks(H):
            if H == 0:
                first[0] = len(prog) - LEAD
            else:
                behind[len(prog)] = first[0]
            cp(R("sg" + x, s_[:, 32 * v:32 * (v + SCH)]), IND(R("sm", s_[:, 0:2048]), R("sl" + x, s_[:, 2 * v:2 * (v + SCH)])))

    def chunks(H):
        return sorted(range(0, NV[H], SCH), key=lambda v: (v % 128 >= 64, v))

    def picks(b, name, G, H):
        return [(R(b, s_[:, r::2, q, :]), R(G, s_[:, NV[H] * q + 128 * r:NV[H] * q + 128 * r + 128]), PK(name, 0, 8)) for r in range(2 - H) for q in range(4)]

    R1, Y4, YM, N2, HD = 0, 1, 2, 3, 4
    KB = ("K", "Oa")
    xt = lambda H, k: R("xw0", s_[:, 1:17:2, :, k]) if H == 0 else R("xw1", s_[:, 3:35:4, :, k])
    slots = lambda H: lambda b, k: R(b, s_[:, 0::1 + H, :, k])

    def prelim(h, H):
        x, G, slot = str(H), "g" + "ab"[h % 2] + str(H), slots(H)
        e = lambda k: slot("e" + x, k)
        pe(picks("PR", "pr", G, H), False)
        cp(slot("yp" + x, s_[0:2]), slot("PR", s_[0:2]))
        relu(e(s_[0:2]), slot("PR", s_[4:6]))
        aff(e(HD), slot("PR", 6), 0.5, 1023.75)
        cp(xt(H, 6), slot("PR", 7))
        tt(slot("yp" + x, 2), slot("PR", 2), slot("yp" + x, 0), MAX)
        tt(e(YM), slot("PR", 3), slot("yp" + x, 2), MAX)
        relu(e(N2), e(YM), -1.0)

    def errs(h, H):
        x, G, bd, slot, I = str(H), "g" + "ab"[h % 2] + str(H), "bd%d" % (h % 2), slots(H), R
        e = lambda k: slot("e" + x, k)
        for c in chunks(H):
            lst = []
            for v in range(c, c + SCH):
                if H and v < 64:
                    o = R("X1", s_[0:32, 4 * v:4 * v + 4, :])
                else:
                    o = R(("Oa", "Ob")[v % 128 // 64], s_[32 * (v // 128):32 * (v // 128) + 32, v % 64 // 4, v % 4, :])
                lst.append((o, R("sg" + x, s_[:, 32 * v:32 * v + 32]), R(bd, s_[:, :, 256 * H + v])))
            pe(lst, False)
        for j, bk in enumerate((("Oa", "Ob"), ("X1", "Ob"))[H]):
            cp(R("os" + x, s_[0:64 >> H, 16 * j:16 * j + 16]), R(bk, s_[0:64 >> H]))
        pe_open(picks(KB[H], "kb", G, H) + [(slot(KB[H], k), I(m), e(j)) for k, m, j in ((1, "p1", Y4), (2, "p1", R1), (4, "n1", Y4), (4, "n1", YM))], True, False)
        if H == 0:
            pe_open([(R("K", s_[:, 2 * gg:2 * gg + 2]), R("os0", s_[0:64, :, :, gg]), R("w", s_[0:64])) for gg in range(8)], False, True)
        else:
            pe_open([(R("Oa", s_[:, 2 * gg]), R("os1", s_[0:32, :, :, gg]), R("w", s_[0:32, 0:4])) for gg in range(8)], False, True)
        pe(picks("D0", "d0", G, H) + [(slot("D0", k), I(m), e(j)) for k, m, j in ((2, "n1", R1), (3, "p2", HD))])
        pe(picks("D1", "d1", G, H) + [(slot("D1", k), I(m), e(j)) for k, m, j in ((3, "p1", R1), (4, "p1", Y4), (4, "p1", YM), (4, "n1", N2), (5, "p1", N2), (7, "n2", Y4), (7, "n1", YM))])

    def logic(h, H):
        x, slot = str(H), slots(H)
        k, y, u = (lambda j: slot(KB[H], j)), (lambda j: slot("y" + x + "f", j)), (lambda j: xt(H, j))
        tau, mu, g2, w, eC, eDs = [u(j) for j in range(6)]
        cp(y(s_[0:2]), k(s_[3:5]))
        relu(y(3), k(5))
        relu(y(2), k(6), 1.0, -BIG)
        tt(y(s_[4:6]), k(s_[0:2]), y(s_[0:2]), MAX)
        tt(k(0), k(5), slot("yp" + x, 1), LT)
        ts(k(5), k(5), 0.0, GT)
        tt(k(1), k(1), y(1), LT)
        tt(k(2), k(2), y(2), MAX)
        tt(k(s_[6:8]), k(s_[6:8]), y(s_[3:5]), MAX)
        tt(k(4), k(2), y(5), LT)
        tt(tau, k(7), y(3), LT)
        tt(k(3), k(6), y(4), LT)
        tt(eC, k(5), tau, MUL)
        tt(eDs, k(0), tau, MUL)
        prod = lambda o, n, b, j, m: tt(u(s_[o:o + n]), slot(b, j), u(s_[m:m + n]), MUL)
        add = lambda terms, first, last: pe_open([(R("PR", s_[:, (f - C) // 4::2, f % 4, 0:8 - 4 * H]), R(m), u(j)) for f, m, j in terms], first, last)
        tt(g2, k(4), eC, MUL)
        prod(22, 2, "D1", s_[0:7:6], 4)
        tt(mu, k(3), g2, ADD)
        prod(24, 2, "D1", s_[2:4], 4)
        tt(w, k(1), mu, MUL)
        prod(7, 2, "D0", s_[0:2], 0)
        prod(19, 3, "D1", s_[5:8], 1)
        add([(C, "p1", 23), (D, "n1", 22), (D, "n1", 23), (BA, "p1", 24), (BC, "n1", 25), (F, "n128", 1), (F, "n128", 5), (D, "n1", 3), (C, "n1", 7)], True, False)
        prod(15, 2, "D1", s_[0:2], 0)
        prod(17, 2, "D1", s_[3:5], 0)
        add([(BC, "p1", 19), (C, "p1", 20), (Q, "p1", 20), (BA, "p1", 21), (C, "n1", 15), (D, "p1", 15), (D, "p1", 16), (BC, "p1", 17), (BB, "p1", 18)], False, False)
        for j in (2, 4, 6):
            prod(7 + j, 2, "D0", s_[j:j + 2], 0)
        add([(BB, "p1", 9), (L, "p1", 10), (F, "n128", 11), (C, "p1", 12), (BA, "p1", 13), (Q, "p1", 14)], False, True)
        cp(R("rt", s_[:, H, :, 8:16, 0:8 - 4 * H]), R("PR", s_[:, :, :, 0:8 - 4 * H]))
        for r in range(2 - H if h == 3 else 0):
            cp(R("md", s_[:, 2 * H + r, :, 2:4, :]), R("PR", s_[:, 0::2, 0:2, 4 * r:4 * r + 4]))

    def back(h, H):
        G, lk, n, nb = "g" + "ab"[h % 2] + str(H), "lk" + str(H), NV[H], 2 + 2 * H
        for ks in ((6,), (22,), (7, 8), (3, 20)):
            pe_open([(R("X1", s_[:, 0:n // 8, :]), R("xw" + str(H), s_[:, nb - 1 - b:8 * nb + nb - 1 - b, :, k]), R("n1" if k == 20 else "p1", s_[:, :, b::nb]))
                     for k in ks for b in range(nb)], ks[0] == 6, ks[0] == 3)
        while fill and H:
            due[fill.pop()] = len(prog)
        cp(R("xl", s_[:, 64 * H:64 * H + n // 4]), R("X1", s_[:, 0:n // 8, :]), LIST)
        for j in (0, 1):
            cp(R(lk, s_[:, 2 * n * j:2 * n * j + 2 * n]), IND(R("num", s_[:, 0:2048]), R("xl", s_[:, 64 * H + n // 8 * j:64 * H + n // 8 * (j + 1)])))
        for bk, qs in ((("Ob", (0, 1)), ("K", (2, 3))), (("Oa", (0, 1)), ("D1", (2, 3))))[H]:
            a = n // 32
            o = lambda q, r: R(bk, s_[:, a * (q % 2) + 4 * r:a * (q % 2) + 4 * r + 4])
            pe_open([(R(bk, s_[:, 0:2 * a]), R("keep"), R(G, s_[:, n * qs[0]:n * qs[0] + 2 * n]))], True, False)
            pe_open([(o(q, r), R("rt", s_[:, H, :, :, 4 * r + q]), R("p1")) for q in qs for r in range(2 - H)], False, False)
            pe_open([(o(q, r), ST("sel", 0), R(lk, s_[:, 4 * r + q::8 - 4 * H])) for q in qs for r in range(2 - H)], False, True)
            if h == 3:
                cp(R("r16", s_[:, qs[0]:qs[0] + 2, 256 * H:256 * H + n]), R(bk, s_[:, 0:2 * a]))
            for q in qs if h < 3 else ():
                cp(R("rec", s_[:, 384 * q + 256 * H:384 * q + 256 * H + n]), R(bk, s_[:, a * (q % 2):a * (q % 2) + a]))

    def msum(h):
        G, lk, av = "g" + "ab"[h % 2], "lk%d" % (h % 2), "av%d" % h
        if h < 3:
            sel(R("r16"), R("rec"), [[0, 1536]], EQ, 0.0, 0, 0)
            for q in range(4):
                pe([(R("X2", s_[:, 6 * q:6 * q + 6]), ST("mr", 12 - 4 * r), R("r16", s_[:, q, 96 * r:96 * r + 96])) for r in range(4)])
            mu, mb = ("mu", "mu0")[h == 0], ("mg", "mg0")[h == 0]
            soon.append(len(prog))
            cp(R(mu), R("X2", s_[:, 0:24]), LIST)
            for q in range(4):
                for a in range(96 * q, 96 * q + 96, MCH):
                    if h:
                        fill.append(len(prog))
                    o, i = R(mb, s_[:, 16 * a:16 * (a + MCH)]), IND(R("mt", s_[:, 0:2048]), R(mu, s_[:, a:a + MCH]))
                    if q in CHAIN and h:
                        tt(o, i, R(mb, s_[:, 16 * (a - 96):16 * (a + MCH - 96)]), ADD)
                    else:
                        cp(o, i)
            if h == 0:
                return
            for r in range(4):
                pe([(R("X2", s_[:, 6 * r:6 * r + 6]), R("p1"), R("mg", s_[:, 1536 * q + 4 * r + t:1536 * q + 1536:16])) for q in range(4) if q + 1 not in CHAIN for t in range(4)])
            cp(R("ef%d" % h), R("X2", s_[:, 0:24]))
            send("ef%d" % h, [(nxt(-h), "el%d" % h)], "er%d" % h, 9000)
            return
        for H in (0, 1):
            nv = NV[H]
            c, n = s_[:, 256 * H:256 * H + nv], "3" + "ab"[H]
            pe_open([(R("X2", s_[:, 0:nv // 16]), ST("mg", 3 - q), R(G + str(H), s_[:, nv * q:nv * q + nv])) for q in range(4)], True, False)
            pe_open([(R("X2", s_[:, 8 * r:8 * r + 8]), R("md", s_[:, 2 * H + r]), R("p1")) for r in range(2 - H)], False, False)
            pe_open([(R("X2", s_[:, 8 * r:8 * r + 8]), ST("ml", 3 - q), R("lk" + str(H), s_[:, 4 * r + q::8 - 4 * H])) for r in range(2 - H) for q in range(4)], False, True)
            cp(R("mu", c), R("X2", s_[:, 0:nv // 16]), LIST)
            for a in range(256 * H, 256 * H + nv, 64):
                cp(R("mg", s_[:, 16 * a:16 * a + 1024]), IND(R("mt", s_[:, 0:2048]), R("mu", s_[:, a:a + 64])), "VS"[a // 64 % 2] if H else "VS")
            for a in range(0, nv, 128 >> H):
                b = 16 * (256 * H + a)
                pe([(R("X2", s_[:, 16 + a // 16:16 + (a + (128 >> H)) // 16]), R("p1"), R("mg", s_[:, b + t:b + (2048 >> H):16])) for t in range(16)])
            tt(R("ef" + n), R("X2", s_[:, 16:16 + nv // 16]), R(av, c), MUL)
            send("ef" + n, [(nxt(-h), "el" + n)], "er%d" % (3 + H), 6000)

    def cut_out():
        bk = R("K", s_[:, 0:12])
        pe([(bk, ST("my", 12 - 4 * q), R("r16", s_[:, q])) for q in range(4)])
        ts(R("y0"), bk, 2048.0, MIN)
        for c, n in ((1, "z1"), (2, "z2"), (3, "y3")):
            relu(R(n), bk, 1.0, -2048.0 * c)
        for c in (1, 2):
            ts(R("y%d" % c), R("z%d" % c), 2048.0, MIN)
        pe([(R("PR", s_[:, 0:12]), ST("st", c), R("y%d" % c)) for c in range(4)])
        ts(R("ycf"), R("PR", s_[:, 0:12]), R("pc"), ADD)
        dma("Y", [(("yc", s_[:, :]), R("ycf"))])

    for h in range(N):
        for H in (0, 1):
            front(h, H)
        if h == 0:
            dist("av3", "ownx", {})
            send("ownx", [(nxt(1), "own1")], "ao", 8000)
            send("ownx", [(nxt(j), "own%d" % j) for j in (2, 3)], "ap", 12000)
        else:
            msum(h - 1)
        if h + 1 < N:
            dma("Y", [(R("bd%d" % ((h + 1) % 2), s_[16 * gg:16 * gg + 16, gg, :]), R("av%d" % (h + 1), s_[16 * gg:16 * gg + 16, :])) for gg in range(8)])
        for H in (0, 1):
            prelim(h, H)
        errs(h, 0)
        while soon:
            due[soon.pop()] = len(prog)
        logic(h, 0)
        errs(h, 1)
        back(h, 0)
        logic(h, 1)
        back(h, 1)
    msum(3)
    cut_out()
    for H in (0, 1):
        c, bk = s_[:, 192 * H:192 * H + 192], "D%d" % H
        pe_open([(R(bk, s_[:, 0:6]), R("i32"), R(n, c)) for n in ("el1", "el2")], True, False)
        for q in range(4):
            pe_open([(R(bk, s_[:, 3 * r:3 * r + 3]), R("p1"), R("mg0", s_[:, 1536 * q + 8 * H + 4 * r + t:1536 * q + 1536:16])) for r in (0, 1) for t in range(4)], False, q == 3)
        tt(R("ef0", c), R(bk, s_[:, 0:6]), R("av0", c), MUL)
    for H in (0, 1):
        c = s_[:, 256 * H:256 * H + NV[H]]
        tt(R("yes", c), R("ef0", c), R("el3" + "ab"[H]), ADD)
        dma("Y", [(("ye", c), R("yes", c))])
    if "order" not in MEMO:
        MEMO["order"] = schedule()
    for i, e in MEMO["order"]:
        issue(prog[i], e)
    for s, c in sorted(total.items()):
        if known["G"].get(s, 0) < c:
            g.wait_ge(T.sem[s], c)
